import numpy as np
import ml_dtypes


def mxq(x, axis, fmt="e4m3"):
    dtype, down = {"e4m3": (ml_dtypes.float8_e4m3fn, 7), "e5m2": (ml_dtypes.float8_e5m2, 14)}[fmt]
    v = np.moveaxis(np.asarray(x, np.float32).astype(ml_dtypes.bfloat16).astype(np.float64), axis, -1)
    blocks = v.reshape(v.shape[:-1] + (-1, 32))
    amax = np.abs(blocks).max(-1, keepdims=True)
    byte = np.maximum(np.where(amax > 0, np.frexp(amax)[1] - 1 + 127, 0) - down, 1)
    scale = np.exp2(byte - 127.0)
    codes = (blocks / scale).astype(np.float32).astype(dtype).astype(np.float64)
    return np.moveaxis((codes * scale).reshape(v.shape), -1, axis)


WIDE = False


def mx_kscale(k):
    if not WIDE:
        return np.ones(k)
    levels = np.array([10, -10, 5, -5, 0])
    if k % 512:
        return np.exp2(np.random.permutation(np.resize(levels, k // 32))).repeat(32)
    a = np.empty((k // 512, 16))
    for p in range(k // 512):
        a[p, :8] = np.random.permutation(np.resize(levels, 8))
        for g in range(8):
            far = levels[np.abs(levels - a[p, g]) >= 10]
            a[p, g + 8] = far[np.random.randint(len(far))]
    return np.exp2(a.ravel()).repeat(32)


def f64(x):
    return np.asarray(x).astype(np.float64)


def striped(idx):
    return np.tile(idx.reshape(-1, 16).T, (8, 1)).astype(np.uint16)


def unstriped(offs):
    return offs[:16].T.reshape(-1).astype(np.int64)


E2M1 = np.array([0.0, 0.5, 1.0, 1.5, 2.0, 3.0, 4.0, 6.0, -0.0, -0.5, -1.0, -1.5, -2.0, -3.0, -4.0, -6.0])


def pack_weight(w, fmt):
    k, n = w.shape
    w = f64(np.asarray(w, np.float32).astype(ml_dtypes.bfloat16)).reshape(k // 32, 32, n)
    amax = np.abs(w).max(1)
    if fmt == "e4m3":
        byte = np.frexp(amax)[1] - 1 + 127 - 7
    else:
        mant, ex = np.frexp(amax / 6.0)
        byte = np.where(mant > 0.5, ex, ex - 1) + 127
    byte = np.clip(np.where(amax > 0, byte, 1), 1, 254)
    scaled = (w * np.exp2(127.0 - byte)[:, None, :]).reshape(k, n).astype(np.float32)
    by_word = np.ascontiguousarray(scaled.reshape(k // 512, 128, 4, n).transpose(0, 1, 3, 2))
    if fmt == "e4m3":
        words = by_word.astype(ml_dtypes.float8_e4m3fn).view(np.uint8)
    else:
        c = by_word.astype(ml_dtypes.float4_e2m1fn).view(np.uint8) & 0xF
        words = (c[..., 0::2] | (c[..., 1::2] << 4)).reshape(k // 512, 128, 2 * n)
    return np.ascontiguousarray(words), np.ascontiguousarray(byte.astype(np.uint8).reshape(k // 512, 16, n))


def unpack_weight(words, scales, fmt):
    g, _, n = scales.shape
    words = np.ascontiguousarray(words).reshape(g, 128, n, -1)
    if fmt == "e4m3":
        vals = words.view(ml_dtypes.float8_e4m3fn).astype(np.float64)
    else:
        nib = np.empty((g, 128, n, 4), np.uint8)
        nib[..., 0::2] = words & 0xF
        nib[..., 1::2] = words >> 4
        vals = E2M1[nib]
    vals = vals * np.repeat(np.exp2(scales.astype(np.float64) - 127.0), 8, axis=1)[..., None]
    return vals.transpose(0, 1, 3, 2).reshape(g * 512, n)


def gelu(v):
    return 0.5 * v * (1.0 + np.tanh(np.sqrt(2.0 / np.pi) * (v + 0.044715 * v**3)))


K, T, S, H, T2, P, N = 512, 4096, 1024, 1536, 2048, 512, 384

def setup_inputs():
    n = np.random.standard_normal
    s = mx_kscale(K)[:, None]
    u = mx_kscale(H)[:, None]
    tab_words, tab_scales = pack_weight(n((K, T)) * s, "e4m3")
    w2_words, w2_scales = pack_weight(n((K, H)) / s / np.sqrt(K), "e2m1")
    return {
        "tab_words": tab_words, "tab_scales": tab_scales,
        "offs": striped(np.random.permutation(T)[:S]),
        "w1": (1.5 * n((K, H)) * u.T / s / np.sqrt(K)).astype(np.float32),
        "w2_words": w2_words, "w2_scales": w2_scales,
        "wgs": np.exp(0.3 * n((128, S))).astype(np.float32),
        "offs2": striped(np.random.permutation(T2)[:S]),
        "offs3": striped(np.random.permutation(T2)[:P]),
        "margin": (0.7 * n((H, P)) * u).astype(np.float32),
        "w3": (1.5 * n((H, N)) / u / np.sqrt(H)).astype(np.float32),
    }

def reference(tab_words, tab_scales, offs, w1, w2_words, w2_scales, wgs, offs2, offs3, margin, w3):
    v = unpack_weight(tab_words, tab_scales, "e4m3")[:, unstriped(offs)]
    a = mxq(f64(w1), 0, "e4m3").T @ v
    b = unpack_weight(w2_words, w2_scales, "e2m1").T @ v
    h = a * np.exp(-np.square(b))
    page = np.zeros((H, T2))
    page[:, unstriped(offs2)] = np.tile(f64(wgs), (H // 128, 1)) * h
    x = page[:, unstriped(offs3)]
    z = np.maximum(x - f64(margin), 0.0)
    out = mxq(f64(w3), 0, "e4m3").T @ mxq(z, 0, "e4m3")
    return out

@@ -1,0 +1,353 @@
+from contextlib import ExitStack
+
+import concourse.mybir as mybir
+
+K, T, S, H, T2, M_OUT, N_OUT = 512, 4096, 1024, 1536, 2048, 512, 384
+FLOPS = 2 * K * H * S * 2 + 2 * H * N_OUT * M_OUT
+
+F32 = mybir.dt.float32
+BF16 = mybir.dt.bfloat16
+I32 = mybir.dt.int32
+U32 = mybir.dt.uint32
+U16 = mybir.dt.uint16
+U8 = mybir.dt.uint8
+FP8X4 = mybir.dt.float8_e4m3fn_x4
+FP4X4 = mybir.dt.float4_e2m1fn_x4
+ACT = mybir.ActivationFunctionType
+ALU = mybir.AluOpType
+
+P = 128
+PACK = 4
+R_PASS = P * PACK
+PASSES = H // R_PASS
+TILES = H // P
+HALF = 512
+PAGES = 3
+AL = 64
+HOLDS = (2, 4, 6, 10)
+
+
+def tile_list_phishing_verdict_slots_kernel(
+    tc, tab_words, tab_scales, offs, w1, w2_words, w2_scales, wgs, offs2, offs3, margin, w3, out
+):
+    nc = tc.nc
+    with ExitStack() as ctx:
+        lists = ctx.enter_context(tc.tile_pool(name="lists", bufs=1))
+        keep = ctx.enter_context(tc.tile_pool(name="keep", bufs=1))
+        ring = ctx.enter_context(tc.tile_pool(name="ring", bufs=1))
+        psum = ctx.enter_context(tc.psum_pool(name="psum", bufs=1))
+
+        idx = lists.tile([P, S // 16], U16, name="idx")
+        idx2 = lists.tile([P, S // 16], U16, name="idx2")
+        idx3 = lists.tile([P, M_OUT // 16], U16, name="idx3")
+
+        ts = ring.tile([P, T], U8, name="ts", tag="wg_rest", bufs=1, align_bytes=AL)
+        w2s_raw = keep.tile([P, H], U8, name="w2s_raw", align_bytes=AL)
+        nc.vector.memset(ts[:].bitcast(I32), 0)
+        nc.gpsimd.memset(w2s_raw[:].bitcast(I32), 0)
+        nc.sync.dma_start(idx[:], offs)
+        for q in range(4):
+            nc.scalar.dma_start(
+                ts[32 * q : 32 * q + 4, :].bitcast(I32), tab_scales[0, 4 * q : 4 * q + 4, :].bitcast(I32)
+            )
+        for q in range(4):
+            nc.gpsimd.dma_start(
+                w2s_raw[32 * q : 32 * q + 4, :].bitcast(I32), w2_scales[0, 4 * q : 4 * q + 4, :].bitcast(I32)
+            )
+        w2_raw = ring.tile([P, 2 * H], U8, name="w2_raw", tag="wg0", bufs=1, align_bytes=AL)
+        nc.sync.dma_start(w2_raw[:].bitcast(I32), w2_words[0].bitcast(I32))
+        tw = ring.tile([P, T], I32, name="tw", tag="big", bufs=1, align_bytes=AL)
+        nc.sync.dma_start(tw[:], tab_words[0].rearrange("p t i -> p (t i)").bitcast(I32))
+        w1_first = ring.tile([P, PACK, R_PASS], F32, name="w1_first", tag="w13", bufs=1, align_bytes=AL)
+        nc.sync.dma_start(w1_first[:], w1[:, 0:R_PASS].rearrange("(p j) c -> p j c", j=PACK))
+        nc.sync.dma_start(idx2[:], offs2)
+        nc.sync.dma_start(idx3[:], offs3)
+        wg_rows = wgs.rearrange("(m t) j -> m t j", t=PACK)
+
+        pages = [keep.tile([P, T2], F32, name=f"page{n}") for n in range(PAGES)]
+        nc.gpsimd.memset(pages[0][:], 0.0)
+        nc.vector.memset(pages[1][:], 0.0)
+        nc.vector.memset(pages[2][:], 0.0)
+
+        w2c = keep.tile([P, 2 * H], U8, name="w2c", align_bytes=AL)
+        w2s_first = keep.tile([P, R_PASS], U8, name="w2s_first", align_bytes=AL)
+        w2s_rest = keep.tile([P, H - R_PASS], U8, name="w2s_rest", align_bytes=AL)
+        nc.vector.tensor_copy(
+            w2c[:].bitcast(U16).rearrange("p (g t m) -> p g m t", g=PASSES, t=PACK),
+            w2_raw[:].bitcast(U16).rearrange("p (g m t) -> p g m t", g=PASSES, t=PACK),
+        )
+        wg0 = ring.tile([P, S], F32, name="wg0", tag="wg0", bufs=1, align_bytes=AL)
+        for q in range(4):
+            nc.sync.dma_start(wg0[32 * q : 32 * q + 32, :], wg_rows[:, 0, :])
+
+        vs = [keep.tile([P, HALF], U8, name=f"vs{h}", align_bytes=AL) for h in range(2)]
+        vw = [keep.tile([P, HALF], U32, name=f"vw{h}", align_bytes=AL) for h in range(2)]
+        nc.vector.tensor_copy(vs[0][:], ts[:].indirect(idx[:, 0:32]))
+        nc.vector.tensor_copy(
+            w2s_first[:].rearrange("p (t m) -> p m t", t=PACK),
+            w2s_raw[:, 0:R_PASS].rearrange("p (m t) -> p m t", t=PACK),
+        )
+        nc.vector.tensor_copy(vw[0][:], tw[:].bitcast(U32).indirect(idx[:, 0:32]))
+
+        def quantised(name, grouped, width, tag=None):
+            codes = ring.tile([P, width], U32, name=name + "_codes", tag=tag or name, bufs=1, align_bytes=AL)
+            scales = keep.tile([P, width], U8, name=name + "_scales", align_bytes=AL)
+            done = 0
+            while done < width:
+                step = max(w for w in (128, 256, 512, 1024) if w <= width - done)
+                nc.vector.quantize_mx(
+                    out=codes[:, done : done + step].bitcast(FP8X4),
+                    scales=scales[:, done : done + step],
+                    in_=grouped[:, PACK * done : PACK * (done + step)],
+                )
+                done = done + step
+            return codes, scales
+
+        by_slot = w1_first[:].rearrange("p j (m t) -> p m t j", t=PACK)
+        w1a = []
+
+        def early_w1(t):
+            bf = keep.tile([P, P * PACK], BF16, name=f"w1a_bf{t}", align_bytes=AL)
+            nc.vector.tensor_copy(bf[:].rearrange("p (m j) -> p m j", j=PACK), by_slot[:, :, t, :])
+            w1a.append(quantised(f"w1a{t}", bf, P))
+
+        early_w1(0)
+        nc.vector.tensor_copy(vw[1][:], tw[:].bitcast(U32).indirect(idx[:, 32:64]))
+        nc.vector.tensor_copy(vs[1][:], ts[:].indirect(idx[:, 32:64]))
+        nc.gpsimd.tensor_copy(
+            w2s_rest[:].rearrange("p (g t m) -> p g m t", g=PASSES - 1, t=PACK),
+            w2s_raw[:, R_PASS:H].rearrange("p (g m t) -> p g m t", g=PASSES - 1, t=PACK),
+        )
+        wg_rest = ring.tile([P, PACK - 1, S], F32, name="wg_rest", tag="big", bufs=1, align_bytes=AL)
+        for q in range(4):
+            nc.sync.dma_start(wg_rest[32 * q : 32 * q + 32, :, :], wg_rows[:, 1:PACK, :])
+        early_w1(1)
+
+        w1_rest = ring.tile([P, PASSES - 1, PACK, R_PASS], F32, name="w1_rest", tag="wg_rest", bufs=1, align_bytes=AL)
+
+        def load_w1(g):
+            nc.sync.dma_start(
+                w1_rest[:, g - 1, :, :], w1[:, g * R_PASS : (g + 1) * R_PASS].rearrange("(p j) c -> p j c", j=PACK)
+            )
+
+        margins = {}
+        margin_rows = margin.rearrange("(g p t) m -> g t p m", g=PASSES, t=PACK)
+
+        def load_margin(i):
+            margins[i] = ring.tile([P, M_OUT], F32, name="margin", tag=f"slot{i % 3}", bufs=1)
+            nc.sync.dma_start(margins[i][:], margin_rows[i // PACK, i % PACK])
+
+        load_w1(1)
+        load_w1(2)
+        w3_raw = ring.tile([P, PASSES, PACK, N_OUT], F32, name="w3_raw", tag="w13", bufs=1, align_bytes=AL)
+        for g in range(PASSES):
+            nc.sync.dma_start(
+                w3_raw[:, g, :, :], w3[g * R_PASS : (g + 1) * R_PASS, :].rearrange("(p j) n -> p j n", j=PACK)
+            )
+
+        stage = {}
+        diffs = {}
+
+        def prepare_w1b():
+            w1b_bf = ring.tile([P, 2 * P * PACK], BF16, name="w1b_bf", tag="sq_last", bufs=1, align_bytes=AL)
+            nc.scalar.activation(
+                w1b_bf[:].rearrange("p (t m j) -> p m t j", t=2, j=PACK), by_slot[:, :, 2:PACK, :], ACT.Copy
+            )
+            stage[0] = quantised("w1b", w1b_bf, 2 * P, "after0_256")
+
+        def prepare_w1(g, tag):
+            w1c_bf = ring.tile([P, R_PASS * PACK], BF16, name="w1c_bf", tag=tag, bufs=1, align_bytes=AL)
+            nc.scalar.activation(
+                w1c_bf[:].rearrange("p (t m j) -> p m t j", t=PACK, j=PACK),
+                w1_rest[:, g - 1, :, :].rearrange("p j (m t) -> p m t j", t=PACK),
+                ACT.Copy,
+            )
+            stage[g] = quantised(f"w1c{g}", w1c_bf, R_PASS)
+
+        def prepare_w3(tag):
+            w3_bf = ring.tile([P, PASSES * N_OUT * PACK], BF16, name="w3_bf", tag=tag, bufs=1, align_bytes=AL)
+            for g in range(PASSES):
+                nc.scalar.activation(
+                    w3_bf[:, g * N_OUT * PACK : (g + 1) * N_OUT * PACK].rearrange(
+                        "p (c i j) -> p c j i", i=4, j=PACK
+                    ),
+                    w3_raw[:, g, :, :].rearrange("p j (c i) -> p c j i", i=4),
+                    ACT.Copy,
+                )
+            stage["w3"] = quantised("w3", w3_bf, PASSES * N_OUT)
+
+        def w1_operand(i):
+            if i < 2:
+                pair, col = w1a[i], 0
+            elif i < PACK:
+                pair, col = stage[0], (i - 2) * P
+            else:
+                pair, col = stage[i // PACK], (i % PACK) * P
+            return pair[0][:, col : col + P].bitcast(FP8X4), pair[1][:, col : col + P]
+
+        def pieces(i):
+            if i == 0:
+                return [(0, 256), (256, 256), (512, 512)]
+            return [(0, HALF), (HALF, HALF)] if i == 1 else [(0, S)]
+
+        def signatures(i):
+            t = i % PACK
+            if i == 0:
+                hw = [
+                    ring.tile([P, width], F32, name="hw", tag=f"after0_{first}", bufs=1, align_bytes=AL)[:]
+                    for first, width in pieces(i)
+                ]
+            else:
+                if i in HOLDS:
+                    whole = ring.tile([P, S], F32, name="hw", tag=f"after{i}", bufs=1, align_bytes=AL)
+                else:
+                    whole = ring.tile([P, S], F32, name="hw", tag="hw", bufs=2)
+                hw = [whole[:, first : first + width] for first, width in pieces(i)]
+            e = ring.tile([P, S], F32, name="e", tag="e", bufs=2)
+            if i < 2:
+                a_own = keep.tile([P, 2, HALF], F32, name=f"a_own{i}")
+                a_sb = a_own[:]
+            else:
+                lag_g, lag_t = divmod(i - 2, PACK)
+                if lag_t == 0:
+                    diffs[lag_g] = ring.tile([P, 2 * PACK, M_OUT], F32, name="d", tag="d", bufs=2)
+                a_sb = diffs[lag_g][:, lag_t :: PACK, :]
+            sig = ring.tile([P, S], F32, name="sig", tag=f"slot{i % 3}", bufs=1)
+            wg = wg0[:] if t == 0 else wg_rest[:, t - 1, :]
+            w1c, w1s = w1_operand(i)
+            w2s_tile = w2s_first[:, i * P : (i + 1) * P] if i < PACK else w2s_rest[:, (i - PACK) * P : (i - PACK + 1) * P]
+            for piece, (first, width) in enumerate(pieces(i)):
+                for c0 in range(first, first + width, HALF):
+                    n = min(width, HALF)
+                    cols = slice(c0, c0 + n)
+                    h = c0 // HALF
+                    part = slice(c0 - h * HALF, c0 - h * HALF + n)
+                    b_ps = psum.tile([P, HALF], F32, name="b_ps", tag="b", bufs=3)
+                    nc.tensor.matmul_mx(
+                        out=b_ps[:, 0:n],
+                        lhsT=w2c[:, 2 * i * P : 2 * (i + 1) * P].bitcast(FP4X4),
+                        lhsT_scale=w2s_tile,
+                        rhs=vw[h][:, part].bitcast(FP8X4),
+                        rhs_scale=vs[h][:, part],
+                        start=True,
+                        stop=True,
+                    )
+                    a_ps = psum.tile([P, HALF], F32, name="a_ps", tag="a", bufs=2)
+                    nc.tensor.matmul_mx(
+                        out=a_ps[:, 0:n],
+                        lhsT=w1c,
+                        lhsT_scale=w1s,
+                        rhs=vw[h][:, part].bitcast(FP8X4),
+                        rhs_scale=vs[h][:, part],
+                        start=True,
+                        stop=True,
+                    )
+                    if i == 0 and c0 == HALF:
+                        sq = ring.tile([P, HALF], F32, name="sq", tag="sq_last", bufs=1, align_bytes=AL)
+                    else:
+                        sq = ring.tile([P, HALF], F32, name="sq", tag="sq", bufs=2)
+                    nc.scalar.activation(sq[:, 0:n], b_ps[:, 0:n], ACT.Square)
+                    nc.scalar.activation(e[:, cols], sq[:, 0:n], ACT.Exp, scale=-1.0)
+                    nc.scalar.copy(a_sb[:, h, part], a_ps[:, 0:n])
+                cols = slice(first, first + width)
+                if width == S:
+                    nc.gpsimd.tensor_tensor(
+                        sig[:].rearrange("p (h c) -> p h c", h=2),
+                        a_sb,
+                        e[:].rearrange("p (h c) -> p h c", h=2),
+                        ALU.mult,
+                    )
+                else:
+                    nc.gpsimd.tensor_tensor(sig[:, cols], a_sb[:, h, part], e[:, cols], ALU.mult)
+                nc.gpsimd.tensor_tensor(hw[piece], sig[:, cols], wg[:, cols], ALU.mult)
+            load_margin(i)
+            return hw
+
+        def scatter(i, hw):
+            for piece, (first, width) in enumerate(pieces(i)):
+                nc.vector.tensor_copy(
+                    pages[i % PAGES][:].indirect(idx2[:, first // 16 : (first + width) // 16]),
+                    hw[piece],
+                )
+
+        out_ps = [psum.tile([P, M_OUT], F32, name=f"out_ps{n}") for n in range(N_OUT // P)]
+
+        def score(g, zc, zs, cols, stop):
+            w3c, w3s = stage["w3"]
+            for n in range(N_OUT // P):
+                wcols = slice(g * N_OUT + n * P, g * N_OUT + (n + 1) * P)
+                nc.tensor.matmul_mx(
+                    out=out_ps[n][:, cols],
+                    lhsT=w3c[:, wcols].bitcast(FP8X4),
+                    lhsT_scale=w3s[:, wcols],
+                    rhs=zc[:].bitcast(FP8X4),
+                    rhs_scale=zs[:],
+                    start=(g == 0),
+                    stop=stop,
+                )
+
+        def interleaved(z_bf, d_part):
+            return z_bf[:].rearrange("p (c i t) -> p c t i", i=4, t=PACK), d_part.rearrange("p t (c i) -> p c t i", i=4)
+
+        def fetch(i):
+            g, t = divmod(i, PACK)
+            d = diffs[g]
+            nc.vector.tensor_tensor(d[:, t, :], pages[i % PAGES][:].indirect(idx3[:]), margins[i][:], ALU.subtract)
+            if t == PACK - 1:
+                stage["z_bf"] = ring.tile([P, M_OUT * PACK], BF16, name="z_bf", tag="z_bf", bufs=1, align_bytes=AL)
+                dst, srcv = interleaved(stage["z_bf"], d[:, 0:PACK, :])
+                nc.scalar.activation(dst, srcv, ACT.Relu)
+
+        def close_pass(g, tag):
+            zc, zs = quantised(f"z{g}", stage["z_bf"], M_OUT, tag)
+            score(g, zc, zs, slice(0, M_OUT), False)
+
+        def last_tile():
+            i = TILES - 1
+            g, t = divmod(i, PACK)
+            d = diffs[g]
+            width = M_OUT // 2
+            halves = [slice(0, width), slice(width, M_OUT)]
+            for cols in halves:
+                nc.vector.tensor_tensor(
+                    d[:, t, cols],
+                    pages[i % PAGES][:].indirect(idx3[:, cols.start // 16 : cols.stop // 16]),
+                    margins[i][:, cols],
+                    ALU.subtract,
+                )
+            z_lo = keep.tile([P, width * PACK], BF16, name="z_lo", align_bytes=AL)
+            z_hi = keep.tile([P, width * PACK], BF16, name="z_hi", align_bytes=AL)
+            dst, srcv = interleaved(z_lo, d[:, 0:PACK, halves[0]])
+            nc.scalar.activation(dst, srcv, ACT.Relu)
+            dst, srcv = interleaved(z_hi, d[:, 0:PACK, halves[1]])
+            nc.vector.tensor_scalar_max(dst, srcv, 0.0)
+            zc, zs = quantised("zhi", z_hi, width)
+            score(g, zc, zs, halves[1], False)
+            zc, zs = quantised("zlo", z_lo, width)
+            score(g, zc, zs, halves[0], True)
+
+        for i in range(TILES):
+            hw = signatures(i)
+            if i >= 2:
+                fetch(i - 2)
+            if i == TILES - 1:
+                fetch(i - 1)
+            scatter(i, hw)
+            if i == 0:
+                prepare_w1b()
+                prepare_w1(1, "after0_512")
+            if i == 2:
+                prepare_w3("after2")
+            if i == 4:
+                prepare_w1(2, "after4")
+            if i in (6, 10):
+                close_pass(i // PACK - 1, f"after{i}")
+        last_tile()
+
+        for n in range(N_OUT // P):
+            res = keep.tile([P, M_OUT], F32, name=f"res{n}")
+            if n == 1:
+                nc.scalar.copy(res[:], out_ps[n][:])
+            else:
+                nc.vector.tensor_copy(res[:], out_ps[n][:])
+            nc.sync.dma_start(out[n * P : (n + 1) * P, :], res[:])

@@ -22,9 +22,9 @@ R_PASS = P * PACK
 PASSES = H // R_PASS
 TILES = H // P
 HALF = 512
-PAGES = 3
+PAGES = 2
 AL = 64
-HOLDS = (2, 4, 6, 10)
+HOLDS = (1, 2, 3, 4, 5, 9)
 
 
 def tile_list_phishing_verdict_slots_kernel(
@@ -41,33 +41,31 @@ def tile_list_phishing_verdict_slots_kernel(
         idx2 = lists.tile([P, S // 16], U16, name="idx2")
         idx3 = lists.tile([P, M_OUT // 16], U16, name="idx3")
 
-        ts = ring.tile([P, T], U8, name="ts", tag="wg_rest", bufs=1, align_bytes=AL)
+        ts = keep.tile([P, T], U8, name="ts", align_bytes=AL)
         w2s_raw = keep.tile([P, H], U8, name="w2s_raw", align_bytes=AL)
         nc.vector.memset(ts[:].bitcast(I32), 0)
         nc.gpsimd.memset(w2s_raw[:].bitcast(I32), 0)
         nc.sync.dma_start(idx[:], offs)
-        for q in range(4):
-            nc.scalar.dma_start(
-                ts[32 * q : 32 * q + 4, :].bitcast(I32), tab_scales[0, 4 * q : 4 * q + 4, :].bitcast(I32)
-            )
+        nc.sync.dma_start(idx2[:], offs2)
+        nc.sync.dma_start(idx3[:], offs3)
         for q in range(4):
             nc.gpsimd.dma_start(
                 w2s_raw[32 * q : 32 * q + 4, :].bitcast(I32), w2_scales[0, 4 * q : 4 * q + 4, :].bitcast(I32)
             )
         w2_raw = ring.tile([P, 2 * H], U8, name="w2_raw", tag="wg0", bufs=1, align_bytes=AL)
         nc.sync.dma_start(w2_raw[:].bitcast(I32), w2_words[0].bitcast(I32))
+        for q in range(4):
+            nc.scalar.dma_start(
+                ts[32 * q : 32 * q + 4, :].bitcast(I32), tab_scales[0, 4 * q : 4 * q + 4, :].bitcast(I32)
+            )
         tw = ring.tile([P, T], I32, name="tw", tag="big", bufs=1, align_bytes=AL)
         nc.sync.dma_start(tw[:], tab_words[0].rearrange("p t i -> p (t i)").bitcast(I32))
         w1_first = ring.tile([P, PACK, R_PASS], F32, name="w1_first", tag="w13", bufs=1, align_bytes=AL)
         nc.sync.dma_start(w1_first[:], w1[:, 0:R_PASS].rearrange("(p j) c -> p j c", j=PACK))
-        nc.sync.dma_start(idx2[:], offs2)
-        nc.sync.dma_start(idx3[:], offs3)
         wg_rows = wgs.rearrange("(m t) j -> m t j", t=PACK)
 
-        pages = [keep.tile([P, T2], F32, name=f"page{n}") for n in range(PAGES)]
-        nc.gpsimd.memset(pages[0][:], 0.0)
-        nc.vector.memset(pages[1][:], 0.0)
-        nc.vector.memset(pages[2][:], 0.0)
+        page0 = keep.tile([P, T2], F32, name="page0")
+        nc.vector.memset(page0[:], 0.0)
 
         w2c = keep.tile([P, 2 * H], U8, name="w2c", align_bytes=AL)
         w2s_first = keep.tile([P, R_PASS], U8, name="w2s_first", align_bytes=AL)
@@ -78,16 +76,16 @@ def tile_list_phishing_verdict_slots_kernel(
         )
         wg0 = ring.tile([P, S], F32, name="wg0", tag="wg0", bufs=1, align_bytes=AL)
         for q in range(4):
-            nc.sync.dma_start(wg0[32 * q : 32 * q + 32, :], wg_rows[:, 0, :])
+            nc.gpsimd.dma_start(wg0[32 * q : 32 * q + 32, :], wg_rows[:, 0, :])
 
-        vs = [keep.tile([P, HALF], U8, name=f"vs{h}", align_bytes=AL) for h in range(2)]
+        vs = keep.tile([P, S], U8, name="vs", align_bytes=AL)
         vw = [keep.tile([P, HALF], U32, name=f"vw{h}", align_bytes=AL) for h in range(2)]
-        nc.vector.tensor_copy(vs[0][:], ts[:].indirect(idx[:, 0:32]))
+        nc.vector.tensor_copy(vs[:], ts[:].indirect(idx[:]))
+        nc.vector.tensor_copy(vw[0][:], tw[:].bitcast(U32).indirect(idx[:, 0:32]))
         nc.vector.tensor_copy(
             w2s_first[:].rearrange("p (t m) -> p m t", t=PACK),
             w2s_raw[:, 0:R_PASS].rearrange("p (m t) -> p m t", t=PACK),
         )
-        nc.vector.tensor_copy(vw[0][:], tw[:].bitcast(U32).indirect(idx[:, 0:32]))
 
         def quantised(name, grouped, width, tag=None):
             codes = ring.tile([P, width], U32, name=name + "_codes", tag=tag or name, bufs=1, align_bytes=AL)
@@ -107,59 +105,63 @@ def tile_list_phishing_verdict_slots_kernel(
         w1a = []
 
         def early_w1(t):
-            bf = keep.tile([P, P * PACK], BF16, name=f"w1a_bf{t}", align_bytes=AL)
+            bf = ring.tile([P, P * PACK], BF16, name="w1a_bf", tag="page1", bufs=1, align_bytes=AL)
             nc.vector.tensor_copy(bf[:].rearrange("p (m j) -> p m j", j=PACK), by_slot[:, :, t, :])
             w1a.append(quantised(f"w1a{t}", bf, P))
 
         early_w1(0)
         nc.vector.tensor_copy(vw[1][:], tw[:].bitcast(U32).indirect(idx[:, 32:64]))
-        nc.vector.tensor_copy(vs[1][:], ts[:].indirect(idx[:, 32:64]))
-        nc.gpsimd.tensor_copy(
+        nc.vector.tensor_copy(
             w2s_rest[:].rearrange("p (g t m) -> p g m t", g=PASSES - 1, t=PACK),
             w2s_raw[:, R_PASS:H].rearrange("p (g m t) -> p g m t", g=PASSES - 1, t=PACK),
         )
+        page1 = ring.tile([P, T2], F32, name="page1", tag="page1", bufs=1, align_bytes=AL)
+        nc.gpsimd.memset(page1[:], 0.0)
+        pages = [page0, page1]
         wg_rest = ring.tile([P, PACK - 1, S], F32, name="wg_rest", tag="big", bufs=1, align_bytes=AL)
         for q in range(4):
             nc.sync.dma_start(wg_rest[32 * q : 32 * q + 32, :, :], wg_rows[:, 1:PACK, :])
-        early_w1(1)
 
-        w1_rest = ring.tile([P, PASSES - 1, PACK, R_PASS], F32, name="w1_rest", tag="wg_rest", bufs=1, align_bytes=AL)
+        w1_rest = {}
 
-        def load_w1(g):
+        def load_w1(g, tag):
+            w1_rest[g] = ring.tile([P, PACK, R_PASS], F32, name="w1_rest", tag=tag, bufs=1, align_bytes=AL)
             nc.sync.dma_start(
-                w1_rest[:, g - 1, :, :], w1[:, g * R_PASS : (g + 1) * R_PASS].rearrange("(p j) c -> p j c", j=PACK)
+                w1_rest[g][:], w1[:, g * R_PASS : (g + 1) * R_PASS].rearrange("(p j) c -> p j c", j=PACK)
             )
 
         margins = {}
-        margin_rows = margin.rearrange("(g p t) m -> g t p m", g=PASSES, t=PACK)
 
-        def load_margin(i):
-            margins[i] = ring.tile([P, M_OUT], F32, name="margin", tag=f"slot{i % 3}", bufs=1)
-            nc.sync.dma_start(margins[i][:], margin_rows[i // PACK, i % PACK])
-
-        load_w1(1)
-        load_w1(2)
-        w3_raw = ring.tile([P, PASSES, PACK, N_OUT], F32, name="w3_raw", tag="w13", bufs=1, align_bytes=AL)
-        for g in range(PASSES):
+        def load_margin(g, tag):
+            margins[g] = ring.tile([P, PACK, M_OUT], F32, name="margin", tag=tag, bufs=1, align_bytes=AL)
             nc.sync.dma_start(
-                w3_raw[:, g, :, :], w3[g * R_PASS : (g + 1) * R_PASS, :].rearrange("(p j) n -> p j n", j=PACK)
+                margins[g][:], margin[g * R_PASS : (g + 1) * R_PASS, :].rearrange("(p t) m -> p t m", t=PACK)
             )
+
+
+        def load_w3(tag):
+            w3_raw = ring.tile([P, PASSES, PACK, N_OUT], F32, name="w3_raw", tag=tag, bufs=1, align_bytes=AL)
+            for g in range(PASSES):
+                nc.sync.dma_start(
+                    w3_raw[:, g, :, :], w3[g * R_PASS : (g + 1) * R_PASS, :].rearrange("(p j) n -> p j n", j=PACK)
+                )
+            stage["w3_raw"] = w3_raw
 
         stage = {}
         diffs = {}
 
         def prepare_w1b():
-            w1b_bf = ring.tile([P, 2 * P * PACK], BF16, name="w1b_bf", tag="sq_last", bufs=1, align_bytes=AL)
+            w1b_bf = ring.tile([P, 3 * P * PACK], BF16, name="w1b_bf", tag="sq_last", bufs=1, align_bytes=AL)
             nc.scalar.activation(
-                w1b_bf[:].rearrange("p (t m j) -> p m t j", t=2, j=PACK), by_slot[:, :, 2:PACK, :], ACT.Copy
+                w1b_bf[:].rearrange("p (t m j) -> p m t j", t=PACK - 1, j=PACK), by_slot[:, :, 1:PACK, :], ACT.Copy
             )
-            stage[0] = quantised("w1b", w1b_bf, 2 * P, "after0_256")
+            stage[0] = quantised("w1b", w1b_bf, 3 * P, "after0_256")
 
         def prepare_w1(g, tag):
             w1c_bf = ring.tile([P, R_PASS * PACK], BF16, name="w1c_bf", tag=tag, bufs=1, align_bytes=AL)
             nc.scalar.activation(
                 w1c_bf[:].rearrange("p (t m j) -> p m t j", t=PACK, j=PACK),
-                w1_rest[:, g - 1, :, :].rearrange("p j (m t) -> p m t j", t=PACK),
+                w1_rest[g][:].rearrange("p j (m t) -> p m t j", t=PACK),
                 ACT.Copy,
             )
             stage[g] = quantised(f"w1c{g}", w1c_bf, R_PASS)
@@ -171,16 +173,16 @@ def tile_list_phishing_verdict_slots_kernel(
                     w3_bf[:, g * N_OUT * PACK : (g + 1) * N_OUT * PACK].rearrange(
                         "p (c i j) -> p c j i", i=4, j=PACK
                     ),
-                    w3_raw[:, g, :, :].rearrange("p j (c i) -> p c j i", i=4),
+                    stage["w3_raw"][:, g, :, :].rearrange("p j (c i) -> p c j i", i=4),
                     ACT.Copy,
                 )
             stage["w3"] = quantised("w3", w3_bf, PASSES * N_OUT)
 
         def w1_operand(i):
-            if i < 2:
+            if i == 0:
                 pair, col = w1a[i], 0
             elif i < PACK:
-                pair, col = stage[0], (i - 2) * P
+                pair, col = stage[0], (i - 1) * P
             else:
                 pair, col = stage[i // PACK], (i % PACK) * P
             return pair[0][:, col : col + P].bitcast(FP8X4), pair[1][:, col : col + P]
@@ -188,38 +190,23 @@ def tile_list_phishing_verdict_slots_kernel(
         def pieces(i):
             if i == 0:
                 return [(0, 256), (256, 256), (512, 512)]
-            return [(0, HALF), (HALF, HALF)] if i == 1 else [(0, S)]
+            return [(0, S)]
 
         def signatures(i):
-            t = i % PACK
             if i == 0:
-                hw = [
-                    ring.tile([P, width], F32, name="hw", tag=f"after0_{first}", bufs=1, align_bytes=AL)[:]
+                sig = [
+                    ring.tile([P, width], F32, name="sig", tag=f"after0_{first}", bufs=1, align_bytes=AL)[:]
                     for first, width in pieces(i)
                 ]
+            elif i in HOLDS:
+                sig = [ring.tile([P, S], F32, name="sig", tag=f"after{i}", bufs=1, align_bytes=AL)[:]]
             else:
-                if i in HOLDS:
-                    whole = ring.tile([P, S], F32, name="hw", tag=f"after{i}", bufs=1, align_bytes=AL)
-                else:
-                    whole = ring.tile([P, S], F32, name="hw", tag="hw", bufs=2)
-                hw = [whole[:, first : first + width] for first, width in pieces(i)]
-            e = ring.tile([P, S], F32, name="e", tag="e", bufs=2)
-            if i < 2:
-                a_own = keep.tile([P, 2, HALF], F32, name=f"a_own{i}")
-                a_sb = a_own[:]
-            else:
-                lag_g, lag_t = divmod(i - 2, PACK)
-                if lag_t == 0:
-                    diffs[lag_g] = ring.tile([P, 2 * PACK, M_OUT], F32, name="d", tag="d", bufs=2)
-                a_sb = diffs[lag_g][:, lag_t :: PACK, :]
-            sig = ring.tile([P, S], F32, name="sig", tag=f"slot{i % 3}", bufs=1)
-            wg = wg0[:] if t == 0 else wg_rest[:, t - 1, :]
+                sig = [ring.tile([P, S], F32, name="sig", tag="sig", bufs=2)[:]]
             w1c, w1s = w1_operand(i)
             w2s_tile = w2s_first[:, i * P : (i + 1) * P] if i < PACK else w2s_rest[:, (i - PACK) * P : (i - PACK + 1) * P]
             for piece, (first, width) in enumerate(pieces(i)):
                 for c0 in range(first, first + width, HALF):
                     n = min(width, HALF)
-                    cols = slice(c0, c0 + n)
                     h = c0 // HALF
                     part = slice(c0 - h * HALF, c0 - h * HALF + n)
                     b_ps = psum.tile([P, HALF], F32, name="b_ps", tag="b", bufs=3)
@@ -228,7 +215,7 @@ def tile_list_phishing_verdict_slots_kernel(
                         lhsT=w2c[:, 2 * i * P : 2 * (i + 1) * P].bitcast(FP4X4),
                         lhsT_scale=w2s_tile,
                         rhs=vw[h][:, part].bitcast(FP8X4),
-                        rhs_scale=vs[h][:, part],
+                        rhs_scale=vs[:, c0 : c0 + n],
                         start=True,
                         stop=True,
                     )
@@ -238,36 +225,39 @@ def tile_list_phishing_verdict_slots_kernel(
                         lhsT=w1c,
                         lhsT_scale=w1s,
                         rhs=vw[h][:, part].bitcast(FP8X4),
-                        rhs_scale=vs[h][:, part],
+                        rhs_scale=vs[:, c0 : c0 + n],
                         start=True,
                         stop=True,
                     )
-                    if i == 0 and c0 == HALF:
-                        sq = ring.tile([P, HALF], F32, name="sq", tag="sq_last", bufs=1, align_bytes=AL)
+                    if i == 0 and h == 1:
+                        sq = ring.tile([P, HALF], F32, name="sq", tag="sq_last", bufs=1, align_bytes=AL)[:]
+                    elif h == 1:
+                        lag_g, lag_t = divmod(i - 1, PACK)
+                        if lag_t == 0:
+                            diffs[lag_g] = ring.tile([P, PACK, M_OUT], F32, name="d", tag="d", bufs=2)
+                        sq = diffs[lag_g][:, lag_t, :]
                     else:
-                        sq = ring.tile([P, HALF], F32, name="sq", tag="sq", bufs=2)
+                        sq = ring.tile([P, HALF], F32, name="sq", tag="sq", bufs=2)[:]
+                    if i == 0 and c0 == 0:
+                        e = ring.tile([P, HALF], F32, name="e", tag="margin1", bufs=1, align_bytes=AL)
+                    else:
+                        e = ring.tile([P, HALF], F32, name="e", tag="e", bufs=4)
                     nc.scalar.activation(sq[:, 0:n], b_ps[:, 0:n], ACT.Square)
-                    nc.scalar.activation(e[:, cols], sq[:, 0:n], ACT.Exp, scale=-1.0)
-                    nc.scalar.copy(a_sb[:, h, part], a_ps[:, 0:n])
-                cols = slice(first, first + width)
-                if width == S:
-                    nc.gpsimd.tensor_tensor(
-                        sig[:].rearrange("p (h c) -> p h c", h=2),
-                        a_sb,
-                        e[:].rearrange("p (h c) -> p h c", h=2),
-                        ALU.mult,
+                    nc.scalar.activation(e[:, 0:n], sq[:, 0:n], ACT.Exp, scale=-1.0)
+                    nc.vector.tensor_tensor(
+                        sig[piece][:, c0 - first : c0 - first + n], a_ps[:, 0:n], e[:, 0:n], ALU.mult
                     )
-                else:
-                    nc.gpsimd.tensor_tensor(sig[:, cols], a_sb[:, h, part], e[:, cols], ALU.mult)
-                nc.gpsimd.tensor_tensor(hw[piece], sig[:, cols], wg[:, cols], ALU.mult)
-            load_margin(i)
-            return hw
+            return sig
 
-        def scatter(i, hw):
+        def scatter(i, sig):
+            t = i % PACK
+            wg = wg0[:] if t == 0 else wg_rest[:, t - 1, :]
             for piece, (first, width) in enumerate(pieces(i)):
-                nc.vector.tensor_copy(
+                nc.vector.tensor_tensor(
                     pages[i % PAGES][:].indirect(idx2[:, first // 16 : (first + width) // 16]),
-                    hw[piece],
+                    sig[piece],
+                    wg[:, first : first + width],
+                    ALU.mult,
                 )
 
         out_ps = [psum.tile([P, M_OUT], F32, name=f"out_ps{n}") for n in range(N_OUT // P)]
@@ -292,7 +282,7 @@ def tile_list_phishing_verdict_slots_kernel(
         def fetch(i):
             g, t = divmod(i, PACK)
             d = diffs[g]
-            nc.vector.tensor_tensor(d[:, t, :], pages[i % PAGES][:].indirect(idx3[:]), margins[i][:], ALU.subtract)
+            nc.vector.tensor_tensor(d[:, t, :], pages[i % PAGES][:].indirect(idx3[:]), margins[g][:, t, :], ALU.subtract)
             if t == PACK - 1:
                 stage["z_bf"] = ring.tile([P, M_OUT * PACK], BF16, name="z_bf", tag="z_bf", bufs=1, align_bytes=AL)
                 dst, srcv = interleaved(stage["z_bf"], d[:, 0:PACK, :])
@@ -312,7 +302,7 @@ def tile_list_phishing_verdict_slots_kernel(
                 nc.vector.tensor_tensor(
                     d[:, t, cols],
                     pages[i % PAGES][:].indirect(idx3[:, cols.start // 16 : cols.stop // 16]),
-                    margins[i][:, cols],
+                    margins[g][:, t, cols],
                     ALU.subtract,
                 )
             z_lo = keep.tile([P, width * PACK], BF16, name="z_lo", align_bytes=AL)
@@ -328,19 +318,25 @@ def tile_list_phishing_verdict_slots_kernel(
 
         for i in range(TILES):
             hw = signatures(i)
-            if i >= 2:
-                fetch(i - 2)
-            if i == TILES - 1:
+            if i >= 1:
                 fetch(i - 1)
             scatter(i, hw)
             if i == 0:
+                load_w1(1, "margin1")
+                load_margin(0, "after0_0")
                 prepare_w1b()
                 prepare_w1(1, "after0_512")
+            if i == 1:
+                load_margin(1, "margin1")
+                load_w3("after1")
             if i == 2:
-                prepare_w3("after2")
+                load_w1(2, "after2")
+            if i == 3:
+                prepare_w3("after3")
             if i == 4:
                 prepare_w1(2, "after4")
-            if i in (6, 10):
+                load_margin(2, "after0_0")
+            if i in (5, 9):
                 close_pass(i // PACK - 1, f"after{i}")
         last_tile()
 

@@ -18,11 +18,12 @@ ALU = mybir.AluOpType
 
 P = 128
 PACK = 4
+QUADS = 4
 R_PASS = P * PACK
 PASSES = H // R_PASS
+LAST = PASSES - 1
 TILES = H // P
 HALF = 512
-PAGES = 2
 AL = 64
 HOLDS = (1, 2, 3, 4, 5, 9)
 
@@ -37,58 +38,20 @@ def tile_list_phishing_verdict_slots_kernel(
         ring = ctx.enter_context(tc.tile_pool(name="ring", bufs=1))
         psum = ctx.enter_context(tc.psum_pool(name="psum", bufs=1))
 
-        idx = lists.tile([P, S // 16], U16, name="idx")
-        idx2 = lists.tile([P, S // 16], U16, name="idx2")
-        idx3 = lists.tile([P, M_OUT // 16], U16, name="idx3")
+        def shared(shape, dtype, name, tag):
+            return ring.tile(shape, dtype, name=name, tag=tag, bufs=1, align_bytes=AL)
 
-        ts = keep.tile([P, T], U8, name="ts", align_bytes=AL)
-        w2s_raw = keep.tile([P, H], U8, name="w2s_raw", align_bytes=AL)
-        nc.vector.memset(ts[:].bitcast(I32), 0)
-        nc.gpsimd.memset(w2s_raw[:].bitcast(I32), 0)
-        nc.sync.dma_start(idx[:], offs)
-        nc.sync.dma_start(idx2[:], offs2)
-        nc.sync.dma_start(idx3[:], offs3)
-        for q in range(4):
-            nc.gpsimd.dma_start(
-                w2s_raw[32 * q : 32 * q + 4, :].bitcast(I32), w2_scales[0, 4 * q : 4 * q + 4, :].bitcast(I32)
-            )
-        w2_raw = ring.tile([P, 2 * H], U8, name="w2_raw", tag="wg0", bufs=1, align_bytes=AL)
-        nc.sync.dma_start(w2_raw[:].bitcast(I32), w2_words[0].bitcast(I32))
-        for q in range(4):
-            nc.scalar.dma_start(
-                ts[32 * q : 32 * q + 4, :].bitcast(I32), tab_scales[0, 4 * q : 4 * q + 4, :].bitcast(I32)
-            )
-        tw = ring.tile([P, T], I32, name="tw", tag="big", bufs=1, align_bytes=AL)
-        nc.sync.dma_start(tw[:], tab_words[0].rearrange("p t i -> p (t i)").bitcast(I32))
-        w1_first = ring.tile([P, PACK, R_PASS], F32, name="w1_first", tag="w13", bufs=1, align_bytes=AL)
-        nc.sync.dma_start(w1_first[:], w1[:, 0:R_PASS].rearrange("(p j) c -> p j c", j=PACK))
-        wg_rows = wgs.rearrange("(m t) j -> m t j", t=PACK)
+        def load_scale_rows(queue, plane, rows):
+            for q in range(QUADS):
+                queue.dma_start(plane[32 * q : 32 * q + 4, :].bitcast(I32), rows[4 * q : 4 * q + 4, :].bitcast(I32))
 
-        page0 = keep.tile([P, T2], F32, name="page0")
-        nc.vector.memset(page0[:], 0.0)
-
-        w2c = keep.tile([P, 2 * H], U8, name="w2c", align_bytes=AL)
-        w2s_first = keep.tile([P, R_PASS], U8, name="w2s_first", align_bytes=AL)
-        w2s_rest = keep.tile([P, H - R_PASS], U8, name="w2s_rest", align_bytes=AL)
-        nc.vector.tensor_copy(
-            w2c[:].bitcast(U16).rearrange("p (g t m) -> p g m t", g=PASSES, t=PACK),
-            w2_raw[:].bitcast(U16).rearrange("p (g m t) -> p g m t", g=PASSES, t=PACK),
-        )
-        wg0 = ring.tile([P, S], F32, name="wg0", tag="wg0", bufs=1, align_bytes=AL)
-        for q in range(4):
-            nc.gpsimd.dma_start(wg0[32 * q : 32 * q + 32, :], wg_rows[:, 0, :])
-
-        vs = keep.tile([P, S], U8, name="vs", align_bytes=AL)
-        vw = [keep.tile([P, HALF], U32, name=f"vw{h}", align_bytes=AL) for h in range(2)]
-        nc.vector.tensor_copy(vs[:], ts[:].indirect(idx[:]))
-        nc.vector.tensor_copy(vw[0][:], tw[:].bitcast(U32).indirect(idx[:, 0:32]))
-        nc.vector.tensor_copy(
-            w2s_first[:].rearrange("p (t m) -> p m t", t=PACK),
-            w2s_raw[:, 0:R_PASS].rearrange("p (m t) -> p m t", t=PACK),
-        )
+        def load_w1(cols, tag):
+            raw = shared([P, PACK, cols.stop - cols.start], F32, "w1_raw", tag)
+            nc.sync.dma_start(raw[:], w1[:, cols].rearrange("(p j) c -> p j c", j=PACK))
+            return raw
 
         def quantised(name, grouped, width, tag=None):
-            codes = ring.tile([P, width], U32, name=name + "_codes", tag=tag or name, bufs=1, align_bytes=AL)
+            codes = shared([P, width], U32, name + "_codes", tag or name)
             scales = keep.tile([P, width], U8, name=name + "_scales", align_bytes=AL)
             done = 0
             while done < width:
@@ -101,109 +64,155 @@ def tile_list_phishing_verdict_slots_kernel(
                 done = done + step
             return codes, scales
 
-        by_slot = w1_first[:].rearrange("p j (m t) -> p m t j", t=PACK)
-        w1a = []
+        def interleaved(grouped, rows):
+            return (
+                grouped.rearrange("p (c i j) -> p c j i", i=4, j=PACK),
+                rows.rearrange("p j (c i) -> p c j i", i=4),
+            )
 
-        def early_w1(t):
-            bf = ring.tile([P, P * PACK], BF16, name="w1a_bf", tag="page1", bufs=1, align_bytes=AL)
-            nc.vector.tensor_copy(bf[:].rearrange("p (m j) -> p m j", j=PACK), by_slot[:, :, t, :])
-            w1a.append(quantised(f"w1a{t}", bf, P))
+        idx = lists.tile([P, S // 16], U16, name="idx")
+        idx2 = lists.tile([P, S // 16], U16, name="idx2")
+        idx3 = lists.tile([P, M_OUT // 16], U16, name="idx3")
 
-        early_w1(0)
-        nc.vector.tensor_copy(vw[1][:], tw[:].bitcast(U32).indirect(idx[:, 32:64]))
-        nc.vector.tensor_copy(
-            w2s_rest[:].rearrange("p (g t m) -> p g m t", g=PASSES - 1, t=PACK),
-            w2s_raw[:, R_PASS:H].rearrange("p (g m t) -> p g m t", g=PASSES - 1, t=PACK),
-        )
-        page1 = ring.tile([P, T2], F32, name="page1", tag="page1", bufs=1, align_bytes=AL)
+        ts_rows = shared([P, T], U8, "ts_rows", "ts_rows")
+        load_scale_rows(nc.sync, ts_rows, tab_scales[0])
+        nc.sync.dma_start(idx[:], offs)
+        w1_first = load_w1(slice(0, P), "w1_first")
+        tw = shared([P, T], I32, "tw", "table")
+        nc.sync.dma_start(tw[:], tab_words[0].rearrange("p t i -> p (t i)").bitcast(I32))
+        w2c = keep.tile([P, 2 * H], U8, name="w2c", align_bytes=AL)
+        nc.sync.dma_start(w2c[:].bitcast(I32), w2_words[0].bitcast(I32))
+        w2s = keep.tile([P, LAST * R_PASS], U8, name="w2s", align_bytes=AL)
+        load_scale_rows(nc.gpsimd, w2s, w2_scales[0, :, 0 : LAST * R_PASS])
+        wg = keep.tile([P, S], F32, name="wg")
+        nc.sync.dma_start(wg[:], wgs)
+        nc.sync.dma_start(idx2[:], offs2)
+        nc.sync.dma_start(idx3[:], offs3)
+        w1_raw = {0: load_w1(slice(P, R_PASS), "w1_pass0")}
+
+        ts = keep.tile([P, T], U8, name="ts", align_bytes=AL)
+        nc.vector.memset(ts[:].bitcast(I32), 0)
+        page0 = keep.tile([P, T2], F32, name="page0")
+        nc.vector.memset(page0[:], 0.0)
+        for q in range(QUADS):
+            rows = slice(32 * q, 32 * q + 4)
+            nc.vector.tensor_copy(ts[rows, :].bitcast(I32), ts_rows[rows, :].bitcast(I32))
+        w2s_last_raw = shared([P, R_PASS], U8, "w2s_last_raw", "ts_rows")
+        nc.gpsimd.memset(w2s_last_raw[:].bitcast(I32), 0)
+
+        first_bf = shared([P, P * PACK], BF16, "first_bf", "page1")
+        nc.vector.tensor_copy(*interleaved(first_bf[:], w1_first[:]))
+        w1q = {"first": quantised("w1_tile0", first_bf, P)}
+        page1 = shared([P, T2], F32, "page1", "page1")
         nc.gpsimd.memset(page1[:], 0.0)
         pages = [page0, page1]
-        wg_rest = ring.tile([P, PACK - 1, S], F32, name="wg_rest", tag="big", bufs=1, align_bytes=AL)
-        for q in range(4):
-            nc.sync.dma_start(wg_rest[32 * q : 32 * q + 32, :, :], wg_rows[:, 1:PACK, :])
 
-        w1_rest = {}
-
-        def load_w1(g, tag):
-            w1_rest[g] = ring.tile([P, PACK, R_PASS], F32, name="w1_rest", tag=tag, bufs=1, align_bytes=AL)
-            nc.sync.dma_start(
-                w1_rest[g][:], w1[:, g * R_PASS : (g + 1) * R_PASS].rearrange("(p j) c -> p j c", j=PACK)
-            )
+        vs = [keep.tile([P, HALF], U8, name=f"vs{h}", align_bytes=AL) for h in range(2)]
+        vw = [keep.tile([P, HALF], U32, name=f"vw{h}", align_bytes=AL) for h in range(2)]
+        for h in range(2):
+            nc.vector.tensor_copy(vs[h][:], ts[:].indirect(idx[:, 32 * h : 32 * h + 32]))
+            nc.vector.tensor_copy(vw[h][:], tw[:].bitcast(U32).indirect(idx[:, 32 * h : 32 * h + 32]))
 
         margins = {}
+        stage = {}
+        diffs = {}
+        fetched = {}
 
         def load_margin(g, tag):
-            margins[g] = ring.tile([P, PACK, M_OUT], F32, name="margin", tag=tag, bufs=1, align_bytes=AL)
-            nc.sync.dma_start(
-                margins[g][:], margin[g * R_PASS : (g + 1) * R_PASS, :].rearrange("(p t) m -> p t m", t=PACK)
-            )
-
+            margins[g] = shared([P, PACK, M_OUT], F32, "margin", tag)
+            rows = margin[g * R_PASS : (g + 1) * R_PASS, :]
+            if g == LAST:
+                nc.sync.dma_start(margins[g][:], rows.rearrange("(p t) m -> p t m", t=PACK))
+            else:
+                nc.sync.dma_start(margins[g][:], rows.rearrange("(t p) m -> p t m", t=PACK))
 
         def load_w3(tag):
-            w3_raw = ring.tile([P, PASSES, PACK, N_OUT], F32, name="w3_raw", tag=tag, bufs=1, align_bytes=AL)
+            w3_raw = shared([P, PASSES, PACK, N_OUT], F32, "w3_raw", tag)
             for g in range(PASSES):
                 nc.sync.dma_start(
                     w3_raw[:, g, :, :], w3[g * R_PASS : (g + 1) * R_PASS, :].rearrange("(p j) n -> p j n", j=PACK)
                 )
             stage["w3_raw"] = w3_raw
 
-        stage = {}
-        diffs = {}
+        def load_last_weights():
+            wg_last = shared([P, PACK, S], F32, "wg_last", "w1_pass0")
+            for q in range(QUADS):
+                nc.sync.dma_start(wg_last[32 * q : 32 * q + 32, :, :], wgs.rearrange("(m t) j -> m t j", t=PACK))
+            stage["wg_last"] = wg_last
 
-        def prepare_w1b():
-            w1b_bf = ring.tile([P, 3 * P * PACK], BF16, name="w1b_bf", tag="sq_last", bufs=1, align_bytes=AL)
-            nc.scalar.activation(
-                w1b_bf[:].rearrange("p (t m j) -> p m t j", t=PACK - 1, j=PACK), by_slot[:, :, 1:PACK, :], ACT.Copy
-            )
-            stage[0] = quantised("w1b", w1b_bf, 3 * P, "after0_256")
+        def prepare_w1(g, bf_tag, codes_tag):
+            width = w1_raw[g].shape[2]
+            bf = shared([P, width * PACK], BF16, "w1_bf", bf_tag)
+            if g == LAST:
+                dst = bf[:].rearrange("p (t m j) -> p m t j", t=PACK, j=PACK)
+                rows = w1_raw[g][:].rearrange("p j (m t) -> p m t j", t=PACK)
+            else:
+                dst, rows = interleaved(bf[:], w1_raw[g][:])
+            nc.scalar.activation(dst, rows, ACT.Copy)
+            w1q[g] = quantised(f"w1_q{g}", bf, width, codes_tag)
 
-        def prepare_w1(g, tag):
-            w1c_bf = ring.tile([P, R_PASS * PACK], BF16, name="w1c_bf", tag=tag, bufs=1, align_bytes=AL)
-            nc.scalar.activation(
-                w1c_bf[:].rearrange("p (t m j) -> p m t j", t=PACK, j=PACK),
-                w1_rest[g][:].rearrange("p j (m t) -> p m t j", t=PACK),
-                ACT.Copy,
+        def prepare_w2_last(tag):
+            words = shared([P, 2 * R_PASS], U8, "w2c_last", tag)
+            nc.vector.tensor_copy(
+                words[:].bitcast(U16).rearrange("p (t m) -> p t m", t=PACK),
+                w2c[:, 2 * LAST * R_PASS : 2 * H].bitcast(U16).rearrange("p (m t) -> p t m", t=PACK),
             )
-            stage[g] = quantised(f"w1c{g}", w1c_bf, R_PASS)
+            scales = shared([P, R_PASS], U8, "w2s_last", "after1")
+            nc.vector.tensor_copy(
+                scales[:].rearrange("p (t m) -> p t m", t=PACK),
+                w2s_last_raw[:].rearrange("p (m t) -> p t m", t=PACK),
+            )
+            stage["w2_last"] = (words, scales)
 
         def prepare_w3(tag):
-            w3_bf = ring.tile([P, PASSES * N_OUT * PACK], BF16, name="w3_bf", tag=tag, bufs=1, align_bytes=AL)
+            w3_bf = shared([P, PASSES * N_OUT * PACK], BF16, "w3_bf", tag)
             for g in range(PASSES):
-                nc.scalar.activation(
-                    w3_bf[:, g * N_OUT * PACK : (g + 1) * N_OUT * PACK].rearrange(
-                        "p (c i j) -> p c j i", i=4, j=PACK
-                    ),
-                    stage["w3_raw"][:, g, :, :].rearrange("p j (c i) -> p c j i", i=4),
-                    ACT.Copy,
+                dst, rows = interleaved(
+                    w3_bf[:, g * N_OUT * PACK : (g + 1) * N_OUT * PACK], stage["w3_raw"][:, g, :, :]
                 )
+                nc.scalar.activation(dst, rows, ACT.Copy)
             stage["w3"] = quantised("w3", w3_bf, PASSES * N_OUT)
 
         def w1_operand(i):
+            g, t = divmod(i, PACK)
             if i == 0:
-                pair, col = w1a[i], 0
-            elif i < PACK:
-                pair, col = stage[0], (i - 1) * P
+                pair, col = w1q["first"], 0
             else:
-                pair, col = stage[i // PACK], (i % PACK) * P
+                pair, col = w1q[g], (t - 1 if g == 0 else t) * P
             return pair[0][:, col : col + P].bitcast(FP8X4), pair[1][:, col : col + P]
 
+        def w2_operand(i):
+            g, t = divmod(i, PACK)
+            if g == LAST:
+                words, scales = stage["w2_last"]
+                col = t * P
+            else:
+                words, scales = w2c, w2s
+                col = i * P
+            return words[:, 2 * col : 2 * (col + P)].bitcast(FP4X4), scales[:, col : col + P]
+
         def pieces(i):
-            if i == 0:
-                return [(0, 256), (256, 256), (512, 512)]
-            return [(0, S)]
+            return [(0, 256), (256, 256), (512, 512)] if i == 0 else [(0, S)]
+
+        def fetch_target(i):
+            g, t = divmod(i, PACK)
+            if t == 0:
+                diffs[g] = ring.tile([P, PACK, M_OUT], F32, name="d", tag="d", bufs=2)
+            if g == LAST:
+                fetched[i] = diffs[g][:, t, :]
+            else:
+                fetched[i] = ring.tile([P, M_OUT], F32, name="d_rows", tag="d_rows", bufs=3)[:]
+            return fetched[i]
 
         def signatures(i):
             if i == 0:
-                sig = [
-                    ring.tile([P, width], F32, name="sig", tag=f"after0_{first}", bufs=1, align_bytes=AL)[:]
-                    for first, width in pieces(i)
-                ]
+                sig = [shared([P, width], F32, "sig", f"after0_{first}")[:] for first, width in pieces(i)]
             elif i in HOLDS:
-                sig = [ring.tile([P, S], F32, name="sig", tag=f"after{i}", bufs=1, align_bytes=AL)[:]]
+                sig = [shared([P, S], F32, "sig", f"after{i}")[:]]
             else:
                 sig = [ring.tile([P, S], F32, name="sig", tag="sig", bufs=2)[:]]
             w1c, w1s = w1_operand(i)
-            w2s_tile = w2s_first[:, i * P : (i + 1) * P] if i < PACK else w2s_rest[:, (i - PACK) * P : (i - PACK + 1) * P]
+            w2w, w2p = w2_operand(i)
             for piece, (first, width) in enumerate(pieces(i)):
                 for c0 in range(first, first + width, HALF):
                     n = min(width, HALF)
@@ -212,10 +221,10 @@ def tile_list_phishing_verdict_slots_kernel(
                     b_ps = psum.tile([P, HALF], F32, name="b_ps", tag="b", bufs=3)
                     nc.tensor.matmul_mx(
                         out=b_ps[:, 0:n],
-                        lhsT=w2c[:, 2 * i * P : 2 * (i + 1) * P].bitcast(FP4X4),
-                        lhsT_scale=w2s_tile,
+                        lhsT=w2w,
+                        lhsT_scale=w2p,
                         rhs=vw[h][:, part].bitcast(FP8X4),
-                        rhs_scale=vs[:, c0 : c0 + n],
+                        rhs_scale=vs[h][:, part],
                         start=True,
                         stop=True,
                     )
@@ -225,23 +234,17 @@ def tile_list_phishing_verdict_slots_kernel(
                         lhsT=w1c,
                         lhsT_scale=w1s,
                         rhs=vw[h][:, part].bitcast(FP8X4),
-                        rhs_scale=vs[:, c0 : c0 + n],
+                        rhs_scale=vs[h][:, part],
                         start=True,
                         stop=True,
                     )
                     if i == 0 and h == 1:
-                        sq = ring.tile([P, HALF], F32, name="sq", tag="sq_last", bufs=1, align_bytes=AL)[:]
+                        sq = shared([P, HALF], F32, "sq", "sq_last")[:]
                     elif h == 1:
-                        lag_g, lag_t = divmod(i - 1, PACK)
-                        if lag_t == 0:
-                            diffs[lag_g] = ring.tile([P, PACK, M_OUT], F32, name="d", tag="d", bufs=2)
-                        sq = diffs[lag_g][:, lag_t, :]
+                        sq = fetch_target(i - 1)
                     else:
                         sq = ring.tile([P, HALF], F32, name="sq", tag="sq", bufs=2)[:]
-                    if i == 0 and c0 == 0:
-                        e = ring.tile([P, HALF], F32, name="e", tag="margin1", bufs=1, align_bytes=AL)
-                    else:
-                        e = ring.tile([P, HALF], F32, name="e", tag="e", bufs=4)
+                    e = ring.tile([P, HALF], F32, name="e", tag="e", bufs=4)
                     nc.scalar.activation(sq[:, 0:n], b_ps[:, 0:n], ACT.Square)
                     nc.scalar.activation(e[:, 0:n], sq[:, 0:n], ACT.Exp, scale=-1.0)
                     nc.vector.tensor_tensor(
@@ -250,13 +253,13 @@ def tile_list_phishing_verdict_slots_kernel(
             return sig
 
         def scatter(i, sig):
-            t = i % PACK
-            wg = wg0[:] if t == 0 else wg_rest[:, t - 1, :]
+            g, t = divmod(i, PACK)
+            weight = stage["wg_last"][:, t, :] if g == LAST else wg[:]
             for piece, (first, width) in enumerate(pieces(i)):
                 nc.vector.tensor_tensor(
-                    pages[i % PAGES][:].indirect(idx2[:, first // 16 : (first + width) // 16]),
+                    pages[i % 2][:].indirect(idx2[:, first // 16 : (first + width) // 16]),
                     sig[piece],
-                    wg[:, first : first + width],
+                    weight[:, first : first + width],
                     ALU.mult,
                 )
 
@@ -276,17 +279,16 @@ def tile_list_phishing_verdict_slots_kernel(
                     stop=stop,
                 )
 
-        def interleaved(z_bf, d_part):
-            return z_bf[:].rearrange("p (c i t) -> p c t i", i=4, t=PACK), d_part.rearrange("p t (c i) -> p c t i", i=4)
-
         def fetch(i):
             g, t = divmod(i, PACK)
-            d = diffs[g]
-            nc.vector.tensor_tensor(d[:, t, :], pages[i % PAGES][:].indirect(idx3[:]), margins[g][:, t, :], ALU.subtract)
+            nc.vector.tensor_tensor(fetched[i], pages[i % 2][:].indirect(idx3[:]), margins[g][:, t, :], ALU.subtract)
+            if g == LAST:
+                return
+            for j in range(PACK):
+                nc.sync.dma_start(diffs[g][32 * t : 32 * t + 32, j, :], fetched[i][j:P:PACK, :])
             if t == PACK - 1:
-                stage["z_bf"] = ring.tile([P, M_OUT * PACK], BF16, name="z_bf", tag="z_bf", bufs=1, align_bytes=AL)
-                dst, srcv = interleaved(stage["z_bf"], d[:, 0:PACK, :])
-                nc.scalar.activation(dst, srcv, ACT.Relu)
+                stage["z_bf"] = shared([P, M_OUT * PACK], BF16, "z_bf", "z_bf")
+                nc.scalar.activation(*interleaved(stage["z_bf"][:], diffs[g][:]), ACT.Relu)
 
         def close_pass(g, tag):
             zc, zs = quantised(f"z{g}", stage["z_bf"], M_OUT, tag)
@@ -294,48 +296,48 @@ def tile_list_phishing_verdict_slots_kernel(
 
         def last_tile():
             i = TILES - 1
-            g, t = divmod(i, PACK)
-            d = diffs[g]
+            d = diffs[LAST]
             width = M_OUT // 2
             halves = [slice(0, width), slice(width, M_OUT)]
             for cols in halves:
                 nc.vector.tensor_tensor(
-                    d[:, t, cols],
-                    pages[i % PAGES][:].indirect(idx3[:, cols.start // 16 : cols.stop // 16]),
-                    margins[g][:, t, cols],
+                    d[:, PACK - 1, cols],
+                    pages[i % 2][:].indirect(idx3[:, cols.start // 16 : cols.stop // 16]),
+                    margins[LAST][:, PACK - 1, cols],
                     ALU.subtract,
                 )
             z_lo = keep.tile([P, width * PACK], BF16, name="z_lo", align_bytes=AL)
             z_hi = keep.tile([P, width * PACK], BF16, name="z_hi", align_bytes=AL)
-            dst, srcv = interleaved(z_lo, d[:, 0:PACK, halves[0]])
-            nc.scalar.activation(dst, srcv, ACT.Relu)
-            dst, srcv = interleaved(z_hi, d[:, 0:PACK, halves[1]])
-            nc.vector.tensor_scalar_max(dst, srcv, 0.0)
+            nc.scalar.activation(*interleaved(z_lo[:], d[:, :, halves[0]]), ACT.Relu)
+            nc.vector.tensor_scalar_max(*interleaved(z_hi[:], d[:, :, halves[1]]), 0.0)
             zc, zs = quantised("zhi", z_hi, width)
-            score(g, zc, zs, halves[1], False)
+            score(LAST, zc, zs, halves[1], False)
             zc, zs = quantised("zlo", z_lo, width)
-            score(g, zc, zs, halves[0], True)
+            score(LAST, zc, zs, halves[0], True)
 
         for i in range(TILES):
-            hw = signatures(i)
+            sig = signatures(i)
             if i >= 1:
                 fetch(i - 1)
-            scatter(i, hw)
+            scatter(i, sig)
             if i == 0:
-                load_w1(1, "margin1")
-                load_margin(0, "after0_0")
-                prepare_w1b()
-                prepare_w1(1, "after0_512")
+                load_margin(0, "table")
+                prepare_w1(0, "sq_last", "after0_256")
+                w1_raw[1] = load_w1(slice(R_PASS, 2 * R_PASS), "after0_0")
+                prepare_w1(1, "after0_512", None)
+                load_last_weights()
+                load_scale_rows(nc.sync, w2s_last_raw, w2_scales[0, :, LAST * R_PASS : H])
             if i == 1:
-                load_margin(1, "margin1")
+                load_margin(1, "after0_0")
                 load_w3("after1")
             if i == 2:
-                load_w1(2, "after2")
+                w1_raw[LAST] = load_w1(slice(LAST * R_PASS, H), "after2")
             if i == 3:
                 prepare_w3("after3")
+                prepare_w2_last("after0_256")
             if i == 4:
-                prepare_w1(2, "after4")
-                load_margin(2, "after0_0")
+                prepare_w1(LAST, "after4", None)
+                load_margin(LAST, "table")
             if i in (5, 9):
                 close_pass(i // PACK - 1, f"after{i}")
         last_tile()

@@ -19,13 +19,25 @@ ALU = mybir.AluOpType
 P = 128
 PACK = 4
 QUADS = 4
+QUAD = P // QUADS
+PER_COLUMN = 16
 R_PASS = P * PACK
 PASSES = H // R_PASS
 LAST = PASSES - 1
 TILES = H // P
 HALF = 512
-AL = 64
-HOLDS = (1, 2, 3, 4, 5, 9)
+ALIGN = 64
+QUANT_WORDS = (128, 256, 512, 1024)
+RUN = 4
+
+FIRST_PIECES = ((0, 256), (256, 256), (512, 512))
+
+LOAD_W3_AFTER = 1
+LOAD_W1_LAST_AFTER = 2
+CAST_W3_AFTER = 3
+CAST_W1_LAST_AFTER = 4
+CLOSE_PASS_AFTER = tuple(PACK * (g + 1) + 1 for g in range(LAST))
+TIMING_TILES = (LOAD_W3_AFTER, LOAD_W1_LAST_AFTER, CAST_W3_AFTER, CAST_W1_LAST_AFTER) + CLOSE_PASS_AFTER
 
 
 def tile_list_phishing_verdict_slots_kernel(
@@ -38,24 +50,35 @@ def tile_list_phishing_verdict_slots_kernel(
         ring = ctx.enter_context(tc.tile_pool(name="ring", bufs=1))
         psum = ctx.enter_context(tc.psum_pool(name="psum", bufs=1))
 
-        def shared(shape, dtype, name, tag):
-            return ring.tile(shape, dtype, name=name, tag=tag, bufs=1, align_bytes=AL)
+        def tenant(shape, dtype, name, tag):
+            return ring.tile(shape, dtype, name=name, tag=tag, bufs=1, align_bytes=ALIGN)
 
-        def load_scale_rows(queue, plane, rows):
+        def entries(offsets, first, count):
+            return offsets[:, first // PER_COLUMN : (first + count) // PER_COLUMN]
+
+        def load_scale_rows(scale_tile, rows):
             for q in range(QUADS):
-                queue.dma_start(plane[32 * q : 32 * q + 4, :].bitcast(I32), rows[4 * q : 4 * q + 4, :].bitcast(I32))
+                nc.sync.dma_start(
+                    scale_tile[QUAD * q : QUAD * q + PACK, :].bitcast(I32),
+                    rows[PACK * q : PACK * (q + 1), :].bitcast(I32),
+                )
 
         def load_w1(cols, tag):
-            raw = shared([P, PACK, cols.stop - cols.start], F32, "w1_raw", tag)
+            raw = tenant([P, PACK, cols.stop - cols.start], F32, "w1_raw", tag)
             nc.sync.dma_start(raw[:], w1[:, cols].rearrange("(p j) c -> p j c", j=PACK))
             return raw
 
+        def load_w2_words(g):
+            words = keep.tile([P, 2 * R_PASS], U8, name=f"w2_w{g}", align_bytes=ALIGN)
+            nc.sync.dma_start(words[:].bitcast(I32), w2_words[0, :, 2 * g * R_PASS : 2 * (g + 1) * R_PASS].bitcast(I32))
+            return words
+
         def quantised(name, grouped, width, tag=None):
-            codes = shared([P, width], U32, name + "_codes", tag or name)
-            scales = keep.tile([P, width], U8, name=name + "_scales", align_bytes=AL)
+            codes = tenant([P, width], U32, name + "_codes", tag or name)
+            scales = keep.tile([P, width], U8, name=name + "_scales", align_bytes=ALIGN)
             done = 0
             while done < width:
-                step = max(w for w in (128, 256, 512, 1024) if w <= width - done)
+                step = max(w for w in QUANT_WORDS if w <= width - done)
                 nc.vector.quantize_mx(
                     out=codes[:, done : done + step].bitcast(FP8X4),
                     scales=scales[:, done : done + step],
@@ -66,215 +89,215 @@ def tile_list_phishing_verdict_slots_kernel(
 
         def interleaved(grouped, rows):
             return (
-                grouped.rearrange("p (c i j) -> p c j i", i=4, j=PACK),
-                rows.rearrange("p j (c i) -> p c j i", i=4),
+                grouped.rearrange("p (c i j) -> p c j i", i=RUN, j=PACK),
+                rows.rearrange("p j (c i) -> p c j i", i=RUN),
             )
 
-        idx = lists.tile([P, S // 16], U16, name="idx")
-        idx2 = lists.tile([P, S // 16], U16, name="idx2")
-        idx3 = lists.tile([P, M_OUT // 16], U16, name="idx3")
+        idx = lists.tile([P, S // PER_COLUMN], U16, name="idx")
+        idx2 = lists.tile([P, S // PER_COLUMN], U16, name="idx2")
+        idx3 = lists.tile([P, M_OUT // PER_COLUMN], U16, name="idx3")
 
-        ts_rows = shared([P, T], U8, "ts_rows", "ts_rows")
-        load_scale_rows(nc.sync, ts_rows, tab_scales[0])
+        tab_scale_rows = tenant([P, T], U8, "tab_scale_rows", "scale_rows")
+        load_scale_rows(tab_scale_rows, tab_scales[0])
         nc.sync.dma_start(idx[:], offs)
         w1_first = load_w1(slice(0, P), "w1_first")
-        tw = shared([P, T], I32, "tw", "table")
-        nc.sync.dma_start(tw[:], tab_words[0].rearrange("p t i -> p (t i)").bitcast(I32))
-        w2c = keep.tile([P, 2 * H], U8, name="w2c", align_bytes=AL)
-        nc.sync.dma_start(w2c[:].bitcast(I32), w2_words[0].bitcast(I32))
-        w2s = keep.tile([P, LAST * R_PASS], U8, name="w2s", align_bytes=AL)
-        load_scale_rows(nc.gpsimd, w2s, w2_scales[0, :, 0 : LAST * R_PASS])
-        wg = keep.tile([P, S], F32, name="wg")
-        nc.sync.dma_start(wg[:], wgs)
+        tab_w = tenant([P, T], I32, "tab_w", "table")
+        nc.sync.dma_start(tab_w[:], tab_words[0].rearrange("p t i -> p (t i)").bitcast(I32))
+        w2_w = {0: load_w2_words(0)}
+        w2_s = keep.tile([P, LAST * R_PASS], U8, name="w2_s", align_bytes=ALIGN)
+        load_scale_rows(w2_s, w2_scales[0, :, 0 : LAST * R_PASS])
+        weights = keep.tile([P, S], F32, name="weights")
+        nc.sync.dma_start(weights[:], wgs)
         nc.sync.dma_start(idx2[:], offs2)
         nc.sync.dma_start(idx3[:], offs3)
         w1_raw = {0: load_w1(slice(P, R_PASS), "w1_pass0")}
+        for g in range(1, PASSES):
+            w2_w[g] = load_w2_words(g)
 
-        ts = keep.tile([P, T], U8, name="ts", align_bytes=AL)
-        nc.vector.memset(ts[:].bitcast(I32), 0)
-        page0 = keep.tile([P, T2], F32, name="page0")
-        nc.vector.memset(page0[:], 0.0)
+        tab_s = keep.tile([P, T], U8, name="tab_s", align_bytes=ALIGN)
+        nc.vector.memset(tab_s[:].bitcast(I32), 0)
+        page_even = keep.tile([P, T2], F32, name="page_even")
+        nc.vector.memset(page_even[:], 0.0)
         for q in range(QUADS):
-            rows = slice(32 * q, 32 * q + 4)
-            nc.vector.tensor_copy(ts[rows, :].bitcast(I32), ts_rows[rows, :].bitcast(I32))
-        w2s_last_raw = shared([P, R_PASS], U8, "w2s_last_raw", "ts_rows")
-        nc.gpsimd.memset(w2s_last_raw[:].bitcast(I32), 0)
+            live = slice(QUAD * q, QUAD * q + PACK)
+            nc.vector.tensor_copy(tab_s[live, :].bitcast(I32), tab_scale_rows[live, :].bitcast(I32))
+        w2_s_last_raw = tenant([P, R_PASS], U8, "w2_s_last_raw", "scale_rows")
+        nc.gpsimd.memset(w2_s_last_raw[:].bitcast(I32), 0)
 
-        first_bf = shared([P, P * PACK], BF16, "first_bf", "page1")
-        nc.vector.tensor_copy(*interleaved(first_bf[:], w1_first[:]))
-        w1q = {"first": quantised("w1_tile0", first_bf, P)}
-        page1 = shared([P, T2], F32, "page1", "page1")
-        nc.gpsimd.memset(page1[:], 0.0)
-        pages = [page0, page1]
+        first_bf = tenant([P, P * PACK], BF16, "first_bf", "page_odd")
+        nc.scalar.activation(*interleaved(first_bf[:], w1_first[:]), ACT.Copy)
+        w1_q_first = quantised("w1_tile0", first_bf, P)
+        page_odd = tenant([P, T2], F32, "page_odd", "page_odd")
+        nc.gpsimd.memset(page_odd[:], 0.0)
+        pages = [page_even, page_odd]
 
-        vs = [keep.tile([P, HALF], U8, name=f"vs{h}", align_bytes=AL) for h in range(2)]
-        vw = [keep.tile([P, HALF], U32, name=f"vw{h}", align_bytes=AL) for h in range(2)]
-        for h in range(2):
-            nc.vector.tensor_copy(vs[h][:], ts[:].indirect(idx[:, 32 * h : 32 * h + 32]))
-            nc.vector.tensor_copy(vw[h][:], tw[:].bitcast(U32).indirect(idx[:, 32 * h : 32 * h + 32]))
+        v_s = [keep.tile([P, HALF], U8, name=f"v_s{h}", align_bytes=ALIGN) for h in range(S // HALF)]
+        v_w = [keep.tile([P, HALF], U32, name=f"v_w{h}", align_bytes=ALIGN) for h in range(S // HALF)]
+        for h in range(S // HALF):
+            nc.vector.tensor_copy(v_s[h][:], tab_s[:].indirect(entries(idx, h * HALF, HALF)))
+            nc.vector.tensor_copy(v_w[h][:], tab_w[:].bitcast(U32).indirect(entries(idx, h * HALF, HALF)))
 
+        w1_q = {}
         margins = {}
-        stage = {}
         diffs = {}
         fetched = {}
+        made = {}
 
         def load_margin(g, tag):
-            margins[g] = shared([P, PACK, M_OUT], F32, "margin", tag)
-            rows = margin[g * R_PASS : (g + 1) * R_PASS, :]
-            if g == LAST:
-                nc.sync.dma_start(margins[g][:], rows.rearrange("(p t) m -> p t m", t=PACK))
-            else:
-                nc.sync.dma_start(margins[g][:], rows.rearrange("(t p) m -> p t m", t=PACK))
+            margins[g] = tenant([P, PACK, M_OUT], F32, "margin", tag)
+            order = "(p t) m -> p t m" if g == LAST else "(t p) m -> p t m"
+            nc.sync.dma_start(margins[g][:], margin[g * R_PASS : (g + 1) * R_PASS, :].rearrange(order, t=PACK))
 
         def load_w3(tag):
-            w3_raw = shared([P, PASSES, PACK, N_OUT], F32, "w3_raw", tag)
+            w3_raw = tenant([P, PASSES, PACK, N_OUT], F32, "w3_raw", tag)
             for g in range(PASSES):
                 nc.sync.dma_start(
                     w3_raw[:, g, :, :], w3[g * R_PASS : (g + 1) * R_PASS, :].rearrange("(p j) n -> p j n", j=PACK)
                 )
-            stage["w3_raw"] = w3_raw
+            made["w3_raw"] = w3_raw
 
-        def load_last_weights():
-            wg_last = shared([P, PACK, S], F32, "wg_last", "w1_pass0")
+        def load_last_weights(tag):
+            weights_last = tenant([P, PACK, S], F32, "weights_last", tag)
             for q in range(QUADS):
-                nc.sync.dma_start(wg_last[32 * q : 32 * q + 32, :, :], wgs.rearrange("(m t) j -> m t j", t=PACK))
-            stage["wg_last"] = wg_last
+                nc.sync.dma_start(
+                    weights_last[QUAD * q : QUAD * (q + 1), :, :], wgs.rearrange("(u t) j -> u t j", t=PACK)
+                )
+            made["weights_last"] = weights_last
 
-        def prepare_w1(g, bf_tag, codes_tag):
+        def prepare_w1(g, bf_tag, codes_tag=None):
             width = w1_raw[g].shape[2]
-            bf = shared([P, width * PACK], BF16, "w1_bf", bf_tag)
+            bf = tenant([P, width * PACK], BF16, "w1_bf", bf_tag)
             if g == LAST:
-                dst = bf[:].rearrange("p (t m j) -> p m t j", t=PACK, j=PACK)
-                rows = w1_raw[g][:].rearrange("p j (m t) -> p m t j", t=PACK)
+                dst = bf[:].rearrange("p (t u j) -> p u t j", t=PACK, j=PACK)
+                rows = w1_raw[g][:].rearrange("p j (u t) -> p u t j", t=PACK)
             else:
                 dst, rows = interleaved(bf[:], w1_raw[g][:])
             nc.scalar.activation(dst, rows, ACT.Copy)
-            w1q[g] = quantised(f"w1_q{g}", bf, width, codes_tag)
+            w1_q[g] = quantised(f"w1_q{g}", bf, width, codes_tag)
 
-        def prepare_w2_last(tag):
-            words = shared([P, 2 * R_PASS], U8, "w2c_last", tag)
+        def prepare_w2_last(words_tag, scales_tag):
+            words = tenant([P, 2 * R_PASS], U8, "w2_w_last", words_tag)
             nc.vector.tensor_copy(
-                words[:].bitcast(U16).rearrange("p (t m) -> p t m", t=PACK),
-                w2c[:, 2 * LAST * R_PASS : 2 * H].bitcast(U16).rearrange("p (m t) -> p t m", t=PACK),
+                words[:].bitcast(U16).rearrange("p (t u) -> p t u", t=PACK),
+                w2_w[LAST][:].bitcast(U16).rearrange("p (u t) -> p t u", t=PACK),
             )
-            scales = shared([P, R_PASS], U8, "w2s_last", "after1")
+            scales = tenant([P, R_PASS], U8, "w2_s_last", scales_tag)
             nc.vector.tensor_copy(
-                scales[:].rearrange("p (t m) -> p t m", t=PACK),
-                w2s_last_raw[:].rearrange("p (m t) -> p t m", t=PACK),
+                scales[:].rearrange("p (t u) -> p t u", t=PACK),
+                w2_s_last_raw[:].rearrange("p (u t) -> p t u", t=PACK),
             )
-            stage["w2_last"] = (words, scales)
+            made["w2_last"] = (words, scales)
 
         def prepare_w3(tag):
-            w3_bf = shared([P, PASSES * N_OUT * PACK], BF16, "w3_bf", tag)
+            w3_bf = tenant([P, PASSES * N_OUT * PACK], BF16, "w3_bf", tag)
             for g in range(PASSES):
                 dst, rows = interleaved(
-                    w3_bf[:, g * N_OUT * PACK : (g + 1) * N_OUT * PACK], stage["w3_raw"][:, g, :, :]
+                    w3_bf[:, g * N_OUT * PACK : (g + 1) * N_OUT * PACK], made["w3_raw"][:, g, :, :]
                 )
                 nc.scalar.activation(dst, rows, ACT.Copy)
-            stage["w3"] = quantised("w3", w3_bf, PASSES * N_OUT)
+            made["w3_q"] = quantised("w3", w3_bf, PASSES * N_OUT)
 
         def w1_operand(i):
             g, t = divmod(i, PACK)
             if i == 0:
-                pair, col = w1q["first"], 0
+                (codes, scales), col = w1_q_first, 0
             else:
-                pair, col = w1q[g], (t - 1 if g == 0 else t) * P
-            return pair[0][:, col : col + P].bitcast(FP8X4), pair[1][:, col : col + P]
+                (codes, scales), col = w1_q[g], (t - 1 if g == 0 else t) * P
+            return codes[:, col : col + P].bitcast(FP8X4), scales[:, col : col + P]
 
         def w2_operand(i):
             g, t = divmod(i, PACK)
             if g == LAST:
-                words, scales = stage["w2_last"]
-                col = t * P
+                words, scales = made["w2_last"]
             else:
-                words, scales = w2c, w2s
-                col = i * P
-            return words[:, 2 * col : 2 * (col + P)].bitcast(FP4X4), scales[:, col : col + P]
+                words, scales = w2_w[g], w2_s[:, g * R_PASS : (g + 1) * R_PASS]
+            return words[:, 2 * t * P : 2 * (t + 1) * P].bitcast(FP4X4), scales[:, t * P : (t + 1) * P]
 
         def pieces(i):
-            return [(0, 256), (256, 256), (512, 512)] if i == 0 else [(0, S)]
+            return FIRST_PIECES if i == 0 else ((0, S),)
 
         def fetch_target(i):
             g, t = divmod(i, PACK)
             if t == 0:
-                diffs[g] = ring.tile([P, PACK, M_OUT], F32, name="d", tag="d", bufs=2)
+                diffs[g] = ring.tile([P, PACK, M_OUT], F32, name="diffs", tag="diffs", bufs=2)
             if g == LAST:
                 fetched[i] = diffs[g][:, t, :]
             else:
-                fetched[i] = ring.tile([P, M_OUT], F32, name="d_rows", tag="d_rows", bufs=3)[:]
+                fetched[i] = ring.tile([P, M_OUT], F32, name="diff_rows", tag="diff_rows", bufs=3)[:]
             return fetched[i]
 
         def signatures(i):
             if i == 0:
-                sig = [shared([P, width], F32, "sig", f"after0_{first}")[:] for first, width in pieces(i)]
-            elif i in HOLDS:
-                sig = [shared([P, S], F32, "sig", f"after{i}")[:]]
+                sig = [tenant([P, count], F32, "sig", f"after_piece{first}")[:] for first, count in pieces(i)]
+            elif i in TIMING_TILES:
+                sig = [tenant([P, S], F32, "sig", f"after_scatter{i}")[:]]
             else:
                 sig = [ring.tile([P, S], F32, name="sig", tag="sig", bufs=2)[:]]
-            w1c, w1s = w1_operand(i)
-            w2w, w2p = w2_operand(i)
-            for piece, (first, width) in enumerate(pieces(i)):
-                for c0 in range(first, first + width, HALF):
-                    n = min(width, HALF)
+            w1_codes, w1_scale = w1_operand(i)
+            w2_codes, w2_scale = w2_operand(i)
+            for piece, (first, count) in enumerate(pieces(i)):
+                for c0 in range(first, first + count, HALF):
+                    n = min(count, HALF)
                     h = c0 // HALF
                     part = slice(c0 - h * HALF, c0 - h * HALF + n)
                     b_ps = psum.tile([P, HALF], F32, name="b_ps", tag="b", bufs=3)
                     nc.tensor.matmul_mx(
                         out=b_ps[:, 0:n],
-                        lhsT=w2w,
-                        lhsT_scale=w2p,
-                        rhs=vw[h][:, part].bitcast(FP8X4),
-                        rhs_scale=vs[h][:, part],
+                        lhsT=w2_codes,
+                        lhsT_scale=w2_scale,
+                        rhs=v_w[h][:, part].bitcast(FP8X4),
+                        rhs_scale=v_s[h][:, part],
                         start=True,
                         stop=True,
                     )
                     a_ps = psum.tile([P, HALF], F32, name="a_ps", tag="a", bufs=2)
                     nc.tensor.matmul_mx(
                         out=a_ps[:, 0:n],
-                        lhsT=w1c,
-                        lhsT_scale=w1s,
-                        rhs=vw[h][:, part].bitcast(FP8X4),
-                        rhs_scale=vs[h][:, part],
+                        lhsT=w1_codes,
+                        lhsT_scale=w1_scale,
+                        rhs=v_w[h][:, part].bitcast(FP8X4),
+                        rhs_scale=v_s[h][:, part],
                         start=True,
                         stop=True,
                     )
-                    if i == 0 and h == 1:
-                        sq = shared([P, HALF], F32, "sq", "sq_last")[:]
-                    elif h == 1:
-                        sq = fetch_target(i - 1)
+                    if h == 0:
+                        square = ring.tile([P, HALF], F32, name="square", tag="square", bufs=2)[:]
+                    elif i == 0:
+                        square = tenant([P, HALF], F32, "square", "after_first_exps")[:]
                     else:
-                        sq = ring.tile([P, HALF], F32, name="sq", tag="sq", bufs=2)[:]
-                    e = ring.tile([P, HALF], F32, name="e", tag="e", bufs=4)
-                    nc.scalar.activation(sq[:, 0:n], b_ps[:, 0:n], ACT.Square)
-                    nc.scalar.activation(e[:, 0:n], sq[:, 0:n], ACT.Exp, scale=-1.0)
+                        square = fetch_target(i - 1)
+                    damp = ring.tile([P, HALF], F32, name="damp", tag="damp", bufs=4)
+                    nc.scalar.activation(square[:, 0:n], b_ps[:, 0:n], ACT.Square)
+                    nc.scalar.activation(damp[:, 0:n], square[:, 0:n], ACT.Exp, scale=-1.0)
                     nc.vector.tensor_tensor(
-                        sig[piece][:, c0 - first : c0 - first + n], a_ps[:, 0:n], e[:, 0:n], ALU.mult
+                        sig[piece][:, c0 - first : c0 - first + n], a_ps[:, 0:n], damp[:, 0:n], ALU.mult
                     )
             return sig
 
         def scatter(i, sig):
             g, t = divmod(i, PACK)
-            weight = stage["wg_last"][:, t, :] if g == LAST else wg[:]
-            for piece, (first, width) in enumerate(pieces(i)):
+            weight = made["weights_last"][:, t, :] if g == LAST else weights[:]
+            for piece, (first, count) in enumerate(pieces(i)):
                 nc.vector.tensor_tensor(
-                    pages[i % 2][:].indirect(idx2[:, first // 16 : (first + width) // 16]),
+                    pages[i % 2][:].indirect(entries(idx2, first, count)),
                     sig[piece],
-                    weight[:, first : first + width],
+                    weight[:, first : first + count],
                     ALU.mult,
                 )
 
         out_ps = [psum.tile([P, M_OUT], F32, name=f"out_ps{n}") for n in range(N_OUT // P)]
 
-        def score(g, zc, zs, cols, stop):
-            w3c, w3s = stage["w3"]
+        def score(g, z_q, cols, stop):
+            w3_codes, w3_scale = made["w3_q"]
+            z_codes, z_scale = z_q
             for n in range(N_OUT // P):
-                wcols = slice(g * N_OUT + n * P, g * N_OUT + (n + 1) * P)
+                w3_cols = slice(g * N_OUT + n * P, g * N_OUT + (n + 1) * P)
                 nc.tensor.matmul_mx(
                     out=out_ps[n][:, cols],
-                    lhsT=w3c[:, wcols].bitcast(FP8X4),
-                    lhsT_scale=w3s[:, wcols],
-                    rhs=zc[:].bitcast(FP8X4),
-                    rhs_scale=zs[:],
+                    lhsT=w3_codes[:, w3_cols].bitcast(FP8X4),
+                    lhsT_scale=w3_scale[:, w3_cols],
+                    rhs=z_codes[:].bitcast(FP8X4),
+                    rhs_scale=z_scale[:],
                     start=(g == 0),
                     stop=stop,
                 )
@@ -285,67 +308,64 @@ def tile_list_phishing_verdict_slots_kernel(
             if g == LAST:
                 return
             for j in range(PACK):
-                nc.sync.dma_start(diffs[g][32 * t : 32 * t + 32, j, :], fetched[i][j:P:PACK, :])
+                nc.sync.dma_start(diffs[g][QUAD * t : QUAD * (t + 1), j, :], fetched[i][j:P:PACK, :])
             if t == PACK - 1:
-                stage["z_bf"] = shared([P, M_OUT * PACK], BF16, "z_bf", "z_bf")
-                nc.scalar.activation(*interleaved(stage["z_bf"][:], diffs[g][:]), ACT.Relu)
+                made["z_bf"] = tenant([P, M_OUT * PACK], BF16, "z_bf", "z_bf")
+                nc.scalar.activation(*interleaved(made["z_bf"][:], diffs[g][:]), ACT.Relu)
 
         def close_pass(g, tag):
-            zc, zs = quantised(f"z{g}", stage["z_bf"], M_OUT, tag)
-            score(g, zc, zs, slice(0, M_OUT), False)
+            score(g, quantised(f"z{g}", made["z_bf"], M_OUT, tag), slice(0, M_OUT), False)
 
-        def last_tile():
-            i = TILES - 1
-            d = diffs[LAST]
+        def finish_last_pass():
             width = M_OUT // 2
-            halves = [slice(0, width), slice(width, M_OUT)]
-            for cols in halves:
+            low, high = slice(0, width), slice(width, M_OUT)
+            for cols in (low, high):
                 nc.vector.tensor_tensor(
-                    d[:, PACK - 1, cols],
-                    pages[i % 2][:].indirect(idx3[:, cols.start // 16 : cols.stop // 16]),
+                    diffs[LAST][:, PACK - 1, cols],
+                    pages[(TILES - 1) % 2][:].indirect(entries(idx3, cols.start, width)),
                     margins[LAST][:, PACK - 1, cols],
                     ALU.subtract,
                 )
-            z_lo = keep.tile([P, width * PACK], BF16, name="z_lo", align_bytes=AL)
-            z_hi = keep.tile([P, width * PACK], BF16, name="z_hi", align_bytes=AL)
-            nc.scalar.activation(*interleaved(z_lo[:], d[:, :, halves[0]]), ACT.Relu)
-            nc.vector.tensor_scalar_max(*interleaved(z_hi[:], d[:, :, halves[1]]), 0.0)
-            zc, zs = quantised("zhi", z_hi, width)
-            score(LAST, zc, zs, halves[1], False)
-            zc, zs = quantised("zlo", z_lo, width)
-            score(LAST, zc, zs, halves[0], True)
+            z_low = keep.tile([P, width * PACK], BF16, name="z_low", align_bytes=ALIGN)
+            z_high = keep.tile([P, width * PACK], BF16, name="z_high", align_bytes=ALIGN)
+            nc.scalar.activation(*interleaved(z_low[:], diffs[LAST][:, :, low]), ACT.Relu)
+            nc.vector.tensor_scalar_max(*interleaved(z_high[:], diffs[LAST][:, :, high]), 0.0)
+            score(LAST, quantised("z_high", z_high, width), high, False)
+            score(LAST, quantised("z_low", z_low, width), low, True)
 
+        piece_tags = [f"after_piece{first}" for first, count in FIRST_PIECES]
         for i in range(TILES):
             sig = signatures(i)
             if i >= 1:
                 fetch(i - 1)
             scatter(i, sig)
+            after_scatter = f"after_scatter{i}"
             if i == 0:
                 load_margin(0, "table")
-                prepare_w1(0, "sq_last", "after0_256")
-                w1_raw[1] = load_w1(slice(R_PASS, 2 * R_PASS), "after0_0")
-                prepare_w1(1, "after0_512", None)
-                load_last_weights()
-                load_scale_rows(nc.sync, w2s_last_raw, w2_scales[0, :, LAST * R_PASS : H])
-            if i == 1:
-                load_margin(1, "after0_0")
-                load_w3("after1")
-            if i == 2:
-                w1_raw[LAST] = load_w1(slice(LAST * R_PASS, H), "after2")
-            if i == 3:
-                prepare_w3("after3")
-                prepare_w2_last("after0_256")
-            if i == 4:
-                prepare_w1(LAST, "after4", None)
+                prepare_w1(0, "after_first_exps", piece_tags[1])
+                w1_raw[1] = load_w1(slice(R_PASS, 2 * R_PASS), piece_tags[0])
+                prepare_w1(1, piece_tags[2])
+                load_last_weights("w1_pass0")
+                load_scale_rows(w2_s_last_raw, w2_scales[0, :, LAST * R_PASS : H])
+            if i == LOAD_W3_AFTER:
+                load_margin(1, piece_tags[0])
+                load_w3(after_scatter)
+            if i == LOAD_W1_LAST_AFTER:
+                w1_raw[LAST] = load_w1(slice(LAST * R_PASS, H), after_scatter)
+            if i == CAST_W3_AFTER:
+                prepare_w3(after_scatter)
+                prepare_w2_last(piece_tags[1], f"after_scatter{LOAD_W3_AFTER}")
+            if i == CAST_W1_LAST_AFTER:
+                prepare_w1(LAST, after_scatter)
                 load_margin(LAST, "table")
-            if i in (5, 9):
-                close_pass(i // PACK - 1, f"after{i}")
-        last_tile()
+            if i in CLOSE_PASS_AFTER:
+                close_pass(CLOSE_PASS_AFTER.index(i), after_scatter)
+        finish_last_pass()
 
         for n in range(N_OUT // P):
-            res = keep.tile([P, M_OUT], F32, name=f"res{n}")
-            if n == 1:
-                nc.scalar.copy(res[:], out_ps[n][:])
+            result = keep.tile([P, M_OUT], F32, name=f"result{n}")
+            if n % 2 == 1:
+                nc.scalar.copy(result[:], out_ps[n][:])
             else:
-                nc.vector.tensor_copy(res[:], out_ps[n][:])
-            nc.sync.dma_start(out[n * P : (n + 1) * P, :], res[:])
+                nc.vector.tensor_copy(result[:], out_ps[n][:])
+            nc.sync.dma_start(out[n * P : (n + 1) * P, :], result[:])

@@ -32,12 +32,11 @@ RUN = 4
 
 FIRST_PIECES = ((0, 256), (256, 256), (512, 512))
 
-LOAD_W3_AFTER = 1
-LOAD_W1_LAST_AFTER = 2
-CAST_W3_AFTER = 3
-CAST_W1_LAST_AFTER = 4
-CLOSE_PASS_AFTER = tuple(PACK * (g + 1) + 1 for g in range(LAST))
-TIMING_TILES = (LOAD_W3_AFTER, LOAD_W1_LAST_AFTER, CAST_W3_AFTER, CAST_W1_LAST_AFTER) + CLOSE_PASS_AFTER
+CAST_W1_BEFORE = {1: 2, LAST: 6}
+CAST_W3_BEFORE = 4
+REORDER_W2_BEFORE = 7
+CLOSE_PASS_BEFORE = tuple(PACK * (g + 1) + 2 for g in range(LAST))
+RING = 3
 
 
 def tile_list_phishing_verdict_slots_kernel(
@@ -111,8 +110,34 @@ def tile_list_phishing_verdict_slots_kernel(
         nc.sync.dma_start(idx2[:], offs2)
         nc.sync.dma_start(idx3[:], offs3)
         w1_raw = {0: load_w1(slice(P, R_PASS), "w1_pass0")}
-        for g in range(1, PASSES):
-            w2_w[g] = load_w2_words(g)
+        margins = {}
+
+        def load_margin(i):
+            g, t = divmod(i, PACK)
+            margins[i] = tenant([P, M_OUT], F32, "margin", f"margin_ew{i % RING}")
+            if g == LAST:
+                rows = margin[g * R_PASS : (g + 1) * R_PASS, :].rearrange("(p t) m -> p t m", t=PACK)[:, t, :]
+            else:
+                rows = margin[i * P : (i + 1) * P, :]
+            nc.sync.dma_start(margins[i][:], rows)
+
+        load_margin(0)
+        w1_raw[1] = load_w1(slice(R_PASS, 2 * R_PASS), "w1_pass1")
+        w2_w[1] = load_w2_words(1)
+        for i in range(1, RING):
+            load_margin(i)
+        w3_raw = keep.tile([P, PASSES, PACK, N_OUT], F32, name="w3_raw")
+        for g in range(PASSES):
+            nc.sync.dma_start(
+                w3_raw[:, g, :, :], w3[g * R_PASS : (g + 1) * R_PASS, :].rearrange("(p j) n -> p j n", j=PACK)
+            )
+        w1_raw[LAST] = load_w1(slice(LAST * R_PASS, H), "w1_last")
+        w2_w[LAST] = load_w2_words(LAST)
+        weights_last = keep.tile([P, PACK, S], F32, name="weights_last")
+        for q in range(QUADS):
+            nc.sync.dma_start(
+                weights_last[QUAD * q : QUAD * (q + 1), :, :], wgs.rearrange("(u t) j -> u t j", t=PACK)
+            )
 
         tab_s = keep.tile([P, T], U8, name="tab_s", align_bytes=ALIGN)
         nc.vector.memset(tab_s[:].bitcast(I32), 0)
@@ -123,6 +148,7 @@ def tile_list_phishing_verdict_slots_kernel(
             nc.vector.tensor_copy(tab_s[live, :].bitcast(I32), tab_scale_rows[live, :].bitcast(I32))
         w2_s_last_raw = tenant([P, R_PASS], U8, "w2_s_last_raw", "scale_rows")
         nc.gpsimd.memset(w2_s_last_raw[:].bitcast(I32), 0)
+        load_scale_rows(w2_s_last_raw, w2_scales[0, :, LAST * R_PASS : H])
 
         first_bf = tenant([P, P * PACK], BF16, "first_bf", "page_odd")
         nc.scalar.activation(*interleaved(first_bf[:], w1_first[:]), ACT.Copy)
@@ -138,31 +164,9 @@ def tile_list_phishing_verdict_slots_kernel(
             nc.vector.tensor_copy(v_w[h][:], tab_w[:].bitcast(U32).indirect(entries(idx, h * HALF, HALF)))
 
         w1_q = {}
-        margins = {}
         diffs = {}
         fetched = {}
         made = {}
-
-        def load_margin(g, tag):
-            margins[g] = tenant([P, PACK, M_OUT], F32, "margin", tag)
-            order = "(p t) m -> p t m" if g == LAST else "(t p) m -> p t m"
-            nc.sync.dma_start(margins[g][:], margin[g * R_PASS : (g + 1) * R_PASS, :].rearrange(order, t=PACK))
-
-        def load_w3(tag):
-            w3_raw = tenant([P, PASSES, PACK, N_OUT], F32, "w3_raw", tag)
-            for g in range(PASSES):
-                nc.sync.dma_start(
-                    w3_raw[:, g, :, :], w3[g * R_PASS : (g + 1) * R_PASS, :].rearrange("(p j) n -> p j n", j=PACK)
-                )
-            made["w3_raw"] = w3_raw
-
-        def load_last_weights(tag):
-            weights_last = tenant([P, PACK, S], F32, "weights_last", tag)
-            for q in range(QUADS):
-                nc.sync.dma_start(
-                    weights_last[QUAD * q : QUAD * (q + 1), :, :], wgs.rearrange("(u t) j -> u t j", t=PACK)
-                )
-            made["weights_last"] = weights_last
 
         def prepare_w1(g, bf_tag, codes_tag=None):
             width = w1_raw[g].shape[2]
@@ -192,7 +196,7 @@ def tile_list_phishing_verdict_slots_kernel(
             w3_bf = tenant([P, PASSES * N_OUT * PACK], BF16, "w3_bf", tag)
             for g in range(PASSES):
                 dst, rows = interleaved(
-                    w3_bf[:, g * N_OUT * PACK : (g + 1) * N_OUT * PACK], made["w3_raw"][:, g, :, :]
+                    w3_bf[:, g * N_OUT * PACK : (g + 1) * N_OUT * PACK], w3_raw[:, g, :, :]
                 )
                 nc.scalar.activation(dst, rows, ACT.Copy)
             made["w3_q"] = quantised("w3", w3_bf, PASSES * N_OUT)
@@ -213,77 +217,83 @@ def tile_list_phishing_verdict_slots_kernel(
                 words, scales = w2_w[g], w2_s[:, g * R_PASS : (g + 1) * R_PASS]
             return words[:, 2 * t * P : 2 * (t + 1) * P].bitcast(FP4X4), scales[:, t * P : (t + 1) * P]
 
-        def pieces(i):
-            return FIRST_PIECES if i == 0 else ((0, S),)
-
-        def fetch_target(i):
-            g, t = divmod(i, PACK)
-            if t == 0:
-                diffs[g] = ring.tile([P, PACK, M_OUT], F32, name="diffs", tag="diffs", bufs=2)
-            if g == LAST:
-                fetched[i] = diffs[g][:, t, :]
-            else:
-                fetched[i] = ring.tile([P, M_OUT], F32, name="diff_rows", tag="diff_rows", bufs=3)[:]
-            return fetched[i]
-
-        def signatures(i):
-            if i == 0:
-                sig = [tenant([P, count], F32, "sig", f"after_piece{first}")[:] for first, count in pieces(i)]
-            elif i in TIMING_TILES:
-                sig = [tenant([P, S], F32, "sig", f"after_scatter{i}")[:]]
-            else:
-                sig = [ring.tile([P, S], F32, name="sig", tag="sig", bufs=2)[:]]
+        def first_stage(i, first, count, damp):
             w1_codes, w1_scale = w1_operand(i)
             w2_codes, w2_scale = w2_operand(i)
-            for piece, (first, count) in enumerate(pieces(i)):
-                for c0 in range(first, first + count, HALF):
-                    n = min(count, HALF)
-                    h = c0 // HALF
-                    part = slice(c0 - h * HALF, c0 - h * HALF + n)
-                    b_ps = psum.tile([P, HALF], F32, name="b_ps", tag="b", bufs=3)
-                    nc.tensor.matmul_mx(
-                        out=b_ps[:, 0:n],
-                        lhsT=w2_codes,
-                        lhsT_scale=w2_scale,
-                        rhs=v_w[h][:, part].bitcast(FP8X4),
-                        rhs_scale=v_s[h][:, part],
-                        start=True,
-                        stop=True,
-                    )
-                    a_ps = psum.tile([P, HALF], F32, name="a_ps", tag="a", bufs=2)
-                    nc.tensor.matmul_mx(
-                        out=a_ps[:, 0:n],
-                        lhsT=w1_codes,
-                        lhsT_scale=w1_scale,
-                        rhs=v_w[h][:, part].bitcast(FP8X4),
-                        rhs_scale=v_s[h][:, part],
-                        start=True,
-                        stop=True,
-                    )
-                    if h == 0:
-                        square = ring.tile([P, HALF], F32, name="square", tag="square", bufs=2)[:]
-                    elif i == 0:
-                        square = tenant([P, HALF], F32, "square", "after_first_exps")[:]
-                    else:
-                        square = fetch_target(i - 1)
-                    damp = ring.tile([P, HALF], F32, name="damp", tag="damp", bufs=4)
-                    nc.scalar.activation(square[:, 0:n], b_ps[:, 0:n], ACT.Square)
-                    nc.scalar.activation(damp[:, 0:n], square[:, 0:n], ACT.Exp, scale=-1.0)
-                    nc.vector.tensor_tensor(
-                        sig[piece][:, c0 - first : c0 - first + n], a_ps[:, 0:n], damp[:, 0:n], ALU.mult
-                    )
-            return sig
+            h = first // HALF
+            part = slice(first - h * HALF, first - h * HALF + count)
+            b_ps = psum.tile([P, HALF], F32, name="b_ps", tag="b", bufs=3)
+            nc.tensor.matmul_mx(
+                out=b_ps[:, 0:count],
+                lhsT=w2_codes,
+                lhsT_scale=w2_scale,
+                rhs=v_w[h][:, part].bitcast(FP8X4),
+                rhs_scale=v_s[h][:, part],
+                start=True,
+                stop=True,
+            )
+            a_ps = psum.tile([P, HALF], F32, name="a_ps", tag="a", bufs=2)
+            nc.tensor.matmul_mx(
+                out=a_ps[:, 0:count],
+                lhsT=w1_codes,
+                lhsT_scale=w1_scale,
+                rhs=v_w[h][:, part].bitcast(FP8X4),
+                rhs_scale=v_s[h][:, part],
+                start=True,
+                stop=True,
+            )
+            square = ring.tile([P, HALF], F32, name="square", tag="square", bufs=2)
+            nc.scalar.activation(square[:, 0:count], b_ps[:, 0:count], ACT.Square)
+            nc.scalar.activation(damp[:, first : first + count], square[:, 0:count], ACT.Exp, scale=-1.0)
+            return a_ps[:, 0:count]
 
-        def scatter(i, sig):
-            g, t = divmod(i, PACK)
-            weight = made["weights_last"][:, t, :] if g == LAST else weights[:]
-            for piece, (first, count) in enumerate(pieces(i)):
+        def first_tile():
+            damp = tenant([P, S], F32, "damp", "damp_fetched0")
+            sums = [first_stage(0, first, count, damp) for first, count in FIRST_PIECES[:2]]
+            for (first, count), a_ps in zip(FIRST_PIECES[:2], sums):
+                sig = keep.tile([P, count], F32, name=f"sig_first{first}")
+                nc.vector.tensor_tensor(sig[:], a_ps, damp[:, first : first + count], ALU.mult)
                 nc.vector.tensor_tensor(
-                    pages[i % 2][:].indirect(entries(idx2, first, count)),
-                    sig[piece],
-                    weight[:, first : first + count],
+                    pages[0][:].indirect(entries(idx2, first, count)),
+                    sig[:],
+                    weights[:, first : first + count],
                     ALU.mult,
                 )
+            first, count = FIRST_PIECES[2]
+            a_ps = first_stage(0, first, count, damp)
+            prepare_w1(0, "first_rest")
+            plain = tenant([P, count], F32, "plain", "first_rest")
+            nc.vector.tensor_tensor(plain[:], a_ps, damp[:, first : first + count], ALU.mult)
+            sig = keep.tile([P, count], F32, name=f"sig_first{first}")
+            nc.vector.tensor_tensor(sig[:], plain[:], weights[:, first : first + count], ALU.mult)
+            nc.vector.tensor_copy(pages[0][:].indirect(entries(idx2, first, count)), sig[:])
+
+        def damp_and_fetched(i):
+            g, t = divmod(i - 1, PACK)
+            if t == 0:
+                diffs[g] = ring.tile([P, PACK * M_OUT], F32, name="diffs", tag="diffs", bufs=2)
+            if g == LAST:
+                fetched[i - 1] = diffs[g][:, t * M_OUT : (t + 1) * M_OUT]
+                return diffs[g][:, t * M_OUT : t * M_OUT + S]
+            return tenant([P, S], F32, "damp", f"damp_fetched{i % RING}")[:]
+
+        def signatures(i):
+            g, t = divmod(i, PACK)
+            damp = damp_and_fetched(i)
+            sums = [first_stage(i, c0, HALF, damp) for c0 in range(0, S, HALF)]
+            weight = weights_last[:, t, :] if g == LAST else weights[:]
+            weighted = tenant([P, S], F32, "weighted", "first_rest" if i == 1 else f"margin_ew{(i - 2) % RING}")
+            nc.gpsimd.tensor_tensor(weighted[:], damp, weight, ALU.mult)
+            sig = ring.tile([P, S], F32, name="sig", tag="sig", bufs=2)
+            for h, a_ps in enumerate(sums):
+                part = slice(h * HALF, (h + 1) * HALF)
+                nc.vector.tensor_tensor(sig[:, part], a_ps, weighted[:, part], ALU.mult)
+            if i >= 2 and i + 1 < TILES:
+                load_margin(i + 1)
+            return sig
+
+        def rows_of(diff):
+            return diff[:].rearrange("p (t m) -> p t m", t=PACK)
 
         out_ps = [psum.tile([P, M_OUT], F32, name=f"out_ps{n}") for n in range(N_OUT // P)]
 
@@ -304,62 +314,51 @@ def tile_list_phishing_verdict_slots_kernel(
 
         def fetch(i):
             g, t = divmod(i, PACK)
-            nc.vector.tensor_tensor(fetched[i], pages[i % 2][:].indirect(idx3[:]), margins[g][:, t, :], ALU.subtract)
+            if g != LAST:
+                fetched[i] = tenant([P, M_OUT], F32, "fetched", f"damp_fetched{(i + 1) % RING}")[:]
+            nc.vector.tensor_tensor(fetched[i], pages[i % 2][:].indirect(idx3[:]), margins[i][:], ALU.subtract)
             if g == LAST:
                 return
             for j in range(PACK):
-                nc.sync.dma_start(diffs[g][QUAD * t : QUAD * (t + 1), j, :], fetched[i][j:P:PACK, :])
+                nc.sync.dma_start(rows_of(diffs[g])[QUAD * t : QUAD * (t + 1), j, :], fetched[i][j:P:PACK, :])
             if t == PACK - 1:
                 made["z_bf"] = tenant([P, M_OUT * PACK], BF16, "z_bf", "z_bf")
-                nc.scalar.activation(*interleaved(made["z_bf"][:], diffs[g][:]), ACT.Relu)
+                nc.scalar.activation(*interleaved(made["z_bf"][:], rows_of(diffs[g])), ACT.Relu)
 
-        def close_pass(g, tag):
-            score(g, quantised(f"z{g}", made["z_bf"], M_OUT, tag), slice(0, M_OUT), False)
+        def close_pass(g):
+            score(g, quantised(f"z{g}", made["z_bf"], M_OUT), slice(0, M_OUT), False)
 
         def finish_last_pass():
             width = M_OUT // 2
             low, high = slice(0, width), slice(width, M_OUT)
             for cols in (low, high):
                 nc.vector.tensor_tensor(
-                    diffs[LAST][:, PACK - 1, cols],
+                    rows_of(diffs[LAST])[:, PACK - 1, cols],
                     pages[(TILES - 1) % 2][:].indirect(entries(idx3, cols.start, width)),
-                    margins[LAST][:, PACK - 1, cols],
+                    margins[TILES - 1][:, cols],
                     ALU.subtract,
                 )
             z_low = keep.tile([P, width * PACK], BF16, name="z_low", align_bytes=ALIGN)
             z_high = keep.tile([P, width * PACK], BF16, name="z_high", align_bytes=ALIGN)
-            nc.scalar.activation(*interleaved(z_low[:], diffs[LAST][:, :, low]), ACT.Relu)
-            nc.vector.tensor_scalar_max(*interleaved(z_high[:], diffs[LAST][:, :, high]), 0.0)
+            nc.scalar.activation(*interleaved(z_low[:], rows_of(diffs[LAST])[:, :, low]), ACT.Relu)
+            nc.vector.tensor_scalar_max(*interleaved(z_high[:], rows_of(diffs[LAST])[:, :, high]), 0.0)
             score(LAST, quantised("z_high", z_high, width), high, False)
             score(LAST, quantised("z_low", z_low, width), low, True)
 
-        piece_tags = [f"after_piece{first}" for first, count in FIRST_PIECES]
-        for i in range(TILES):
+        first_tile()
+        for i in range(1, TILES):
+            for g in CAST_W1_BEFORE:
+                if i == CAST_W1_BEFORE[g]:
+                    prepare_w1(g, f"w1_bf{g}")
+            if i == CAST_W3_BEFORE:
+                prepare_w3("w3_bf")
+            if i == REORDER_W2_BEFORE:
+                prepare_w2_last("w2_w_last", "w2_s_last")
+            if i in CLOSE_PASS_BEFORE:
+                close_pass(CLOSE_PASS_BEFORE.index(i))
             sig = signatures(i)
-            if i >= 1:
-                fetch(i - 1)
-            scatter(i, sig)
-            after_scatter = f"after_scatter{i}"
-            if i == 0:
-                load_margin(0, "table")
-                prepare_w1(0, "after_first_exps", piece_tags[1])
-                w1_raw[1] = load_w1(slice(R_PASS, 2 * R_PASS), piece_tags[0])
-                prepare_w1(1, piece_tags[2])
-                load_last_weights("w1_pass0")
-                load_scale_rows(w2_s_last_raw, w2_scales[0, :, LAST * R_PASS : H])
-            if i == LOAD_W3_AFTER:
-                load_margin(1, piece_tags[0])
-                load_w3(after_scatter)
-            if i == LOAD_W1_LAST_AFTER:
-                w1_raw[LAST] = load_w1(slice(LAST * R_PASS, H), after_scatter)
-            if i == CAST_W3_AFTER:
-                prepare_w3(after_scatter)
-                prepare_w2_last(piece_tags[1], f"after_scatter{LOAD_W3_AFTER}")
-            if i == CAST_W1_LAST_AFTER:
-                prepare_w1(LAST, after_scatter)
-                load_margin(LAST, "table")
-            if i in CLOSE_PASS_AFTER:
-                close_pass(CLOSE_PASS_AFTER.index(i), after_scatter)
+            fetch(i - 1)
+            nc.vector.tensor_copy(pages[i % 2][:].indirect(idx2[:]), sig[:])
         finish_last_pass()
 
         for n in range(N_OUT // P):

@@ -32,11 +32,12 @@ RUN = 4
 
 FIRST_PIECES = ((0, 256), (256, 256), (512, 512))
 
-CAST_W1_BEFORE = {1: 2, LAST: 6}
-CAST_W3_BEFORE = 4
-REORDER_W2_BEFORE = 7
-CLOSE_PASS_BEFORE = tuple(PACK * (g + 1) + 2 for g in range(LAST))
 RING = 3
+PAGES = 3
+
+SIDE_AFTER = {1: "w1_pass1", 2: "w2_words", 3: "w2_scales", 4: "w1_last", 6: "z0", 7: "w3_wide", 8: "w3_rest", 10: "z1"}
+LOAD_AFTER = {2: "table", 4: "late"}
+W3_WIDE = 1024
 
 
 def tile_list_phishing_verdict_slots_kernel(
@@ -103,41 +104,33 @@ def tile_list_phishing_verdict_slots_kernel(
         tab_w = tenant([P, T], I32, "tab_w", "table")
         nc.sync.dma_start(tab_w[:], tab_words[0].rearrange("p t i -> p (t i)").bitcast(I32))
         w2_w = {0: load_w2_words(0)}
-        w2_s = keep.tile([P, LAST * R_PASS], U8, name="w2_s", align_bytes=ALIGN)
-        load_scale_rows(w2_s, w2_scales[0, :, 0 : LAST * R_PASS])
+        w2_s = keep.tile([P, H], U8, name="w2_s", align_bytes=ALIGN)
+        nc.gpsimd.memset(w2_s[:].bitcast(I32), 0)
+        load_scale_rows(w2_s, w2_scales[0])
         weights = keep.tile([P, S], F32, name="weights")
         nc.sync.dma_start(weights[:], wgs)
         nc.sync.dma_start(idx2[:], offs2)
         nc.sync.dma_start(idx3[:], offs3)
-        w1_raw = {0: load_w1(slice(P, R_PASS), "w1_pass0")}
-        margins = {}
+        w1_raw = {0: load_w1(slice(P, R_PASS), "w3_wide")}
+        slots = keep.tile([P, (TILES + 2) * M_OUT], F32, name="slots")
+        margins = {i: slots[:, (i + 2) * M_OUT : (i + 3) * M_OUT] for i in range(TILES)}
 
-        def load_margin(i):
-            g, t = divmod(i, PACK)
-            margins[i] = tenant([P, M_OUT], F32, "margin", f"margin_ew{i % RING}")
-            if g == LAST:
-                rows = margin[g * R_PASS : (g + 1) * R_PASS, :].rearrange("(p t) m -> p t m", t=PACK)[:, t, :]
-            else:
-                rows = margin[i * P : (i + 1) * P, :]
-            nc.sync.dma_start(margins[i][:], rows)
+        def load_margins(first, count):
+            g = first // PACK
+            order = "(p t) m -> p t m" if g == LAST else "(t p) m -> p t m"
+            rows = margin[g * R_PASS : (g + 1) * R_PASS, :].rearrange(order, t=PACK)
+            nc.sync.dma_start(
+                slots[:, (first + 2) * M_OUT : (first + 2 + count) * M_OUT].rearrange("p (t m) -> p t m", t=count),
+                rows[:, first - g * PACK : first - g * PACK + count, :],
+            )
 
-        load_margin(0)
-        w1_raw[1] = load_w1(slice(R_PASS, 2 * R_PASS), "w1_pass1")
+        load_margins(0, 1)
+        w1_raw[1] = load_w1(slice(R_PASS, 2 * R_PASS), "z0")
         w2_w[1] = load_w2_words(1)
-        for i in range(1, RING):
-            load_margin(i)
-        w3_raw = keep.tile([P, PASSES, PACK, N_OUT], F32, name="w3_raw")
-        for g in range(PASSES):
-            nc.sync.dma_start(
-                w3_raw[:, g, :, :], w3[g * R_PASS : (g + 1) * R_PASS, :].rearrange("(p j) n -> p j n", j=PACK)
-            )
-        w1_raw[LAST] = load_w1(slice(LAST * R_PASS, H), "w1_last")
+        load_margins(1, PACK - 1)
         w2_w[LAST] = load_w2_words(LAST)
-        weights_last = keep.tile([P, PACK, S], F32, name="weights_last")
-        for q in range(QUADS):
-            nc.sync.dma_start(
-                weights_last[QUAD * q : QUAD * (q + 1), :, :], wgs.rearrange("(u t) j -> u t j", t=PACK)
-            )
+        w1_raw[LAST] = load_w1(slice(LAST * R_PASS, H), SIDE_AFTER[8])
+        load_margins(PACK, PACK)
 
         tab_s = keep.tile([P, T], U8, name="tab_s", align_bytes=ALIGN)
         nc.vector.memset(tab_s[:].bitcast(I32), 0)
@@ -146,16 +139,15 @@ def tile_list_phishing_verdict_slots_kernel(
         for q in range(QUADS):
             live = slice(QUAD * q, QUAD * q + PACK)
             nc.vector.tensor_copy(tab_s[live, :].bitcast(I32), tab_scale_rows[live, :].bitcast(I32))
-        w2_s_last_raw = tenant([P, R_PASS], U8, "w2_s_last_raw", "scale_rows")
-        nc.gpsimd.memset(w2_s_last_raw[:].bitcast(I32), 0)
-        load_scale_rows(w2_s_last_raw, w2_scales[0, :, LAST * R_PASS : H])
 
         first_bf = tenant([P, P * PACK], BF16, "first_bf", "page_odd")
         nc.scalar.activation(*interleaved(first_bf[:], w1_first[:]), ACT.Copy)
         w1_q_first = quantised("w1_tile0", first_bf, P)
         page_odd = tenant([P, T2], F32, "page_odd", "page_odd")
         nc.gpsimd.memset(page_odd[:], 0.0)
-        pages = [page_even, page_odd]
+        page_third = keep.tile([P, T2], F32, name="page_third")
+        nc.gpsimd.memset(page_third[:], 0.0)
+        pages = [page_even, page_odd, page_third]
 
         v_s = [keep.tile([P, HALF], U8, name=f"v_s{h}", align_bytes=ALIGN) for h in range(S // HALF)]
         v_w = [keep.tile([P, HALF], U32, name=f"v_w{h}", align_bytes=ALIGN) for h in range(S // HALF)]
@@ -168,6 +160,24 @@ def tile_list_phishing_verdict_slots_kernel(
         fetched = {}
         made = {}
 
+        def load_w3(tag):
+            w3_raw = tenant([P, PASSES, PACK, N_OUT], F32, "w3_raw", tag)
+            for g in range(PASSES):
+                nc.sync.dma_start(
+                    w3_raw[:, g, :, :], w3[g * R_PASS : (g + 1) * R_PASS, :].rearrange("(p j) n -> p j n", j=PACK)
+                )
+            made["w3_raw"] = w3_raw
+
+        def load_last_weights(tag):
+            weights_last = tenant([P, PACK, S], F32, "weights_last", tag)
+            for q in range(QUADS):
+                nc.sync.dma_start(
+                    weights_last[QUAD * q : QUAD * (q + 1), :, :], wgs.rearrange("(u t) j -> u t j", t=PACK)
+                )
+            made["weights_last"] = weights_last
+
+        late_loads = {"table": load_w3, "late": load_last_weights}
+
         def prepare_w1(g, bf_tag, codes_tag=None):
             width = w1_raw[g].shape[2]
             bf = tenant([P, width * PACK], BF16, "w1_bf", bf_tag)
@@ -179,27 +189,56 @@ def tile_list_phishing_verdict_slots_kernel(
             nc.scalar.activation(dst, rows, ACT.Copy)
             w1_q[g] = quantised(f"w1_q{g}", bf, width, codes_tag)
 
-        def prepare_w2_last(words_tag, scales_tag):
-            words = tenant([P, 2 * R_PASS], U8, "w2_w_last", words_tag)
+        def reorder_w2_words(tag):
+            words = tenant([P, 2 * R_PASS], U8, "w2_w_last", tag)
             nc.vector.tensor_copy(
                 words[:].bitcast(U16).rearrange("p (t u) -> p t u", t=PACK),
                 w2_w[LAST][:].bitcast(U16).rearrange("p (u t) -> p t u", t=PACK),
             )
-            scales = tenant([P, R_PASS], U8, "w2_s_last", scales_tag)
+            made["w2_words"] = words
+
+        def reorder_w2_scales(tag):
+            scales = tenant([P, R_PASS], U8, "w2_s_last", tag)
             nc.vector.tensor_copy(
                 scales[:].rearrange("p (t u) -> p t u", t=PACK),
-                w2_s_last_raw[:].rearrange("p (u t) -> p t u", t=PACK),
+                w2_s[:, LAST * R_PASS : H].rearrange("p (u t) -> p t u", t=PACK),
             )
-            made["w2_last"] = (words, scales)
+            made["w2_scales"] = scales
 
-        def prepare_w3(tag):
-            w3_bf = tenant([P, PASSES * N_OUT * PACK], BF16, "w3_bf", tag)
+        w3_q = {}
+        z_q = {}
+
+        def prepare_w3(words, tag):
+            w3_bf = tenant([P, (words.stop - words.start) * PACK], BF16, "w3_bf", "cast_" + tag)
             for g in range(PASSES):
-                dst, rows = interleaved(
-                    w3_bf[:, g * N_OUT * PACK : (g + 1) * N_OUT * PACK], w3_raw[:, g, :, :]
-                )
-                nc.scalar.activation(dst, rows, ACT.Copy)
-            made["w3_q"] = quantised("w3", w3_bf, PASSES * N_OUT)
+                lo, hi = max(words.start, g * N_OUT), min(words.stop, (g + 1) * N_OUT)
+                if lo < hi:
+                    dst, rows = interleaved(
+                        w3_bf[:, (lo - words.start) * PACK : (hi - words.start) * PACK],
+                        made["w3_raw"][:, g, :, lo - g * N_OUT : hi - g * N_OUT],
+                    )
+                    nc.scalar.activation(dst, rows, ACT.Copy)
+            w3_q[words.start] = quantised(tag, w3_bf, words.stop - words.start, tag)
+
+        def w3_operand(word):
+            first = W3_WIDE if word >= W3_WIDE else 0
+            codes, scales = w3_q[first]
+            cols = slice(word - first, word - first + P)
+            return codes[:, cols].bitcast(FP8X4), scales[:, cols]
+
+        def quantise_z(g, tag):
+            z_q[g] = quantised(tag, made["z_bf"], M_OUT, tag)
+
+        side_work = {
+            "w1_pass1": lambda tag: prepare_w1(1, "cast_" + tag, tag),
+            "w1_last": lambda tag: prepare_w1(LAST, "cast_" + tag, tag),
+            "w2_words": reorder_w2_words,
+            "w2_scales": reorder_w2_scales,
+            "w3_wide": lambda tag: prepare_w3(slice(0, W3_WIDE), tag),
+            "w3_rest": lambda tag: prepare_w3(slice(W3_WIDE, PASSES * N_OUT), tag),
+            "z0": lambda tag: quantise_z(0, tag),
+            "z1": lambda tag: quantise_z(1, tag),
+        }
 
         def w1_operand(i):
             g, t = divmod(i, PACK)
@@ -212,7 +251,7 @@ def tile_list_phishing_verdict_slots_kernel(
         def w2_operand(i):
             g, t = divmod(i, PACK)
             if g == LAST:
-                words, scales = made["w2_last"]
+                words, scales = made["w2_words"], made["w2_scales"]
             else:
                 words, scales = w2_w[g], w2_s[:, g * R_PASS : (g + 1) * R_PASS]
             return words[:, 2 * t * P : 2 * (t + 1) * P].bitcast(FP4X4), scales[:, t * P : (t + 1) * P]
@@ -222,7 +261,7 @@ def tile_list_phishing_verdict_slots_kernel(
             w2_codes, w2_scale = w2_operand(i)
             h = first // HALF
             part = slice(first - h * HALF, first - h * HALF + count)
-            b_ps = psum.tile([P, HALF], F32, name="b_ps", tag="b", bufs=3)
+            b_ps = psum.tile([P, HALF], F32, name="b_ps", tag="b", bufs=4)
             nc.tensor.matmul_mx(
                 out=b_ps[:, 0:count],
                 lhsT=w2_codes,
@@ -232,7 +271,7 @@ def tile_list_phishing_verdict_slots_kernel(
                 start=True,
                 stop=True,
             )
-            a_ps = psum.tile([P, HALF], F32, name="a_ps", tag="a", bufs=2)
+            a_ps = psum.tile([P, HALF], F32, name="a_ps", tag="a", bufs=4)
             nc.tensor.matmul_mx(
                 out=a_ps[:, 0:count],
                 lhsT=w1_codes,
@@ -248,10 +287,10 @@ def tile_list_phishing_verdict_slots_kernel(
             return a_ps[:, 0:count]
 
         def first_tile():
-            damp = tenant([P, S], F32, "damp", "damp_fetched0")
+            damp = ring.tile([P, S], F32, name="damp", tag="damp", bufs=2)
             sums = [first_stage(0, first, count, damp) for first, count in FIRST_PIECES[:2]]
             for (first, count), a_ps in zip(FIRST_PIECES[:2], sums):
-                sig = keep.tile([P, count], F32, name=f"sig_first{first}")
+                sig = tenant([P, count], F32, "sig_first", f"sig{first // count}")
                 nc.vector.tensor_tensor(sig[:], a_ps, damp[:, first : first + count], ALU.mult)
                 nc.vector.tensor_tensor(
                     pages[0][:].indirect(entries(idx2, first, count)),
@@ -264,48 +303,56 @@ def tile_list_phishing_verdict_slots_kernel(
             prepare_w1(0, "first_rest")
             plain = tenant([P, count], F32, "plain", "first_rest")
             nc.vector.tensor_tensor(plain[:], a_ps, damp[:, first : first + count], ALU.mult)
-            sig = keep.tile([P, count], F32, name=f"sig_first{first}")
+            sig = tenant([P, count], F32, "sig_first", "z1")
             nc.vector.tensor_tensor(sig[:], plain[:], weights[:, first : first + count], ALU.mult)
             nc.vector.tensor_copy(pages[0][:].indirect(entries(idx2, first, count)), sig[:])
 
-        def damp_and_fetched(i):
-            g, t = divmod(i - 1, PACK)
-            if t == 0:
-                diffs[g] = ring.tile([P, PACK * M_OUT], F32, name="diffs", tag="diffs", bufs=2)
-            if g == LAST:
-                fetched[i - 1] = diffs[g][:, t * M_OUT : (t + 1) * M_OUT]
-                return diffs[g][:, t * M_OUT : t * M_OUT + S]
-            return tenant([P, S], F32, "damp", f"damp_fetched{i % RING}")[:]
-
         def signatures(i):
             g, t = divmod(i, PACK)
-            damp = damp_and_fetched(i)
-            sums = [first_stage(i, c0, HALF, damp) for c0 in range(0, S, HALF)]
-            weight = weights_last[:, t, :] if g == LAST else weights[:]
-            weighted = tenant([P, S], F32, "weighted", "first_rest" if i == 1 else f"margin_ew{(i - 2) % RING}")
-            nc.gpsimd.tensor_tensor(weighted[:], damp, weight, ALU.mult)
-            sig = ring.tile([P, S], F32, name="sig", tag="sig", bufs=2)
-            for h, a_ps in enumerate(sums):
-                part = slice(h * HALF, (h + 1) * HALF)
-                nc.vector.tensor_tensor(sig[:, part], a_ps, weighted[:, part], ALU.mult)
-            if i >= 2 and i + 1 < TILES:
-                load_margin(i + 1)
+            if i in LOAD_AFTER:
+                damp = tenant([P, S], F32, "damp", LOAD_AFTER[i])
+            elif i > PACK and t == PACK - 1:
+                damp = tenant([P, S], F32, "damp", f"diffs{g - 1}")
+            else:
+                damp = ring.tile([P, S], F32, name="damp", tag="damp", bufs=2)
+            if i > 1:
+                amplitude = ring.tile([P, S], F32, name="amplitude", tag="amplitude", bufs=3)
+            sums = []
+            for c0 in range(0, S, HALF):
+                a_ps = first_stage(i, c0, HALF, damp)
+                if i > 1:
+                    nc.scalar.copy(amplitude[:, c0 : c0 + HALF], a_ps)
+                sums.append(a_ps)
+            weight = made["weights_last"][:, t, :] if g == LAST else weights[:]
+            if i == 1:
+                weighted = tenant([P, S], F32, "weighted", "first_rest")[:]
+            else:
+                weighted = slots[:, (i - 2) * M_OUT : i * M_OUT]
+            nc.gpsimd.tensor_tensor(weighted, damp[:], weight, ALU.mult)
+            if i in LOAD_AFTER:
+                late_loads[LOAD_AFTER[i]](LOAD_AFTER[i])
+            sig = tenant([P, S], F32, "sig", SIDE_AFTER.get(i, f"sig{i % 2}"))
+            if i == 1:
+                for h, a_ps in enumerate(sums):
+                    part = slice(h * HALF, (h + 1) * HALF)
+                    nc.vector.tensor_tensor(sig[:, part], a_ps, weighted[:, part], ALU.mult)
+            else:
+                nc.gpsimd.tensor_tensor(sig[:], amplitude[:], weighted, ALU.mult)
             return sig
 
         def rows_of(diff):
-            return diff[:].rearrange("p (t m) -> p t m", t=PACK)
+            return diff.rearrange("p (t m) -> p t m", t=PACK)
 
-        out_ps = [psum.tile([P, M_OUT], F32, name=f"out_ps{n}") for n in range(N_OUT // P)]
+        out_ps = []
 
-        def score(g, z_q, cols, stop):
-            w3_codes, w3_scale = made["w3_q"]
-            z_codes, z_scale = z_q
+        def score(g, z_part, cols, stop):
+            z_codes, z_scale = z_part
             for n in range(N_OUT // P):
-                w3_cols = slice(g * N_OUT + n * P, g * N_OUT + (n + 1) * P)
+                w3_codes, w3_scale = w3_operand(g * N_OUT + n * P)
                 nc.tensor.matmul_mx(
                     out=out_ps[n][:, cols],
-                    lhsT=w3_codes[:, w3_cols].bitcast(FP8X4),
-                    lhsT_scale=w3_scale[:, w3_cols],
+                    lhsT=w3_codes,
+                    lhsT_scale=w3_scale,
                     rhs=z_codes[:].bitcast(FP8X4),
                     rhs_scale=z_scale[:],
                     start=(g == 0),
@@ -314,32 +361,34 @@ def tile_list_phishing_verdict_slots_kernel(
 
         def fetch(i):
             g, t = divmod(i, PACK)
-            if g != LAST:
-                fetched[i] = tenant([P, M_OUT], F32, "fetched", f"damp_fetched{(i + 1) % RING}")[:]
-            nc.vector.tensor_tensor(fetched[i], pages[i % 2][:].indirect(idx3[:]), margins[i][:], ALU.subtract)
+            if i == 0:
+                fetched[i] = tenant([P, M_OUT], F32, "fetched", "first_rest")[:]
+            else:
+                fetched[i] = slots[:, (i - 1) * M_OUT : i * M_OUT]
+            nc.vector.tensor_tensor(fetched[i], pages[i % PAGES][:].indirect(idx3[:]), margins[i], ALU.subtract)
             if g == LAST:
                 return
+            if t == 0:
+                diffs[g] = tenant([P, PACK * M_OUT], F32, "diffs", f"diffs{g}")[:]
             for j in range(PACK):
                 nc.sync.dma_start(rows_of(diffs[g])[QUAD * t : QUAD * (t + 1), j, :], fetched[i][j:P:PACK, :])
             if t == PACK - 1:
                 made["z_bf"] = tenant([P, M_OUT * PACK], BF16, "z_bf", "z_bf")
                 nc.scalar.activation(*interleaved(made["z_bf"][:], rows_of(diffs[g])), ACT.Relu)
 
-        def close_pass(g):
-            score(g, quantised(f"z{g}", made["z_bf"], M_OUT), slice(0, M_OUT), False)
-
         def finish_last_pass():
+            diffs[LAST] = slots[:, (LAST * PACK - 1) * M_OUT : (TILES - 1) * M_OUT]
             width = M_OUT // 2
             low, high = slice(0, width), slice(width, M_OUT)
             for cols in (low, high):
                 nc.vector.tensor_tensor(
                     rows_of(diffs[LAST])[:, PACK - 1, cols],
-                    pages[(TILES - 1) % 2][:].indirect(entries(idx3, cols.start, width)),
+                    pages[(TILES - 1) % PAGES][:].indirect(entries(idx3, cols.start, width)),
                     margins[TILES - 1][:, cols],
                     ALU.subtract,
                 )
-            z_low = keep.tile([P, width * PACK], BF16, name="z_low", align_bytes=ALIGN)
-            z_high = keep.tile([P, width * PACK], BF16, name="z_high", align_bytes=ALIGN)
+            z_low = tenant([P, width * PACK], BF16, "z_low", "cast_w1_last")
+            z_high = tenant([P, width * PACK], BF16, "z_high", "z_bf")
             nc.scalar.activation(*interleaved(z_low[:], rows_of(diffs[LAST])[:, :, low]), ACT.Relu)
             nc.vector.tensor_scalar_max(*interleaved(z_high[:], rows_of(diffs[LAST])[:, :, high]), 0.0)
             score(LAST, quantised("z_high", z_high, width), high, False)
@@ -347,22 +396,20 @@ def tile_list_phishing_verdict_slots_kernel(
 
         first_tile()
         for i in range(1, TILES):
-            for g in CAST_W1_BEFORE:
-                if i == CAST_W1_BEFORE[g]:
-                    prepare_w1(g, f"w1_bf{g}")
-            if i == CAST_W3_BEFORE:
-                prepare_w3("w3_bf")
-            if i == REORDER_W2_BEFORE:
-                prepare_w2_last("w2_w_last", "w2_s_last")
-            if i in CLOSE_PASS_BEFORE:
-                close_pass(CLOSE_PASS_BEFORE.index(i))
             sig = signatures(i)
+            nc.vector.tensor_copy(pages[i % PAGES][:].indirect(idx2[:]), sig[:])
             fetch(i - 1)
-            nc.vector.tensor_copy(pages[i % 2][:].indirect(idx2[:]), sig[:])
+            if i in SIDE_AFTER:
+                side_work[SIDE_AFTER[i]](SIDE_AFTER[i])
+            if i == PACK:
+                load_margins(LAST * PACK, PACK)
+        out_ps.extend(psum.tile([P, M_OUT], F32, name="out_ps", tag="a", bufs=4) for n in range(N_OUT // P))
+        for g in range(LAST):
+            score(g, z_q[g], slice(0, M_OUT), False)
         finish_last_pass()
 
         for n in range(N_OUT // P):
-            result = keep.tile([P, M_OUT], F32, name=f"result{n}")
+            result = tenant([P, M_OUT], F32, "result", ("sig0", "sig1", "w2_words")[n])
             if n % 2 == 1:
                 nc.scalar.copy(result[:], out_ps[n][:])
             else:

@@ -32,12 +32,14 @@ RUN = 4
 
 FIRST_PIECES = ((0, 256), (256, 256), (512, 512))
 
-RING = 3
-PAGES = 3
+SHARE = 256
+OWN = S - SHARE
 
-SIDE_AFTER = {1: "w1_pass1", 2: "w2_words", 3: "w2_scales", 4: "w1_last", 6: "z0", 7: "w3_wide", 8: "w3_rest", 10: "z1"}
+SIDE_WITH = {1: "w1_pass0", 2: "w1_pass1", 3: "w2_words", 4: "w2_scales", 5: "w1_last", 6: "z0", 7: "w3_wide", 8: "w3_rest", 10: "z1"}
 LOAD_AFTER = {2: "table", 4: "late"}
 W3_WIDE = 1024
+W3_PARTS = (slice(0, W3_WIDE), slice(W3_WIDE, PASSES * N_OUT))
+LAST_PIECES = (slice(0, 128), slice(128, 256), slice(256, 512))
 
 
 def tile_list_phishing_verdict_slots_kernel(
@@ -108,28 +110,33 @@ def tile_list_phishing_verdict_slots_kernel(
         nc.gpsimd.memset(w2_s[:].bitcast(I32), 0)
         load_scale_rows(w2_s, w2_scales[0])
         weights = keep.tile([P, S], F32, name="weights")
-        nc.sync.dma_start(weights[:], wgs)
+        first_count = FIRST_PIECES[0][1]
         nc.sync.dma_start(idx2[:], offs2)
+        nc.sync.dma_start(weights[:, 0:first_count], wgs[:, 0:first_count])
+        w1_second = load_w1(slice(P, 2 * P), "w1_second")
+        nc.sync.dma_start(weights[:, first_count:S], wgs[:, first_count:S])
+        w1_raw = {0: load_w1(slice(2 * P, R_PASS), "w1_pass0_raw")}
         nc.sync.dma_start(idx3[:], offs3)
-        w1_raw = {0: load_w1(slice(P, R_PASS), "w3_wide")}
-        slots = keep.tile([P, (TILES + 2) * M_OUT], F32, name="slots")
-        margins = {i: slots[:, (i + 2) * M_OUT : (i + 3) * M_OUT] for i in range(TILES)}
+        slots = keep.tile([P, (TILES + 1) * M_OUT], F32, name="slots")
+
+        def slot(k, count=1):
+            return slots[:, k * M_OUT : (k + count) * M_OUT]
 
         def load_margins(first, count):
             g = first // PACK
             order = "(p t) m -> p t m" if g == LAST else "(t p) m -> p t m"
             rows = margin[g * R_PASS : (g + 1) * R_PASS, :].rearrange(order, t=PACK)
             nc.sync.dma_start(
-                slots[:, (first + 2) * M_OUT : (first + 2 + count) * M_OUT].rearrange("p (t m) -> p t m", t=count),
+                slot(first + 1, count).rearrange("p (t m) -> p t m", t=count),
                 rows[:, first - g * PACK : first - g * PACK + count, :],
             )
 
         load_margins(0, 1)
-        w1_raw[1] = load_w1(slice(R_PASS, 2 * R_PASS), "z0")
+        w1_raw[1] = load_w1(slice(R_PASS, 2 * R_PASS), "w1_pass1_raw")
         w2_w[1] = load_w2_words(1)
         load_margins(1, PACK - 1)
         w2_w[LAST] = load_w2_words(LAST)
-        w1_raw[LAST] = load_w1(slice(LAST * R_PASS, H), SIDE_AFTER[8])
+        w1_raw[LAST] = load_w1(slice(LAST * R_PASS, H), "w1_last_raw")
         load_margins(PACK, PACK)
 
         tab_s = keep.tile([P, T], U8, name="tab_s", align_bytes=ALIGN)
@@ -145,9 +152,7 @@ def tile_list_phishing_verdict_slots_kernel(
         w1_q_first = quantised("w1_tile0", first_bf, P)
         page_odd = tenant([P, T2], F32, "page_odd", "page_odd")
         nc.gpsimd.memset(page_odd[:], 0.0)
-        page_third = keep.tile([P, T2], F32, name="page_third")
-        nc.gpsimd.memset(page_third[:], 0.0)
-        pages = [page_even, page_odd, page_third]
+        pages = [page_even, page_odd]
 
         v_s = [keep.tile([P, HALF], U8, name=f"v_s{h}", align_bytes=ALIGN) for h in range(S // HALF)]
         v_w = [keep.tile([P, HALF], U32, name=f"v_w{h}", align_bytes=ALIGN) for h in range(S // HALF)]
@@ -157,7 +162,6 @@ def tile_list_phishing_verdict_slots_kernel(
 
         w1_q = {}
         diffs = {}
-        fetched = {}
         made = {}
 
         def load_w3(tag):
@@ -178,7 +182,9 @@ def tile_list_phishing_verdict_slots_kernel(
 
         late_loads = {"table": load_w3, "late": load_last_weights}
 
-        def prepare_w1(g, bf_tag, codes_tag=None):
+        casts = {}
+
+        def cast_w1(g, bf_tag):
             width = w1_raw[g].shape[2]
             bf = tenant([P, width * PACK], BF16, "w1_bf", bf_tag)
             if g == LAST:
@@ -187,7 +193,10 @@ def tile_list_phishing_verdict_slots_kernel(
             else:
                 dst, rows = interleaved(bf[:], w1_raw[g][:])
             nc.scalar.activation(dst, rows, ACT.Copy)
-            w1_q[g] = quantised(f"w1_q{g}", bf, width, codes_tag)
+            casts[f"w1_q{g}"] = bf
+
+        def quantise_w1(g, tag):
+            w1_q[g] = quantised(f"w1_q{g}", casts[f"w1_q{g}"], w1_raw[g].shape[2], tag)
 
         def reorder_w2_words(tag):
             words = tenant([P, 2 * R_PASS], U8, "w2_w_last", tag)
@@ -208,8 +217,8 @@ def tile_list_phishing_verdict_slots_kernel(
         w3_q = {}
         z_q = {}
 
-        def prepare_w3(words, tag):
-            w3_bf = tenant([P, (words.stop - words.start) * PACK], BF16, "w3_bf", "cast_" + tag)
+        def cast_w3(words):
+            w3_bf = keep.tile([P, (words.stop - words.start) * PACK], BF16, name=f"w3_bf{words.start}", align_bytes=ALIGN)
             for g in range(PASSES):
                 lo, hi = max(words.start, g * N_OUT), min(words.stop, (g + 1) * N_OUT)
                 if lo < hi:
@@ -218,7 +227,10 @@ def tile_list_phishing_verdict_slots_kernel(
                         made["w3_raw"][:, g, :, lo - g * N_OUT : hi - g * N_OUT],
                     )
                     nc.scalar.activation(dst, rows, ACT.Copy)
-            w3_q[words.start] = quantised(tag, w3_bf, words.stop - words.start, tag)
+            casts[words.start] = w3_bf
+
+        def quantise_w3(words, tag):
+            w3_q[words.start] = quantised(tag, casts[words.start], words.stop - words.start, tag)
 
         def w3_operand(word):
             first = W3_WIDE if word >= W3_WIDE else 0
@@ -230,12 +242,13 @@ def tile_list_phishing_verdict_slots_kernel(
             z_q[g] = quantised(tag, made["z_bf"], M_OUT, tag)
 
         side_work = {
-            "w1_pass1": lambda tag: prepare_w1(1, "cast_" + tag, tag),
-            "w1_last": lambda tag: prepare_w1(LAST, "cast_" + tag, tag),
+            "w1_pass0": lambda tag: quantise_w1(0, tag),
+            "w1_pass1": lambda tag: quantise_w1(1, tag),
+            "w1_last": lambda tag: quantise_w1(LAST, tag),
             "w2_words": reorder_w2_words,
             "w2_scales": reorder_w2_scales,
-            "w3_wide": lambda tag: prepare_w3(slice(0, W3_WIDE), tag),
-            "w3_rest": lambda tag: prepare_w3(slice(W3_WIDE, PASSES * N_OUT), tag),
+            "w3_wide": lambda tag: quantise_w3(W3_PARTS[0], tag),
+            "w3_rest": lambda tag: quantise_w3(W3_PARTS[1], tag),
             "z0": lambda tag: quantise_z(0, tag),
             "z1": lambda tag: quantise_z(1, tag),
         }
@@ -244,8 +257,10 @@ def tile_list_phishing_verdict_slots_kernel(
             g, t = divmod(i, PACK)
             if i == 0:
                 (codes, scales), col = w1_q_first, 0
+            elif i == 1:
+                (codes, scales), col = made["w1_second"], 0
             else:
-                (codes, scales), col = w1_q[g], (t - 1 if g == 0 else t) * P
+                (codes, scales), col = w1_q[g], (t - 2 if g == 0 else t) * P
             return codes[:, col : col + P].bitcast(FP8X4), scales[:, col : col + P]
 
         def w2_operand(i):
@@ -256,7 +271,7 @@ def tile_list_phishing_verdict_slots_kernel(
                 words, scales = w2_w[g], w2_s[:, g * R_PASS : (g + 1) * R_PASS]
             return words[:, 2 * t * P : 2 * (t + 1) * P].bitcast(FP4X4), scales[:, t * P : (t + 1) * P]
 
-        def first_stage(i, first, count, damp):
+        def first_stage(i, first, count):
             w1_codes, w1_scale = w1_operand(i)
             w2_codes, w2_scale = w2_operand(i)
             h = first // HALF
@@ -281,137 +296,172 @@ def tile_list_phishing_verdict_slots_kernel(
                 start=True,
                 stop=True,
             )
-            square = ring.tile([P, HALF], F32, name="square", tag="square", bufs=2)
+            if (i, first) == (1, 0):
+                square = tenant([P, HALF], F32, "square", "w1_second")
+            else:
+                square = ring.tile([P, HALF], F32, name="square", tag="square", bufs=2)
             nc.scalar.activation(square[:, 0:count], b_ps[:, 0:count], ACT.Square)
-            nc.scalar.activation(damp[:, first : first + count], square[:, 0:count], ACT.Exp, scale=-1.0)
-            return a_ps[:, 0:count]
+            return a_ps[:, 0:count], square[:, 0:count]
+
+        def damping(dst, square):
+            nc.scalar.activation(dst, square, ACT.Exp, scale=-1.0)
+
+        def scatter(i, first, count, sig):
+            g, t = divmod(i, PACK)
+            weight = made["weights_last"][:, t, :] if g == LAST else weights[:]
+            nc.vector.tensor_tensor(
+                pages[i % 2][:].indirect(entries(idx2, first, count)), sig, weight[:, first : first + count], ALU.mult
+            )
 
         def first_tile():
-            damp = ring.tile([P, S], F32, name="damp", tag="damp", bufs=2)
-            sums = [first_stage(0, first, count, damp) for first, count in FIRST_PIECES[:2]]
-            for (first, count), a_ps in zip(FIRST_PIECES[:2], sums):
-                sig = tenant([P, count], F32, "sig_first", f"sig{first // count}")
-                nc.vector.tensor_tensor(sig[:], a_ps, damp[:, first : first + count], ALU.mult)
-                nc.vector.tensor_tensor(
-                    pages[0][:].indirect(entries(idx2, first, count)),
-                    sig[:],
-                    weights[:, first : first + count],
-                    ALU.mult,
-                )
-            first, count = FIRST_PIECES[2]
-            a_ps = first_stage(0, first, count, damp)
-            prepare_w1(0, "first_rest")
-            plain = tenant([P, count], F32, "plain", "first_rest")
-            nc.vector.tensor_tensor(plain[:], a_ps, damp[:, first : first + count], ALU.mult)
-            sig = tenant([P, count], F32, "sig_first", "z1")
-            nc.vector.tensor_tensor(sig[:], plain[:], weights[:, first : first + count], ALU.mult)
-            nc.vector.tensor_copy(pages[0][:].indirect(entries(idx2, first, count)), sig[:])
+            low = ring.tile([P, OWN], F32, name="damp", tag="damp", bufs=2)
+            for first, count in FIRST_PIECES:
+                a_ps, square = first_stage(0, first, count)
+                if first < HALF:
+                    damp = low[:, first : first + count]
+                    damping(damp, square)
+                    sig = keep.tile([P, count], F32, name=f"sig_first{first}")
+                else:
+                    damp = slot(0)
+                    damping(damp, square)
+                    second_bf = tenant([P, P * PACK], BF16, "second_bf", "first_rest")
+                    nc.scalar.activation(*interleaved(second_bf[:], w1_second[:]), ACT.Copy)
+                    made["w1_second"] = quantised("w1_tile1", second_bf, P)
+                    sig = tenant([P, count], F32, "sig_first", "first_rest")
+                nc.vector.tensor_tensor(sig[:], a_ps, damp, ALU.mult)
+                scatter(0, first, count, sig[:])
 
         def signatures(i):
-            g, t = divmod(i, PACK)
-            if i in LOAD_AFTER:
-                damp = tenant([P, S], F32, "damp", LOAD_AFTER[i])
-            elif i > PACK and t == PACK - 1:
-                damp = tenant([P, S], F32, "damp", f"diffs{g - 1}")
+            if SIDE_WITH.get(i) in ("z0", "z1"):
+                damp = tenant([P, S], F32, "damp", SIDE_WITH[i])
+                damp_share = damp[:, OWN:S]
             else:
-                damp = ring.tile([P, S], F32, name="damp", tag="damp", bufs=2)
-            if i > 1:
-                amplitude = ring.tile([P, S], F32, name="amplitude", tag="amplitude", bufs=3)
-            sums = []
-            for c0 in range(0, S, HALF):
-                a_ps = first_stage(i, c0, HALF, damp)
-                if i > 1:
-                    nc.scalar.copy(amplitude[:, c0 : c0 + HALF], a_ps)
-                sums.append(a_ps)
-            weight = made["weights_last"][:, t, :] if g == LAST else weights[:]
-            if i == 1:
-                weighted = tenant([P, S], F32, "weighted", "first_rest")[:]
-            else:
-                weighted = slots[:, (i - 2) * M_OUT : i * M_OUT]
-            nc.gpsimd.tensor_tensor(weighted, damp[:], weight, ALU.mult)
+                if i in LOAD_AFTER:
+                    damp = tenant([P, OWN], F32, "damp", LOAD_AFTER[i])
+                else:
+                    damp = ring.tile([P, OWN], F32, name="damp", tag="damp", bufs=2)
+                damp_share = tenant([P, SHARE], F32, "damp_share", SIDE_WITH.get(i, f"damp_share{i % 2}"))[:]
+            a_share = slot(i - 1)[:, 0:SHARE]
+            sig = ring.tile([P, S], F32, name="sig", tag="sig", bufs=2)
+            a_low, square_low = first_stage(i, 0, HALF)
+            damping(damp[:, 0:HALF], square_low)
+            a_high, square_high = first_stage(i, HALF, HALF)
+            damping(damp[:, HALF:OWN], square_high[:, 0 : OWN - HALF])
+            damping(damp_share, square_high[:, OWN - HALF : HALF])
+            nc.scalar.copy(a_share, a_high[:, OWN - HALF : HALF])
+            nc.gpsimd.tensor_tensor(sig[:, OWN:S], a_share, damp_share, ALU.mult)
+            nc.vector.tensor_tensor(sig[:, 0:HALF], a_low, damp[:, 0:HALF], ALU.mult)
+            nc.vector.tensor_tensor(sig[:, HALF:OWN], a_high[:, 0 : OWN - HALF], damp[:, HALF:OWN], ALU.mult)
             if i in LOAD_AFTER:
                 late_loads[LOAD_AFTER[i]](LOAD_AFTER[i])
-            sig = tenant([P, S], F32, "sig", SIDE_AFTER.get(i, f"sig{i % 2}"))
-            if i == 1:
-                for h, a_ps in enumerate(sums):
-                    part = slice(h * HALF, (h + 1) * HALF)
-                    nc.vector.tensor_tensor(sig[:, part], a_ps, weighted[:, part], ALU.mult)
-            else:
-                nc.gpsimd.tensor_tensor(sig[:], amplitude[:], weighted, ALU.mult)
             return sig
 
         def rows_of(diff):
             return diff.rearrange("p (t m) -> p t m", t=PACK)
 
-        out_ps = []
+        def fetch(i, cols=slice(0, M_OUT)):
+            nc.vector.tensor_tensor(
+                slot(i)[:, cols],
+                pages[i % 2][:].indirect(entries(idx3, cols.start, cols.stop - cols.start)),
+                slot(i + 1)[:, cols],
+                ALU.subtract,
+            )
 
-        def score(g, z_part, cols, stop):
-            z_codes, z_scale = z_part
-            for n in range(N_OUT // P):
-                w3_codes, w3_scale = w3_operand(g * N_OUT + n * P)
-                nc.tensor.matmul_mx(
-                    out=out_ps[n][:, cols],
-                    lhsT=w3_codes,
-                    lhsT_scale=w3_scale,
-                    rhs=z_codes[:].bitcast(FP8X4),
-                    rhs_scale=z_scale[:],
-                    start=(g == 0),
-                    stop=stop,
-                )
-
-        def fetch(i):
+        def deal_rows(i):
             g, t = divmod(i, PACK)
-            if i == 0:
-                fetched[i] = tenant([P, M_OUT], F32, "fetched", "first_rest")[:]
-            else:
-                fetched[i] = slots[:, (i - 1) * M_OUT : i * M_OUT]
-            nc.vector.tensor_tensor(fetched[i], pages[i % PAGES][:].indirect(idx3[:]), margins[i], ALU.subtract)
-            if g == LAST:
-                return
             if t == 0:
-                diffs[g] = tenant([P, PACK * M_OUT], F32, "diffs", f"diffs{g}")[:]
+                diffs[g] = tenant([P, PACK * M_OUT], F32, "diffs", f"z{g}")[:]
             for j in range(PACK):
-                nc.sync.dma_start(rows_of(diffs[g])[QUAD * t : QUAD * (t + 1), j, :], fetched[i][j:P:PACK, :])
+                nc.sync.dma_start(rows_of(diffs[g])[QUAD * t : QUAD * (t + 1), j, :], slot(i)[j:P:PACK, :])
             if t == PACK - 1:
                 made["z_bf"] = tenant([P, M_OUT * PACK], BF16, "z_bf", "z_bf")
                 nc.scalar.activation(*interleaved(made["z_bf"][:], rows_of(diffs[g])), ACT.Relu)
 
-        def finish_last_pass():
-            diffs[LAST] = slots[:, (LAST * PACK - 1) * M_OUT : (TILES - 1) * M_OUT]
-            width = M_OUT // 2
-            low, high = slice(0, width), slice(width, M_OUT)
-            for cols in (low, high):
-                nc.vector.tensor_tensor(
-                    rows_of(diffs[LAST])[:, PACK - 1, cols],
-                    pages[(TILES - 1) % PAGES][:].indirect(entries(idx3, cols.start, width)),
-                    margins[TILES - 1][:, cols],
-                    ALU.subtract,
-                )
-            z_low = tenant([P, width * PACK], BF16, "z_low", "cast_w1_last")
-            z_high = tenant([P, width * PACK], BF16, "z_high", "z_bf")
-            nc.scalar.activation(*interleaved(z_low[:], rows_of(diffs[LAST])[:, :, low]), ACT.Relu)
-            nc.vector.tensor_scalar_max(*interleaved(z_high[:], rows_of(diffs[LAST])[:, :, high]), 0.0)
-            score(LAST, quantised("z_high", z_high, width), high, False)
-            score(LAST, quantised("z_low", z_low, width), low, True)
+        def out_sums():
+            blocks = N_OUT // P
+            sums = []
+            for cols in LAST_PIECES:
+                width = cols.stop - cols.start
+                per_bank = blocks if blocks * width <= HALF else 1
+                banks = []
+                for n in range(0, blocks, per_bank):
+                    tag = "b" if sum(len(b) for b in sums) + len(banks) < 4 else "a"
+                    bank = psum.tile([P, per_bank * width], F32, name="out_ps", tag=tag, bufs=4)
+                    banks.append((bank, n, per_bank))
+                sums.append(banks)
+            return sums
+
+        def score(g, banks, z_codes, z_scale):
+            width = z_codes.shape[1]
+            for bank, first, count in banks:
+                for k in range(count):
+                    w3_codes, w3_scale = w3_operand(g * N_OUT + (first + k) * P)
+                    nc.tensor.matmul_mx(
+                        out=bank[:, k * width : (k + 1) * width],
+                        lhsT=w3_codes,
+                        lhsT_scale=w3_scale,
+                        rhs=z_codes.bitcast(FP8X4),
+                        rhs_scale=z_scale,
+                        start=(g == 0 and k == 0),
+                        stop=(g == LAST and k == count - 1),
+                    )
+
+        def store(cols, bank, first, count, on_vector):
+            width = cols.stop - cols.start
+            result = keep.tile([P, count * width], F32, name=f"result{cols.start}_{first}")
+            if on_vector:
+                nc.vector.tensor_copy(result[:], bank[:])
+            else:
+                nc.scalar.copy(result[:], bank[:])
+            nc.sync.dma_start(
+                out[first * P : (first + count) * P, cols].rearrange("(k p) m -> p k m", p=P),
+                result[:].rearrange("p (k m) -> p k m", k=count),
+            )
+
+        def finish(sums):
+            for g in range(LAST):
+                codes, scales = z_q[g]
+                for cols, banks in zip(LAST_PIECES, sums):
+                    score(g, banks, codes[:, cols], scales[:, cols])
+            for cols in LAST_PIECES:
+                fetch(TILES - 1, cols)
+            rows = rows_of(slot(LAST * PACK, PACK))
+            z_bf = [
+                keep.tile([P, (cols.stop - cols.start) * PACK], BF16, name=f"z_last{cols.start}", align_bytes=ALIGN)
+                for cols in LAST_PIECES
+            ]
+
+            def close(k):
+                width = LAST_PIECES[k].stop - LAST_PIECES[k].start
+                codes, scales = quantised(f"z_last{k}", z_bf[k], width)
+                score(LAST, sums[k], codes[:], scales[:])
+
+            for k in range(2):
+                nc.scalar.activation(*interleaved(z_bf[k][:], rows[:, :, LAST_PIECES[k]]), ACT.Relu)
+            close(0)
+            nc.vector.tensor_scalar_max(*interleaved(z_bf[2][:], rows[:, :, LAST_PIECES[2]]), 0.0)
+            close(1)
+            close(2)
+            for k, (cols, banks) in enumerate(zip(LAST_PIECES, sums)):
+                for j, (bank, first, count) in enumerate(banks):
+                    store(cols, bank, first, count, on_vector=(k == 2 and j % 2 == 0))
 
         first_tile()
         for i in range(1, TILES):
             sig = signatures(i)
-            nc.vector.tensor_copy(pages[i % PAGES][:].indirect(idx2[:]), sig[:])
+            if i == 1:
+                cast_w1(0, "cast0")
+            if i in SIDE_WITH:
+                side_work[SIDE_WITH[i]](SIDE_WITH[i])
             fetch(i - 1)
-            if i in SIDE_AFTER:
-                side_work[SIDE_AFTER[i]](SIDE_AFTER[i])
+            if i - 1 < LAST * PACK:
+                deal_rows(i - 1)
+            scatter(i, 0, S, sig[:])
+            if i < PASSES:
+                cast_w1(i, f"cast{i}")
+            if i == PASSES:
+                for words in W3_PARTS:
+                    cast_w3(words)
             if i == PACK:
                 load_margins(LAST * PACK, PACK)
-        out_ps.extend(psum.tile([P, M_OUT], F32, name="out_ps", tag="a", bufs=4) for n in range(N_OUT // P))
-        for g in range(LAST):
-            score(g, z_q[g], slice(0, M_OUT), False)
-        finish_last_pass()
-
-        for n in range(N_OUT // P):
-            result = tenant([P, M_OUT], F32, "result", ("sig0", "sig1", "w2_words")[n])
-            if n % 2 == 1:
-                nc.scalar.copy(result[:], out_ps[n][:])
-            else:
-                nc.vector.tensor_copy(result[:], out_ps[n][:])
-            nc.sync.dma_start(out[n * P : (n + 1) * P, :], result[:])
+        finish(out_sums())

@@ -1,6 +1,7 @@
 from contextlib import ExitStack
 
 import concourse.mybir as mybir
+from concourse.masks import make_identity
 
 K, T, S, H, T2, M_OUT, N_OUT = 512, 4096, 1024, 1536, 2048, 512, 384
 FLOPS = 2 * K * H * S * 2 + 2 * H * N_OUT * M_OUT
@@ -32,14 +33,21 @@ RUN = 4
 
 FIRST_PIECES = ((0, 256), (256, 256), (512, 512))
 
-SHARE = 256
-OWN = S - SHARE
 
-SIDE_WITH = {1: "w1_pass0", 2: "w1_pass1", 3: "w2_words", 4: "w2_scales", 5: "w1_last", 6: "z0", 7: "w3_wide", 8: "w3_rest", 10: "z1"}
-LOAD_AFTER = {2: "table", 4: "late"}
+SIDE_WITH = {
+    1: "w1_pass0",
+    2: "w1_pass1",
+    4: "w1_pass2",
+    5: "w3_wide",
+    6: "z0",
+    7: "w3_rest",
+    10: "z1",
+}
+W3_LOAD_AFTER = 2
 W3_WIDE = 1024
 W3_PARTS = (slice(0, W3_WIDE), slice(W3_WIDE, PASSES * N_OUT))
-LAST_PIECES = (slice(0, 128), slice(128, 256), slice(256, 512))
+BLOCKS = M_OUT // P
+FETCH_RING = 2
 
 
 def tile_list_phishing_verdict_slots_kernel(
@@ -107,7 +115,6 @@ def tile_list_phishing_verdict_slots_kernel(
         nc.sync.dma_start(tab_w[:], tab_words[0].rearrange("p t i -> p (t i)").bitcast(I32))
         w2_w = {0: load_w2_words(0)}
         w2_s = keep.tile([P, H], U8, name="w2_s", align_bytes=ALIGN)
-        nc.gpsimd.memset(w2_s[:].bitcast(I32), 0)
         load_scale_rows(w2_s, w2_scales[0])
         weights = keep.tile([P, S], F32, name="weights")
         first_count = FIRST_PIECES[0][1]
@@ -117,27 +124,20 @@ def tile_list_phishing_verdict_slots_kernel(
         nc.sync.dma_start(weights[:, first_count:S], wgs[:, first_count:S])
         w1_raw = {0: load_w1(slice(2 * P, R_PASS), "w1_pass0_raw")}
         nc.sync.dma_start(idx3[:], offs3)
-        slots = keep.tile([P, (TILES + 1) * M_OUT], F32, name="slots")
 
-        def slot(k, count=1):
-            return slots[:, k * M_OUT : (k + count) * M_OUT]
+        margins = {}
 
-        def load_margins(first, count):
-            g = first // PACK
-            order = "(p t) m -> p t m" if g == LAST else "(t p) m -> p t m"
-            rows = margin[g * R_PASS : (g + 1) * R_PASS, :].rearrange(order, t=PACK)
+        def load_margin(g):
+            margins[g] = keep.tile([P, PACK, M_OUT], F32, name=f"margin{g}")
             nc.sync.dma_start(
-                slot(first + 1, count).rearrange("p (t m) -> p t m", t=count),
-                rows[:, first - g * PACK : first - g * PACK + count, :],
+                margins[g][:], margin[g * R_PASS : (g + 1) * R_PASS, :].rearrange("(t p) m -> p t m", t=PACK)
             )
 
-        load_margins(0, 1)
-        w1_raw[1] = load_w1(slice(R_PASS, 2 * R_PASS), "w1_pass1_raw")
-        w2_w[1] = load_w2_words(1)
-        load_margins(1, PACK - 1)
-        w2_w[LAST] = load_w2_words(LAST)
-        w1_raw[LAST] = load_w1(slice(LAST * R_PASS, H), "w1_last_raw")
-        load_margins(PACK, PACK)
+        for g in range(1, PASSES):
+            load_margin(g - 1)
+            w1_raw[g] = load_w1(slice(g * R_PASS, (g + 1) * R_PASS), f"w1_pass{g}_raw")
+            w2_w[g] = load_w2_words(g)
+        load_margin(LAST)
 
         tab_s = keep.tile([P, T], U8, name="tab_s", align_bytes=ALIGN)
         nc.vector.memset(tab_s[:].bitcast(I32), 0)
@@ -160,8 +160,16 @@ def tile_list_phishing_verdict_slots_kernel(
             nc.vector.tensor_copy(v_s[h][:], tab_s[:].indirect(entries(idx, h * HALF, HALF)))
             nc.vector.tensor_copy(v_w[h][:], tab_w[:].bitcast(U32).indirect(entries(idx, h * HALF, HALF)))
 
+        identity = keep.tile([P, P], F32, name="identity")
+        make_identity(nc, identity[:])
+
         w1_q = {}
-        diffs = {}
+        w3_q = {}
+        z_q = {}
+        casts = {}
+        fetched = {}
+        negated = {}
+        turned = {}
         made = {}
 
         def load_w3(tag):
@@ -172,50 +180,13 @@ def tile_list_phishing_verdict_slots_kernel(
                 )
             made["w3_raw"] = w3_raw
 
-        def load_last_weights(tag):
-            weights_last = tenant([P, PACK, S], F32, "weights_last", tag)
-            for q in range(QUADS):
-                nc.sync.dma_start(
-                    weights_last[QUAD * q : QUAD * (q + 1), :, :], wgs.rearrange("(u t) j -> u t j", t=PACK)
-                )
-            made["weights_last"] = weights_last
-
-        late_loads = {"table": load_w3, "late": load_last_weights}
-
-        casts = {}
-
-        def cast_w1(g, bf_tag):
-            width = w1_raw[g].shape[2]
-            bf = tenant([P, width * PACK], BF16, "w1_bf", bf_tag)
-            if g == LAST:
-                dst = bf[:].rearrange("p (t u j) -> p u t j", t=PACK, j=PACK)
-                rows = w1_raw[g][:].rearrange("p j (u t) -> p u t j", t=PACK)
-            else:
-                dst, rows = interleaved(bf[:], w1_raw[g][:])
-            nc.scalar.activation(dst, rows, ACT.Copy)
-            casts[f"w1_q{g}"] = bf
+        def cast_w1(g):
+            bf = keep.tile([P, w1_raw[g].shape[2] * PACK], BF16, name=f"w1_bf{g}", align_bytes=ALIGN)
+            nc.scalar.activation(*interleaved(bf[:], w1_raw[g][:]), ACT.Copy)
+            casts[f"w1_pass{g}"] = bf
 
         def quantise_w1(g, tag):
-            w1_q[g] = quantised(f"w1_q{g}", casts[f"w1_q{g}"], w1_raw[g].shape[2], tag)
-
-        def reorder_w2_words(tag):
-            words = tenant([P, 2 * R_PASS], U8, "w2_w_last", tag)
-            nc.vector.tensor_copy(
-                words[:].bitcast(U16).rearrange("p (t u) -> p t u", t=PACK),
-                w2_w[LAST][:].bitcast(U16).rearrange("p (u t) -> p t u", t=PACK),
-            )
-            made["w2_words"] = words
-
-        def reorder_w2_scales(tag):
-            scales = tenant([P, R_PASS], U8, "w2_s_last", tag)
-            nc.vector.tensor_copy(
-                scales[:].rearrange("p (t u) -> p t u", t=PACK),
-                w2_s[:, LAST * R_PASS : H].rearrange("p (u t) -> p t u", t=PACK),
-            )
-            made["w2_scales"] = scales
-
-        w3_q = {}
-        z_q = {}
+            w1_q[g] = quantised(tag, casts[tag], w1_raw[g].shape[2])
 
         def cast_w3(words):
             w3_bf = keep.tile([P, (words.stop - words.start) * PACK], BF16, name=f"w3_bf{words.start}", align_bytes=ALIGN)
@@ -239,14 +210,12 @@ def tile_list_phishing_verdict_slots_kernel(
             return codes[:, cols].bitcast(FP8X4), scales[:, cols]
 
         def quantise_z(g, tag):
-            z_q[g] = quantised(tag, made["z_bf"], M_OUT, tag)
+            z_q[g] = quantised(tag, casts[tag], M_OUT)
 
         side_work = {
             "w1_pass0": lambda tag: quantise_w1(0, tag),
             "w1_pass1": lambda tag: quantise_w1(1, tag),
-            "w1_last": lambda tag: quantise_w1(LAST, tag),
-            "w2_words": reorder_w2_words,
-            "w2_scales": reorder_w2_scales,
+            "w1_pass2": lambda tag: quantise_w1(2, tag),
             "w3_wide": lambda tag: quantise_w3(W3_PARTS[0], tag),
             "w3_rest": lambda tag: quantise_w3(W3_PARTS[1], tag),
             "z0": lambda tag: quantise_z(0, tag),
@@ -265,203 +234,188 @@ def tile_list_phishing_verdict_slots_kernel(
 
         def w2_operand(i):
             g, t = divmod(i, PACK)
-            if g == LAST:
-                words, scales = made["w2_words"], made["w2_scales"]
-            else:
-                words, scales = w2_w[g], w2_s[:, g * R_PASS : (g + 1) * R_PASS]
-            return words[:, 2 * t * P : 2 * (t + 1) * P].bitcast(FP4X4), scales[:, t * P : (t + 1) * P]
+            return w2_w[g][:, 2 * t * P : 2 * (t + 1) * P].bitcast(FP4X4), w2_s[:, i * P : (i + 1) * P]
 
-        def first_stage(i, first, count):
-            w1_codes, w1_scale = w1_operand(i)
-            w2_codes, w2_scale = w2_operand(i)
+        def first_sum(tag, operand, first, count):
+            codes, scale = operand
             h = first // HALF
             part = slice(first - h * HALF, first - h * HALF + count)
-            b_ps = psum.tile([P, HALF], F32, name="b_ps", tag="b", bufs=4)
+            bank = psum.tile([P, HALF], F32, name="first_ps", tag=tag, bufs=2)
             nc.tensor.matmul_mx(
-                out=b_ps[:, 0:count],
-                lhsT=w2_codes,
-                lhsT_scale=w2_scale,
+                out=bank[:, 0:count],
+                lhsT=codes,
+                lhsT_scale=scale,
                 rhs=v_w[h][:, part].bitcast(FP8X4),
                 rhs_scale=v_s[h][:, part],
                 start=True,
                 stop=True,
             )
-            a_ps = psum.tile([P, HALF], F32, name="a_ps", tag="a", bufs=4)
-            nc.tensor.matmul_mx(
-                out=a_ps[:, 0:count],
-                lhsT=w1_codes,
-                lhsT_scale=w1_scale,
-                rhs=v_w[h][:, part].bitcast(FP8X4),
-                rhs_scale=v_s[h][:, part],
-                start=True,
-                stop=True,
-            )
-            if (i, first) == (1, 0):
-                square = tenant([P, HALF], F32, "square", "w1_second")
-            else:
-                square = ring.tile([P, HALF], F32, name="square", tag="square", bufs=2)
-            nc.scalar.activation(square[:, 0:count], b_ps[:, 0:count], ACT.Square)
-            return a_ps[:, 0:count], square[:, 0:count]
+            return bank[:, 0:count]
 
-        def damping(dst, square):
+        def scratch(count):
+            return ring.tile([P, HALF], F32, name="square", tag="square", bufs=2)[:, 0:count]
+
+        def damping(i, first, count, dst, square):
+            nc.scalar.activation(square, first_sum("b", w2_operand(i), first, count), ACT.Square)
             nc.scalar.activation(dst, square, ACT.Exp, scale=-1.0)
 
         def scatter(i, first, count, sig):
-            g, t = divmod(i, PACK)
-            weight = made["weights_last"][:, t, :] if g == LAST else weights[:]
             nc.vector.tensor_tensor(
-                pages[i % 2][:].indirect(entries(idx2, first, count)), sig, weight[:, first : first + count], ALU.mult
+                pages[i % 2][:].indirect(entries(idx2, first, count)), sig, weights[:, first : first + count], ALU.mult
             )
 
         def first_tile():
-            low = ring.tile([P, OWN], F32, name="damp", tag="damp", bufs=2)
+            low = ring.tile([P, HALF], F32, name="damp", tag="damp", bufs=2)
             for first, count in FIRST_PIECES:
-                a_ps, square = first_stage(0, first, count)
                 if first < HALF:
                     damp = low[:, first : first + count]
-                    damping(damp, square)
+                    damping(0, first, count, damp, scratch(count))
                     sig = keep.tile([P, count], F32, name=f"sig_first{first}")
                 else:
-                    damp = slot(0)
-                    damping(damp, square)
+                    damp = tenant([P, count], F32, "damp", f"fetch{FETCH_RING - 1}")[:]
+                    damping(0, first, count, damp, scratch(count))
                     second_bf = tenant([P, P * PACK], BF16, "second_bf", "first_rest")
                     nc.scalar.activation(*interleaved(second_bf[:], w1_second[:]), ACT.Copy)
                     made["w1_second"] = quantised("w1_tile1", second_bf, P)
                     sig = tenant([P, count], F32, "sig_first", "first_rest")
-                nc.vector.tensor_tensor(sig[:], a_ps, damp, ALU.mult)
+                nc.vector.tensor_tensor(sig[:], first_sum("a", w1_operand(0), first, count), damp, ALU.mult)
                 scatter(0, first, count, sig[:])
 
-        def signatures(i):
-            if SIDE_WITH.get(i) in ("z0", "z1"):
-                damp = tenant([P, S], F32, "damp", SIDE_WITH[i])
-                damp_share = damp[:, OWN:S]
+        def damping_share(i):
+            damp_share = tenant([P, HALF], F32, "damp_share", SIDE_WITH.get(i, f"damp_share{i % 2}"))
+            damping(i, HALF, HALF, damp_share[:], scratch(HALF))
+            return damp_share
+
+        def signatures(i, damp_share):
+            if i == W3_LOAD_AFTER:
+                damp = tenant([P, HALF], F32, "damp", "table")
             else:
-                if i in LOAD_AFTER:
-                    damp = tenant([P, OWN], F32, "damp", LOAD_AFTER[i])
-                else:
-                    damp = ring.tile([P, OWN], F32, name="damp", tag="damp", bufs=2)
-                damp_share = tenant([P, SHARE], F32, "damp_share", SIDE_WITH.get(i, f"damp_share{i % 2}"))[:]
-            a_share = slot(i - 1)[:, 0:SHARE]
+                damp = ring.tile([P, HALF], F32, name="damp", tag="damp", bufs=2)
+            square = tenant([P, HALF], F32, "square", f"fetch{(i - 1) % FETCH_RING}")
+            damping(i, 0, HALF, damp[:], square[:])
             sig = ring.tile([P, S], F32, name="sig", tag="sig", bufs=2)
-            a_low, square_low = first_stage(i, 0, HALF)
-            damping(damp[:, 0:HALF], square_low)
-            a_high, square_high = first_stage(i, HALF, HALF)
-            damping(damp[:, HALF:OWN], square_high[:, 0 : OWN - HALF])
-            damping(damp_share, square_high[:, OWN - HALF : HALF])
-            nc.scalar.copy(a_share, a_high[:, OWN - HALF : HALF])
-            nc.gpsimd.tensor_tensor(sig[:, OWN:S], a_share, damp_share, ALU.mult)
-            nc.vector.tensor_tensor(sig[:, 0:HALF], a_low, damp[:, 0:HALF], ALU.mult)
-            nc.vector.tensor_tensor(sig[:, HALF:OWN], a_high[:, 0 : OWN - HALF], damp[:, HALF:OWN], ALU.mult)
-            if i in LOAD_AFTER:
-                late_loads[LOAD_AFTER[i]](LOAD_AFTER[i])
+            a_low = first_sum("a", w1_operand(i), 0, HALF)
+            a_high = first_sum("a", w1_operand(i), HALF, HALF)
+            a_share = tenant([P, HALF], F32, "a_share", f"fetch{i % FETCH_RING}")
+            nc.scalar.copy(a_share[:], a_high)
+            nc.gpsimd.tensor_tensor(sig[:, HALF:S], a_share[:], damp_share[:], ALU.mult)
+            nc.vector.tensor_tensor(sig[:, 0:HALF], a_low, damp[:], ALU.mult)
+            if i == W3_LOAD_AFTER:
+                load_w3("table")
             return sig
 
-        def rows_of(diff):
-            return diff.rearrange("p (t m) -> p t m", t=PACK)
-
-        def fetch(i, cols=slice(0, M_OUT)):
-            nc.vector.tensor_tensor(
-                slot(i)[:, cols],
-                pages[i % 2][:].indirect(entries(idx3, cols.start, cols.stop - cols.start)),
-                slot(i + 1)[:, cols],
-                ALU.subtract,
-            )
-
-        def deal_rows(i):
+        def negate_margin(i):
             g, t = divmod(i, PACK)
-            if t == 0:
-                diffs[g] = tenant([P, PACK * M_OUT], F32, "diffs", f"z{g}")[:]
-            for j in range(PACK):
-                nc.sync.dma_start(rows_of(diffs[g])[QUAD * t : QUAD * (t + 1), j, :], slot(i)[j:P:PACK, :])
-            if t == PACK - 1:
-                made["z_bf"] = tenant([P, M_OUT * PACK], BF16, "z_bf", "z_bf")
-                nc.scalar.activation(*interleaved(made["z_bf"][:], rows_of(diffs[g])), ACT.Relu)
+            negated[i] = ring.tile([P, M_OUT], F32, name="negated", tag="negated", bufs=2)
+            nc.scalar.activation(negated[i][:], margins[g][:, t, :], ACT.Copy, scale=-1.0)
 
-        def out_sums():
-            blocks = N_OUT // P
-            sums = []
-            for cols in LAST_PIECES:
-                width = cols.stop - cols.start
-                per_bank = blocks if blocks * width <= HALF else 1
-                banks = []
-                for n in range(0, blocks, per_bank):
-                    tag = "b" if sum(len(b) for b in sums) + len(banks) < 4 else "a"
-                    bank = psum.tile([P, per_bank * width], F32, name="out_ps", tag=tag, bufs=4)
-                    banks.append((bank, n, per_bank))
-                sums.append(banks)
-            return sums
-
-        def score(g, banks, z_codes, z_scale):
-            width = z_codes.shape[1]
-            for bank, first, count in banks:
-                for k in range(count):
-                    w3_codes, w3_scale = w3_operand(g * N_OUT + (first + k) * P)
-                    nc.tensor.matmul_mx(
-                        out=bank[:, k * width : (k + 1) * width],
-                        lhsT=w3_codes,
-                        lhsT_scale=w3_scale,
-                        rhs=z_codes.bitcast(FP8X4),
-                        rhs_scale=z_scale,
-                        start=(g == 0 and k == 0),
-                        stop=(g == LAST and k == count - 1),
+        def exceed(i, blocks, terms):
+            g, t = divmod(i, PACK)
+            count = blocks.stop - blocks.start
+            bank = psum.tile([P, count * P], F32, name="turn_ps", tag="turn", bufs=2)
+            for k in range(count):
+                cols = slice((blocks.start + k) * P, (blocks.start + k + 1) * P)
+                for n, rows in enumerate(terms):
+                    nc.tensor.matmul(
+                        bank[:, k * P : (k + 1) * P],
+                        lhsT=rows[:, cols],
+                        rhs=identity[:],
+                        start=(n == 0),
+                        stop=(n == len(terms) - 1),
+                        is_transpose=True,
                     )
-
-        def store(cols, bank, first, count, on_vector):
-            width = cols.stop - cols.start
-            result = keep.tile([P, count * width], F32, name=f"result{cols.start}_{first}")
-            if on_vector:
-                nc.vector.tensor_copy(result[:], bank[:])
-            else:
-                nc.scalar.copy(result[:], bank[:])
-            nc.sync.dma_start(
-                out[first * P : (first + count) * P, cols].rearrange("(k p) m -> p k m", p=P),
-                result[:].rearrange("p (k m) -> p k m", k=count),
+            nc.scalar.activation(
+                turned[g][:, blocks, t * P : (t + 1) * P], bank[:].rearrange("p (k r) -> p k r", k=count), ACT.Relu
             )
 
-        def finish(sums):
+        def turn_back(g, blocks, z_bf, on_vector):
+            count = blocks.stop - blocks.start
+            bank = psum.tile([P, count * 2 * P], F32, name="back_ps", tag="back", bufs=2)
+            for k in range(count):
+                pairs = turned[g][:, blocks.start + k, :].bitcast(F32)
+                for u in range(2):
+                    nc.tensor.transpose(
+                        bank[:, (2 * k + u) * P : (2 * k + u + 1) * P], pairs[:, u : 2 * P : 2], identity[:]
+                    )
+            dst = z_bf.bitcast(F32).rearrange("p (k m u) -> p k m u", k=count, u=2)
+            src = bank[:].rearrange("p (k u m) -> p k m u", k=count, u=2)
+            if on_vector:
+                nc.vector.tensor_copy(dst, src)
+            else:
+                nc.scalar.copy(dst, src)
+
+        def finish_tile(i):
+            g, t = divmod(i, PACK)
+            every = slice(0, BLOCKS)
+            if t == 0:
+                turned[g] = tenant([P, BLOCKS, R_PASS], BF16, "turned", f"z{g}")
+            fetched[i] = tenant([P, M_OUT], F32, "fetched", f"fetch{i % FETCH_RING}")
+            nc.vector.tensor_copy(fetched[i][:], pages[i % 2][:].indirect(idx3[:]))
+            negate_margin(i)
+            exceed(i, every, (negated[i], fetched[i]))
+            if t == PACK - 1:
+                z_bf = tenant([P, M_OUT * PACK], BF16, "z_bf", "z_bf")
+                for first in range(0, BLOCKS, 2):
+                    part = z_bf[:, first * P * PACK : (first + 2) * P * PACK]
+                    turn_back(g, slice(first, first + 2), part, on_vector=False)
+                casts[f"z{g}"] = z_bf
+
+        def score(g, bank, z_codes, z_scale):
+            for k in range(N_OUT // P):
+                w3_codes, w3_scale = w3_operand(g * N_OUT + k * P)
+                nc.tensor.matmul_mx(
+                    out=bank[:, k * P : (k + 1) * P],
+                    lhsT=w3_codes,
+                    lhsT_scale=w3_scale,
+                    rhs=z_codes.bitcast(FP8X4),
+                    rhs_scale=z_scale,
+                    start=(g == 0 and k == 0),
+                    stop=(g == LAST and k == N_OUT // P - 1),
+                )
+
+        def finish():
+            i = TILES - 1
+            banks = [psum.tile([P, N_OUT], F32, name="out_ps", tag="ba"[b % 2], bufs=2) for b in range(BLOCKS)]
             for g in range(LAST):
                 codes, scales = z_q[g]
-                for cols, banks in zip(LAST_PIECES, sums):
-                    score(g, banks, codes[:, cols], scales[:, cols])
-            for cols in LAST_PIECES:
-                fetch(TILES - 1, cols)
-            rows = rows_of(slot(LAST * PACK, PACK))
-            z_bf = [
-                keep.tile([P, (cols.stop - cols.start) * PACK], BF16, name=f"z_last{cols.start}", align_bytes=ALIGN)
-                for cols in LAST_PIECES
-            ]
-
-            def close(k):
-                width = LAST_PIECES[k].stop - LAST_PIECES[k].start
-                codes, scales = quantised(f"z_last{k}", z_bf[k], width)
-                score(LAST, sums[k], codes[:], scales[:])
-
-            for k in range(2):
-                nc.scalar.activation(*interleaved(z_bf[k][:], rows[:, :, LAST_PIECES[k]]), ACT.Relu)
-            close(0)
-            nc.vector.tensor_scalar_max(*interleaved(z_bf[2][:], rows[:, :, LAST_PIECES[2]]), 0.0)
-            close(1)
-            close(2)
-            for k, (cols, banks) in enumerate(zip(LAST_PIECES, sums)):
-                for j, (bank, first, count) in enumerate(banks):
-                    store(cols, bank, first, count, on_vector=(k == 2 and j % 2 == 0))
+                for b in range(BLOCKS):
+                    score(g, banks[b], codes[:, b * P : (b + 1) * P], scales[:, b * P : (b + 1) * P])
+            fetched[i] = tenant([P, M_OUT], F32, "fetched", f"fetch{(i - 1) % FETCH_RING}")
+            for b in range(BLOCKS):
+                cols = slice(b * P, (b + 1) * P)
+                nc.vector.tensor_tensor(
+                    fetched[i][:, cols],
+                    pages[i % 2][:].indirect(entries(idx3, cols.start, P)),
+                    margins[LAST][:, PACK - 1, cols],
+                    ALU.subtract,
+                )
+                exceed(i, slice(b, b + 1), (fetched[i],))
+            for b in range(BLOCKS):
+                z_bf = keep.tile([P, P * PACK], BF16, name=f"z_last{b}", align_bytes=ALIGN)
+                turn_back(LAST, slice(b, b + 1), z_bf[:], on_vector=True)
+                codes, scales = quantised(f"z_last{b}", z_bf, P)
+                score(LAST, banks[b], codes[:], scales[:])
+            for b in range(BLOCKS):
+                result = keep.tile([P, N_OUT], F32, name=f"result{b}")
+                nc.scalar.copy(result[:], banks[b][:])
+                nc.sync.dma_start(
+                    out[:, b * P : (b + 1) * P].rearrange("(k p) m -> p k m", p=P),
+                    result[:].rearrange("p (k m) -> p k m", m=P),
+                )
 
         first_tile()
+        ahead = damping_share(1)
         for i in range(1, TILES):
-            sig = signatures(i)
-            if i == 1:
-                cast_w1(0, "cast0")
-            if i in SIDE_WITH:
-                side_work[SIDE_WITH[i]](SIDE_WITH[i])
-            fetch(i - 1)
-            if i - 1 < LAST * PACK:
-                deal_rows(i - 1)
-            scatter(i, 0, S, sig[:])
-            if i < PASSES:
-                cast_w1(i, f"cast{i}")
-            if i == PASSES:
+            sig = signatures(i, ahead)
+            if i + 1 < TILES:
+                ahead = damping_share(i + 1)
+            if i <= PASSES:
+                cast_w1(i - 1)
+            if i == PACK:
                 for words in W3_PARTS:
                     cast_w3(words)
-            if i == PACK:
-                load_margins(LAST * PACK, PACK)
-        finish(out_sums())
+            finish_tile(i - 1)
+            if i in SIDE_WITH:
+                side_work[SIDE_WITH[i]](SIDE_WITH[i])
+            scatter(i, 0, S, sig[:])
+        finish()

@@ -34,20 +34,18 @@ RUN = 4
 FIRST_PIECES = ((0, 256), (256, 256), (512, 512))
 
 
-SIDE_WITH = {
-    1: "w1_pass0",
-    2: "w1_pass1",
-    4: "w1_pass2",
-    5: "w3_wide",
-    6: "z0",
-    7: "w3_rest",
-    10: "z1",
-}
-W3_LOAD_AFTER = 2
-W3_WIDE = 1024
-W3_PARTS = (slice(0, W3_WIDE), slice(W3_WIDE, PASSES * N_OUT))
+ROUNDS = (
+    ((1, 2), 512, "w1_second"),
+    ((3, 4), 640, "w1_third"),
+    ((5, 6), 640, "w1_last"),
+    ((7, 8), 640, "z0"),
+    ((9, 10), 640, "w3"),
+    ((11,), 896, "z1"),
+)
+SPARE = 896
+W1_PARTS = {"w1_tile0": (0, 1), "w1_early": (1, 3), "w1_second": (3, 5), "w1_third": (5, 9), "w1_last": (9, 12)}
+BANKS = {"a_own": 2, "a_share": 1, "b": 1, "turn": 2, "back": 2}
 BLOCKS = M_OUT // P
-FETCH_RING = 2
 
 
 def tile_list_phishing_verdict_slots_kernel(
@@ -73,10 +71,12 @@ def tile_list_phishing_verdict_slots_kernel(
                     rows[PACK * q : PACK * (q + 1), :].bitcast(I32),
                 )
 
-        def load_w1(cols, tag):
-            raw = tenant([P, PACK, cols.stop - cols.start], F32, "w1_raw", tag)
-            nc.sync.dma_start(raw[:], w1[:, cols].rearrange("(p j) c -> p j c", j=PACK))
-            return raw
+        w1_raw = {}
+
+        def load_w1(part):
+            first, stop = W1_PARTS[part]
+            w1_raw[part] = keep.tile([P, PACK, (stop - first) * P], F32, name=part + "_raw")
+            nc.sync.dma_start(w1_raw[part][:], w1[:, first * P : stop * P].rearrange("(p j) c -> p j c", j=PACK))
 
         def load_w2_words(g):
             words = keep.tile([P, 2 * R_PASS], U8, name=f"w2_w{g}", align_bytes=ALIGN)
@@ -110,7 +110,7 @@ def tile_list_phishing_verdict_slots_kernel(
         tab_scale_rows = tenant([P, T], U8, "tab_scale_rows", "scale_rows")
         load_scale_rows(tab_scale_rows, tab_scales[0])
         nc.sync.dma_start(idx[:], offs)
-        w1_first = load_w1(slice(0, P), "w1_first")
+        load_w1("w1_tile0")
         tab_w = tenant([P, T], I32, "tab_w", "table")
         nc.sync.dma_start(tab_w[:], tab_words[0].rearrange("p t i -> p (t i)").bitcast(I32))
         w2_w = {0: load_w2_words(0)}
@@ -120,23 +120,25 @@ def tile_list_phishing_verdict_slots_kernel(
         first_count = FIRST_PIECES[0][1]
         nc.sync.dma_start(idx2[:], offs2)
         nc.sync.dma_start(weights[:, 0:first_count], wgs[:, 0:first_count])
-        w1_second = load_w1(slice(P, 2 * P), "w1_second")
+        load_w1("w1_early")
         nc.sync.dma_start(weights[:, first_count:S], wgs[:, first_count:S])
-        w1_raw = {0: load_w1(slice(2 * P, R_PASS), "w1_pass0_raw")}
         nc.sync.dma_start(idx3[:], offs3)
 
         margins = {}
 
         def load_margin(g):
-            margins[g] = keep.tile([P, PACK, M_OUT], F32, name=f"margin{g}")
+            margins[g] = tenant([P, PACK, M_OUT], F32, "margin", f"margin{g}")
             nc.sync.dma_start(
                 margins[g][:], margin[g * R_PASS : (g + 1) * R_PASS, :].rearrange("(t p) m -> p t m", t=PACK)
             )
 
-        for g in range(1, PASSES):
-            load_margin(g - 1)
-            w1_raw[g] = load_w1(slice(g * R_PASS, (g + 1) * R_PASS), f"w1_pass{g}_raw")
-            w2_w[g] = load_w2_words(g)
+        load_w1("w1_second")
+        w2_w[1] = load_w2_words(1)
+        load_margin(0)
+        load_w1("w1_third")
+        load_w1("w1_last")
+        w2_w[LAST] = load_w2_words(LAST)
+        load_margin(1)
         load_margin(LAST)
 
         tab_s = keep.tile([P, T], U8, name="tab_s", align_bytes=ALIGN)
@@ -148,8 +150,8 @@ def tile_list_phishing_verdict_slots_kernel(
             nc.vector.tensor_copy(tab_s[live, :].bitcast(I32), tab_scale_rows[live, :].bitcast(I32))
 
         first_bf = tenant([P, P * PACK], BF16, "first_bf", "page_odd")
-        nc.scalar.activation(*interleaved(first_bf[:], w1_first[:]), ACT.Copy)
-        w1_q_first = quantised("w1_tile0", first_bf, P)
+        nc.scalar.activation(*interleaved(first_bf[:], w1_raw["w1_tile0"][:]), ACT.Copy)
+        w1_q = {"w1_tile0": quantised("w1_tile0", first_bf, P)}
         page_odd = tenant([P, T2], F32, "page_odd", "page_odd")
         nc.gpsimd.memset(page_odd[:], 0.0)
         pages = [page_even, page_odd]
@@ -163,73 +165,38 @@ def tile_list_phishing_verdict_slots_kernel(
         identity = keep.tile([P, P], F32, name="identity")
         make_identity(nc, identity[:])
 
-        w1_q = {}
-        w3_q = {}
-        z_q = {}
         casts = {}
-        fetched = {}
-        negated = {}
+        quants = {}
         turned = {}
-        made = {}
 
-        def load_w3(tag):
-            w3_raw = tenant([P, PASSES, PACK, N_OUT], F32, "w3_raw", tag)
-            for g in range(PASSES):
-                nc.sync.dma_start(
-                    w3_raw[:, g, :, :], w3[g * R_PASS : (g + 1) * R_PASS, :].rearrange("(p j) n -> p j n", j=PACK)
-                )
-            made["w3_raw"] = w3_raw
+        def cast_w1(part, tag):
+            bf = tenant([P, w1_raw[part].shape[2] * PACK], BF16, part + "_bf", tag)
+            nc.scalar.activation(*interleaved(bf[:], w1_raw[part][:]), ACT.Copy)
+            casts[part] = bf
 
-        def cast_w1(g):
-            bf = keep.tile([P, w1_raw[g].shape[2] * PACK], BF16, name=f"w1_bf{g}", align_bytes=ALIGN)
-            nc.scalar.activation(*interleaved(bf[:], w1_raw[g][:]), ACT.Copy)
-            casts[f"w1_pass{g}"] = bf
+        w3_raw = tenant([P, PASSES, PACK, N_OUT], F32, "w3_raw", "table")
+        for g in range(PASSES):
+            nc.sync.dma_start(
+                w3_raw[:, g, :, :], w3[g * R_PASS : (g + 1) * R_PASS, :].rearrange("(p j) n -> p j n", j=PACK)
+            )
+        casts["w3"] = keep.tile([P, LAST * N_OUT * PACK], BF16, name="w3_bf", align_bytes=ALIGN)
+        casts["w3_last"] = keep.tile([P, N_OUT * PACK], BF16, name="w3_last_bf", align_bytes=ALIGN)
 
-        def quantise_w1(g, tag):
-            w1_q[g] = quantised(tag, casts[tag], w1_raw[g].shape[2])
+        def cast_w3(g):
+            part = casts["w3_last"][:] if g == LAST else casts["w3"][:, g * N_OUT * PACK : (g + 1) * N_OUT * PACK]
+            nc.scalar.activation(*interleaved(part, w3_raw[:, g, :, :]), ACT.Copy)
 
-        def cast_w3(words):
-            w3_bf = keep.tile([P, (words.stop - words.start) * PACK], BF16, name=f"w3_bf{words.start}", align_bytes=ALIGN)
-            for g in range(PASSES):
-                lo, hi = max(words.start, g * N_OUT), min(words.stop, (g + 1) * N_OUT)
-                if lo < hi:
-                    dst, rows = interleaved(
-                        w3_bf[:, (lo - words.start) * PACK : (hi - words.start) * PACK],
-                        made["w3_raw"][:, g, :, lo - g * N_OUT : hi - g * N_OUT],
-                    )
-                    nc.scalar.activation(dst, rows, ACT.Copy)
-            casts[words.start] = w3_bf
-
-        def quantise_w3(words, tag):
-            w3_q[words.start] = quantised(tag, casts[words.start], words.stop - words.start, tag)
-
-        def w3_operand(word):
-            first = W3_WIDE if word >= W3_WIDE else 0
-            codes, scales = w3_q[first]
-            cols = slice(word - first, word - first + P)
-            return codes[:, cols].bitcast(FP8X4), scales[:, cols]
-
-        def quantise_z(g, tag):
-            z_q[g] = quantised(tag, casts[tag], M_OUT)
-
-        side_work = {
-            "w1_pass0": lambda tag: quantise_w1(0, tag),
-            "w1_pass1": lambda tag: quantise_w1(1, tag),
-            "w1_pass2": lambda tag: quantise_w1(2, tag),
-            "w3_wide": lambda tag: quantise_w3(W3_PARTS[0], tag),
-            "w3_rest": lambda tag: quantise_w3(W3_PARTS[1], tag),
-            "z0": lambda tag: quantise_z(0, tag),
-            "z1": lambda tag: quantise_z(1, tag),
-        }
+        def side_work(name):
+            made = quantised(name, casts[name], casts[name].shape[1] // PACK)
+            if name in W1_PARTS:
+                w1_q[name] = made
+            else:
+                quants[name] = made
 
         def w1_operand(i):
-            g, t = divmod(i, PACK)
-            if i == 0:
-                (codes, scales), col = w1_q_first, 0
-            elif i == 1:
-                (codes, scales), col = made["w1_second"], 0
-            else:
-                (codes, scales), col = w1_q[g], (t - 2 if g == 0 else t) * P
+            part = [name for name in W1_PARTS if W1_PARTS[name][0] <= i < W1_PARTS[name][1]][0]
+            codes, scales = w1_q[part]
+            col = (i - W1_PARTS[part][0]) * P
             return codes[:, col : col + P].bitcast(FP8X4), scales[:, col : col + P]
 
         def w2_operand(i):
@@ -240,7 +207,7 @@ def tile_list_phishing_verdict_slots_kernel(
             codes, scale = operand
             h = first // HALF
             part = slice(first - h * HALF, first - h * HALF + count)
-            bank = psum.tile([P, HALF], F32, name="first_ps", tag=tag, bufs=2)
+            bank = psum.tile([P, HALF], F32, name="first_ps", tag=tag, bufs=BANKS[tag])
             nc.tensor.matmul_mx(
                 out=bank[:, 0:count],
                 lhsT=codes,
@@ -255,8 +222,12 @@ def tile_list_phishing_verdict_slots_kernel(
         def scratch(count):
             return ring.tile([P, HALF], F32, name="square", tag="square", bufs=2)[:, 0:count]
 
-        def damping(i, first, count, dst, square):
-            nc.scalar.activation(square, first_sum("b", w2_operand(i), first, count), ACT.Square)
+        def squared(i, first, count, square):
+            tag = ("turn", "back")[first // HALF] if i <= ROUNDS[0][0][0] else "b"
+            nc.scalar.activation(square, first_sum(tag, w2_operand(i), first, count), ACT.Square)
+            return square
+
+        def damping(dst, square):
             nc.scalar.activation(dst, square, ACT.Exp, scale=-1.0)
 
         def scatter(i, first, count, sig):
@@ -264,55 +235,94 @@ def tile_list_phishing_verdict_slots_kernel(
                 pages[i % 2][:].indirect(entries(idx2, first, count)), sig, weights[:, first : first + count], ALU.mult
             )
 
+        stretches = keep.tile([P, 2 * (SPARE + 2 * S)], F32, name="stretches")
+
+        def stretch(r, first, count):
+            start = (r % 2) * (SPARE + 2 * S) + SPARE + first
+            return stretches[:, start : start + count]
+
         def first_tile():
-            low = ring.tile([P, HALF], F32, name="damp", tag="damp", bufs=2)
+            low = keep.tile([P, HALF], F32, name="damp_first")
             for first, count in FIRST_PIECES:
+                damp = low[:, first : first + count] if first < HALF else stretch(0, -count // 2, count)
+                damping(damp, squared(0, first, count, scratch(count)))
                 if first < HALF:
-                    damp = low[:, first : first + count]
-                    damping(0, first, count, damp, scratch(count))
-                    sig = keep.tile([P, count], F32, name=f"sig_first{first}")
+                    sig = stretch(-1, first, count)
                 else:
-                    damp = tenant([P, count], F32, "damp", f"fetch{FETCH_RING - 1}")[:]
-                    damping(0, first, count, damp, scratch(count))
-                    second_bf = tenant([P, P * PACK], BF16, "second_bf", "first_rest")
-                    nc.scalar.activation(*interleaved(second_bf[:], w1_second[:]), ACT.Copy)
-                    made["w1_second"] = quantised("w1_tile1", second_bf, P)
-                    sig = tenant([P, count], F32, "sig_first", "first_rest")
-                nc.vector.tensor_tensor(sig[:], first_sum("a", w1_operand(0), first, count), damp, ALU.mult)
-                scatter(0, first, count, sig[:])
+                    cast_w1("w1_early", "first_rest")
+                    side_work("w1_early")
+                    sig = tenant([P, count], F32, "sig_first", "first_rest")[:]
+                a_ps = first_sum("a_own", w1_operand(0), first, count)
+                nc.vector.tensor_tensor(sig, a_ps, damp, ALU.mult)
+                scatter(0, first, count, sig)
 
-        def damping_share(i):
-            damp_share = tenant([P, HALF], F32, "damp_share", SIDE_WITH.get(i, f"damp_share{i % 2}"))
-            damping(i, HALF, HALF, damp_share[:], scratch(HALF))
-            return damp_share
+        def parts(r, k):
+            own = S - ROUNDS[r][1]
+            if k == 0:
+                return 0, slice(0, own), slice(own, HALF)
+            return 1, slice(HALF - own, HALF), slice(0, HALF - own)
 
-        def signatures(i, damp_share):
-            if i == W3_LOAD_AFTER:
-                damp = tenant([P, HALF], F32, "damp", "table")
-            else:
-                damp = ring.tile([P, HALF], F32, name="damp", tag="damp", bufs=2)
-            square = tenant([P, HALF], F32, "square", f"fetch{(i - 1) % FETCH_RING}")
-            damping(i, 0, HALF, damp[:], square[:])
-            sig = ring.tile([P, S], F32, name="sig", tag="sig", bufs=2)
-            a_low = first_sum("a", w1_operand(i), 0, HALF)
-            a_high = first_sum("a", w1_operand(i), HALF, HALF)
-            a_share = tenant([P, HALF], F32, "a_share", f"fetch{i % FETCH_RING}")
-            nc.scalar.copy(a_share[:], a_high)
-            nc.gpsimd.tensor_tensor(sig[:, HALF:S], a_share[:], damp_share[:], ALU.mult)
-            nc.vector.tensor_tensor(sig[:, 0:HALF], a_low, damp[:], ALU.mult)
-            if i == W3_LOAD_AFTER:
-                load_w3("table")
-            return sig
+        def shared(r, k, half, cols):
+            first = k * S + half * HALF - (S - ROUNDS[r][1])
+            return slice(first + cols.start, first + cols.stop)
 
-        def negate_margin(i):
+        gathered = keep.tile([P, 2 * M_OUT], F32, name="gathered")
+
+        def rest_damping(r, k, damp_share, square):
+            half, own, rest = parts(r, k)
+            squared(ROUNDS[r][0][k], half * HALF, HALF, square)
+            if rest.start < rest.stop:
+                damping(damp_share[:, shared(r, k, half, rest)], square[:, rest])
+            return square[:, own]
+
+        def dampings(r):
+            tiles, share, side = ROUNDS[r]
+            damp_share = tenant([P, len(tiles) * share], F32, "damp_share", side)
+            damp = []
+            for k, i in enumerate(tiles):
+                if i != tiles[-1]:
+                    damp.append(ring.tile([P, HALF], F32, name="damp", tag="damp", bufs=2)[:, 0 : S - share])
+                    damping(damp[k], rest_damping(r, k, damp_share, scratch(HALF)))
+                other = 1 - parts(r, k)[0]
+                square = squared(i, other * HALF, HALF, scratch(HALF))
+                damping(damp_share[:, shared(r, k, other, slice(0, HALF))], square)
+            return damp, damp_share
+
+        def signatures(r, damp, damp_share):
+            tiles, share, side = ROUNDS[r]
+            count = len(tiles)
+            own = parts(r, count - 1)[1]
+            across = M_OUT - (own.start + own.stop) // 2
+            square = rest_damping(r, count - 1, damp_share, gathered[:, across : across + HALF])
+            end = S - ROUNDS[r - 1][1] if r > 0 else HALF
+            a_share = stretch(r - 1, end - share * count, share * count)
+            a_own = []
+            for k, i in enumerate(tiles):
+                half, own, rest = parts(r, k)
+                bank = first_sum("a_own", w1_operand(i), half * HALF, HALF)
+                a_own.append(bank[:, own])
+                other = first_sum("a_share", w1_operand(i), (1 - half) * HALF, HALF)
+                nc.scalar.copy(a_share[:, shared(r, k, 1 - half, slice(0, HALF))], other)
+                if rest.start < rest.stop:
+                    nc.scalar.copy(a_share[:, shared(r, k, half, rest)], bank[:, rest])
+            nc.gpsimd.tensor_tensor(stretch(r, S - share, share * count), a_share, damp_share[:], ALU.mult)
+            damp.append(stretch(r - 1, end, S - share) if r > 0 else stretch(0, -HALF, HALF))
+            damping(damp[-1], square)
+            for k in range(count):
+                half, own, rest = parts(r, k)
+                sig = stretch(r, k * S + half * HALF + own.start, S - share)
+                nc.vector.tensor_tensor(sig, a_own[k], damp[k], ALU.mult)
+
+        def negated_margin(i):
             g, t = divmod(i, PACK)
-            negated[i] = ring.tile([P, M_OUT], F32, name="negated", tag="negated", bufs=2)
-            nc.scalar.activation(negated[i][:], margins[g][:, t, :], ACT.Copy, scale=-1.0)
+            negated = ring.tile([P, M_OUT], F32, name="negated", tag="negated", bufs=2)
+            nc.scalar.activation(negated[:], margins[g][:, t, :], ACT.Copy, scale=-1.0)
+            return negated
 
         def exceed(i, blocks, terms):
             g, t = divmod(i, PACK)
             count = blocks.stop - blocks.start
-            bank = psum.tile([P, count * P], F32, name="turn_ps", tag="turn", bufs=2)
+            bank = psum.tile([P, count * P], F32, name="turn_ps", tag="turn", bufs=BANKS["turn"])
             for k in range(count):
                 cols = slice((blocks.start + k) * P, (blocks.start + k + 1) * P)
                 for n, rows in enumerate(terms):
@@ -324,18 +334,22 @@ def tile_list_phishing_verdict_slots_kernel(
                         stop=(n == len(terms) - 1),
                         is_transpose=True,
                     )
-            nc.scalar.activation(
-                turned[g][:, blocks, t * P : (t + 1) * P], bank[:].rearrange("p (k r) -> p k r", k=count), ACT.Relu
-            )
+            words = turned[g][:].rearrange("p k (u w e) -> p k u w e", u=2, e=2)[:, blocks, :, QUAD * t : QUAD * (t + 1), :]
+            rows = bank[:].rearrange("p (k q u e) -> p k u q e", k=count, u=2, e=2)
+            if count == 1:
+                nc.scalar.activation(words[:, 0], rows[:, 0], ACT.Relu)
+            else:
+                for u in range(2):
+                    nc.scalar.activation(words[:, :, u], rows[:, :, u], ACT.Relu)
 
         def turn_back(g, blocks, z_bf, on_vector):
             count = blocks.stop - blocks.start
-            bank = psum.tile([P, count * 2 * P], F32, name="back_ps", tag="back", bufs=2)
+            bank = psum.tile([P, count * 2 * P], F32, name="back_ps", tag="back", bufs=BANKS["back"])
             for k in range(count):
                 pairs = turned[g][:, blocks.start + k, :].bitcast(F32)
                 for u in range(2):
                     nc.tensor.transpose(
-                        bank[:, (2 * k + u) * P : (2 * k + u + 1) * P], pairs[:, u : 2 * P : 2], identity[:]
+                        bank[:, (2 * k + u) * P : (2 * k + u + 1) * P], pairs[:, u * P : (u + 1) * P], identity[:]
                     )
             dst = z_bf.bitcast(F32).rearrange("p (k m u) -> p k m u", k=count, u=2)
             src = bank[:].rearrange("p (k u m) -> p k m u", k=count, u=2)
@@ -344,17 +358,15 @@ def tile_list_phishing_verdict_slots_kernel(
             else:
                 nc.scalar.copy(dst, src)
 
-        def finish_tile(i):
+        def finish_tile(i, fetched):
             g, t = divmod(i, PACK)
             every = slice(0, BLOCKS)
             if t == 0:
-                turned[g] = tenant([P, BLOCKS, R_PASS], BF16, "turned", f"z{g}")
-            fetched[i] = tenant([P, M_OUT], F32, "fetched", f"fetch{i % FETCH_RING}")
-            nc.vector.tensor_copy(fetched[i][:], pages[i % 2][:].indirect(idx3[:]))
-            negate_margin(i)
-            exceed(i, every, (negated[i], fetched[i]))
+                turned[g] = tenant([P, BLOCKS, R_PASS], BF16, "turned", f"turned{g % 2}")
+            nc.vector.tensor_copy(fetched, pages[i % 2][:].indirect(idx3[:]))
+            exceed(i, every, (negated_margin(i), fetched))
             if t == PACK - 1:
-                z_bf = tenant([P, M_OUT * PACK], BF16, "z_bf", "z_bf")
+                z_bf = tenant([P, M_OUT * PACK], BF16, "z_bf", f"z_bf{g}")
                 for first in range(0, BLOCKS, 2):
                     part = z_bf[:, first * P * PACK : (first + 2) * P * PACK]
                     turn_back(g, slice(first, first + 2), part, on_vector=False)
@@ -362,11 +374,13 @@ def tile_list_phishing_verdict_slots_kernel(
 
         def score(g, bank, z_codes, z_scale):
             for k in range(N_OUT // P):
-                w3_codes, w3_scale = w3_operand(g * N_OUT + k * P)
+                w3_codes, w3_scales = quants["w3_last" if g == LAST else "w3"]
+                first = k * P if g == LAST else g * N_OUT + k * P
+                cols = slice(first, first + P)
                 nc.tensor.matmul_mx(
                     out=bank[:, k * P : (k + 1) * P],
-                    lhsT=w3_codes,
-                    lhsT_scale=w3_scale,
+                    lhsT=w3_codes[:, cols].bitcast(FP8X4),
+                    lhsT_scale=w3_scales[:, cols],
                     rhs=z_codes.bitcast(FP8X4),
                     rhs_scale=z_scale,
                     start=(g == 0 and k == 0),
@@ -375,47 +389,55 @@ def tile_list_phishing_verdict_slots_kernel(
 
         def finish():
             i = TILES - 1
-            banks = [psum.tile([P, N_OUT], F32, name="out_ps", tag="ba"[b % 2], bufs=2) for b in range(BLOCKS)]
+            tags = ("b", "a_share", "a_own", "a_own")
+            banks = [psum.tile([P, N_OUT], F32, name="out_ps", tag=tag, bufs=BANKS[tag]) for tag in tags]
             for g in range(LAST):
-                codes, scales = z_q[g]
+                codes, scales = quants[f"z{g}"]
                 for b in range(BLOCKS):
                     score(g, banks[b], codes[:, b * P : (b + 1) * P], scales[:, b * P : (b + 1) * P])
-            fetched[i] = tenant([P, M_OUT], F32, "fetched", f"fetch{(i - 1) % FETCH_RING}")
+            fetched = gathered[:, 0:M_OUT]
             for b in range(BLOCKS):
                 cols = slice(b * P, (b + 1) * P)
                 nc.vector.tensor_tensor(
-                    fetched[i][:, cols],
+                    fetched[:, cols],
                     pages[i % 2][:].indirect(entries(idx3, cols.start, P)),
                     margins[LAST][:, PACK - 1, cols],
                     ALU.subtract,
                 )
-                exceed(i, slice(b, b + 1), (fetched[i],))
+                exceed(i, slice(b, b + 1), (fetched,))
+            quants["w3_last"] = quantised("w3_last", casts["w3_last"], N_OUT, f"margin{LAST}")
             for b in range(BLOCKS):
                 z_bf = keep.tile([P, P * PACK], BF16, name=f"z_last{b}", align_bytes=ALIGN)
-                turn_back(LAST, slice(b, b + 1), z_bf[:], on_vector=True)
+                turn_back(LAST, slice(b, b + 1), z_bf[:], on_vector=(b != 1))
                 codes, scales = quantised(f"z_last{b}", z_bf, P)
                 score(LAST, banks[b], codes[:], scales[:])
             for b in range(BLOCKS):
-                result = keep.tile([P, N_OUT], F32, name=f"result{b}")
-                nc.scalar.copy(result[:], banks[b][:])
+                result = tenant([P, N_OUT], F32, "result", ("table", "scale_rows", "first_rest", "page_odd")[b])
+                if b == BLOCKS - 1:
+                    nc.vector.tensor_copy(result[:], banks[b][:])
+                else:
+                    nc.scalar.copy(result[:], banks[b][:])
                 nc.sync.dma_start(
                     out[:, b * P : (b + 1) * P].rearrange("(k p) m -> p k m", p=P),
                     result[:].rearrange("p (k m) -> p k m", m=P),
                 )
 
         first_tile()
-        ahead = damping_share(1)
-        for i in range(1, TILES):
-            sig = signatures(i, ahead)
-            if i + 1 < TILES:
-                ahead = damping_share(i + 1)
-            if i <= PASSES:
-                cast_w1(i - 1)
-            if i == PACK:
-                for words in W3_PARTS:
-                    cast_w3(words)
-            finish_tile(i - 1)
-            if i in SIDE_WITH:
-                side_work[SIDE_WITH[i]](SIDE_WITH[i])
-            scatter(i, 0, S, sig[:])
+        before = (0,)
+        ahead = dampings(0)
+        cast_w1(ROUNDS[0][2], "cast0")
+        for r, (tiles, share, side) in enumerate(ROUNDS):
+            signatures(r, *ahead)
+            if r + 1 < len(ROUNDS):
+                ahead = dampings(r + 1)
+                if ROUNDS[r + 1][2] in W1_PARTS:
+                    cast_w1(ROUNDS[r + 1][2], f"cast{r + 1}")
+            if 1 <= r <= PASSES:
+                cast_w3(r - 1)
+            for k, i in enumerate(before):
+                finish_tile(i, gathered[:, k * M_OUT : (k + 1) * M_OUT])
+            side_work(side)
+            for k, i in enumerate(tiles):
+                scatter(i, 0, S, stretch(r, k * S, S))
+            before = tiles
         finish()

@@ -43,7 +43,7 @@ ROUNDS = (
     ((11,), 896, "z1"),
 )
 SPARE = 896
-W1_PARTS = {"w1_tile0": (0, 1), "w1_early": (1, 3), "w1_second": (3, 5), "w1_third": (5, 9), "w1_last": (9, 12)}
+W1_PARTS = {"w1_tile0": (0, 1), "w1_early": (1, 3), "w1_second": (3, 5), "w1_third": (5, 8), "w1_last": (8, 12)}
 BANKS = {"a_own": 2, "a_share": 1, "b": 1, "turn": 2, "back": 2}
 BLOCKS = M_OUT // P
 
@@ -75,7 +75,7 @@ def tile_list_phishing_verdict_slots_kernel(
 
         def load_w1(part):
             first, stop = W1_PARTS[part]
-            w1_raw[part] = keep.tile([P, PACK, (stop - first) * P], F32, name=part + "_raw")
+            w1_raw[part] = tenant([P, PACK, (stop - first) * P], F32, "w1_raw", part + "_raw")
             nc.sync.dma_start(w1_raw[part][:], w1[:, first * P : stop * P].rearrange("(p j) c -> p j c", j=PACK))
 
         def load_w2_words(g):
@@ -83,8 +83,9 @@ def tile_list_phishing_verdict_slots_kernel(
             nc.sync.dma_start(words[:].bitcast(I32), w2_words[0, :, 2 * g * R_PASS : 2 * (g + 1) * R_PASS].bitcast(I32))
             return words
 
-        def quantised(name, grouped, width, tag=None):
-            codes = tenant([P, width], U32, name + "_codes", tag or name)
+        def quantised(name, grouped, width, tag=None, codes=None):
+            if codes is None:
+                codes = tenant([P, width], U32, name + "_codes", tag or name)
             scales = keep.tile([P, width], U8, name=name + "_scales", align_bytes=ALIGN)
             done = 0
             while done < width:
@@ -115,6 +116,7 @@ def tile_list_phishing_verdict_slots_kernel(
         nc.sync.dma_start(tab_w[:], tab_words[0].rearrange("p t i -> p (t i)").bitcast(I32))
         w2_w = {0: load_w2_words(0)}
         w2_s = keep.tile([P, H], U8, name="w2_s", align_bytes=ALIGN)
+        nc.gpsimd.memset(w2_s[:].bitcast(I32), 0)
         load_scale_rows(w2_s, w2_scales[0])
         weights = keep.tile([P, S], F32, name="weights")
         first_count = FIRST_PIECES[0][1]
@@ -128,16 +130,15 @@ def tile_list_phishing_verdict_slots_kernel(
 
         def load_margin(g):
             margins[g] = tenant([P, PACK, M_OUT], F32, "margin", f"margin{g}")
-            nc.sync.dma_start(
-                margins[g][:], margin[g * R_PASS : (g + 1) * R_PASS, :].rearrange("(t p) m -> p t m", t=PACK)
-            )
+            order = "(p t) m -> p t m" if g == LAST else "(t p) m -> p t m"
+            nc.sync.dma_start(margins[g][:], margin[g * R_PASS : (g + 1) * R_PASS, :].rearrange(order, t=PACK))
 
         load_w1("w1_second")
         w2_w[1] = load_w2_words(1)
         load_margin(0)
         load_w1("w1_third")
-        load_w1("w1_last")
         w2_w[LAST] = load_w2_words(LAST)
+        load_w1("w1_last")
         load_margin(1)
         load_margin(LAST)
 
@@ -167,27 +168,58 @@ def tile_list_phishing_verdict_slots_kernel(
 
         casts = {}
         quants = {}
+        dealt = {}
         turned = {}
 
         def cast_w1(part, tag):
             bf = tenant([P, w1_raw[part].shape[2] * PACK], BF16, part + "_bf", tag)
-            nc.scalar.activation(*interleaved(bf[:], w1_raw[part][:]), ACT.Copy)
+            if part == "w1_last":
+                dst = bf[:].rearrange("p (t u j) -> p u t j", t=PACK, j=PACK)
+                rows = w1_raw[part][:].rearrange("p j (u t) -> p u t j", t=PACK)
+            else:
+                dst, rows = interleaved(bf[:], w1_raw[part][:])
+            nc.scalar.activation(dst, rows, ACT.Copy)
             casts[part] = bf
+
+        def load_last_weights(tag):
+            weights_last = tenant([P, PACK, S], F32, "weights_last", tag)
+            for q in range(QUADS):
+                nc.sync.dma_start(
+                    weights_last[QUAD * q : QUAD * (q + 1), :, :], wgs.rearrange("(u t) j -> u t j", t=PACK)
+                )
+            dealt["weights"] = weights_last
+
+        def reorder_w2(words, scales):
+            nc.vector.tensor_copy(
+                words.bitcast(U16).rearrange("p (t u) -> p t u", t=PACK),
+                w2_w[LAST][:].bitcast(U16).rearrange("p (u t) -> p t u", t=PACK),
+            )
+            nc.vector.tensor_copy(
+                scales.rearrange("p (t u) -> p t u", t=PACK),
+                w2_s[:, LAST * R_PASS : H].rearrange("p (u t) -> p t u", t=PACK),
+            )
+            dealt["w2"] = (words, scales)
 
         w3_raw = tenant([P, PASSES, PACK, N_OUT], F32, "w3_raw", "table")
         for g in range(PASSES):
             nc.sync.dma_start(
                 w3_raw[:, g, :, :], w3[g * R_PASS : (g + 1) * R_PASS, :].rearrange("(p j) n -> p j n", j=PACK)
             )
-        casts["w3"] = keep.tile([P, LAST * N_OUT * PACK], BF16, name="w3_bf", align_bytes=ALIGN)
-        casts["w3_last"] = keep.tile([P, N_OUT * PACK], BF16, name="w3_last_bf", align_bytes=ALIGN)
+        casts["w3"] = keep.tile([P, PASSES * N_OUT * PACK], BF16, name="w3_bf", align_bytes=ALIGN)
 
         def cast_w3(g):
-            part = casts["w3_last"][:] if g == LAST else casts["w3"][:, g * N_OUT * PACK : (g + 1) * N_OUT * PACK]
+            part = casts["w3"][:, g * N_OUT * PACK : (g + 1) * N_OUT * PACK]
             nc.scalar.activation(*interleaved(part, w3_raw[:, g, :, :]), ACT.Copy)
 
         def side_work(name):
-            made = quantised(name, casts[name], casts[name].shape[1] // PACK)
+            width = casts[name].shape[1] // PACK
+            if name == "w1_third":
+                both = tenant([P, 4 * width + 3 * R_PASS], U8, "both", name)
+                made = quantised(name, casts[name], width, codes=both[:, 0 : 4 * width].bitcast(U32))
+                words, scales = 4 * width, 4 * width + 2 * R_PASS
+                reorder_w2(both[:, words:scales], both[:, scales : scales + R_PASS])
+            else:
+                made = quantised(name, casts[name], width)
             if name in W1_PARTS:
                 w1_q[name] = made
             else:
@@ -201,7 +233,8 @@ def tile_list_phishing_verdict_slots_kernel(
 
         def w2_operand(i):
             g, t = divmod(i, PACK)
-            return w2_w[g][:, 2 * t * P : 2 * (t + 1) * P].bitcast(FP4X4), w2_s[:, i * P : (i + 1) * P]
+            words, scales = dealt["w2"] if g == LAST else (w2_w[g], w2_s[:, g * R_PASS : (g + 1) * R_PASS])
+            return words[:, 2 * t * P : 2 * (t + 1) * P].bitcast(FP4X4), scales[:, t * P : (t + 1) * P]
 
         def first_sum(tag, operand, first, count):
             codes, scale = operand
@@ -231,8 +264,10 @@ def tile_list_phishing_verdict_slots_kernel(
             nc.scalar.activation(dst, square, ACT.Exp, scale=-1.0)
 
         def scatter(i, first, count, sig):
+            g, t = divmod(i, PACK)
+            weight = dealt["weights"][:, t, :] if g == LAST else weights[:]
             nc.vector.tensor_tensor(
-                pages[i % 2][:].indirect(entries(idx2, first, count)), sig, weights[:, first : first + count], ALU.mult
+                pages[i % 2][:].indirect(entries(idx2, first, count)), sig, weight[:, first : first + count], ALU.mult
             )
 
         stretches = keep.tile([P, 2 * (SPARE + 2 * S)], F32, name="stretches")
@@ -319,68 +354,59 @@ def tile_list_phishing_verdict_slots_kernel(
             nc.scalar.activation(negated[:], margins[g][:, t, :], ACT.Copy, scale=-1.0)
             return negated
 
-        def exceed(i, blocks, terms):
-            g, t = divmod(i, PACK)
-            count = blocks.stop - blocks.start
-            bank = psum.tile([P, count * P], F32, name="turn_ps", tag="turn", bufs=BANKS["turn"])
-            for k in range(count):
-                cols = slice((blocks.start + k) * P, (blocks.start + k + 1) * P)
+        def turn(terms, tag):
+            bank = psum.tile([P, M_OUT], F32, name="turn_ps", tag=tag, bufs=BANKS[tag])
+            for k in range(BLOCKS):
+                cols = slice(k * P, (k + 1) * P)
                 for n, rows in enumerate(terms):
                     nc.tensor.matmul(
-                        bank[:, k * P : (k + 1) * P],
+                        bank[:, cols],
                         lhsT=rows[:, cols],
                         rhs=identity[:],
                         start=(n == 0),
                         stop=(n == len(terms) - 1),
                         is_transpose=True,
                     )
-            words = turned[g][:].rearrange("p k (u w e) -> p k u w e", u=2, e=2)[:, blocks, :, QUAD * t : QUAD * (t + 1), :]
-            rows = bank[:].rearrange("p (k q u e) -> p k u q e", k=count, u=2, e=2)
-            if count == 1:
-                nc.scalar.activation(words[:, 0], rows[:, 0], ACT.Relu)
-            else:
-                for u in range(2):
-                    nc.scalar.activation(words[:, :, u], rows[:, :, u], ACT.Relu)
+            return bank
 
-        def turn_back(g, blocks, z_bf, on_vector):
-            count = blocks.stop - blocks.start
-            bank = psum.tile([P, count * 2 * P], F32, name="back_ps", tag="back", bufs=BANKS["back"])
-            for k in range(count):
-                pairs = turned[g][:, blocks.start + k, :].bitcast(F32)
-                for u in range(2):
-                    nc.tensor.transpose(
-                        bank[:, (2 * k + u) * P : (2 * k + u + 1) * P], pairs[:, u * P : (u + 1) * P], identity[:]
-                    )
-            dst = z_bf.bitcast(F32).rearrange("p (k m u) -> p k m u", k=count, u=2)
-            src = bank[:].rearrange("p (k u m) -> p k m u", k=count, u=2)
-            if on_vector:
-                nc.vector.tensor_copy(dst, src)
-            else:
-                nc.scalar.copy(dst, src)
+        def turn_back(g):
+            z_bf = tenant([P, M_OUT * PACK], BF16, "z_bf", f"z_bf{g}")
+            pairs = turned[g][:].bitcast(F32)
+            for half in range(2):
+                bank = turn((pairs[:, half * M_OUT : (half + 1) * M_OUT],), "back")
+                nc.scalar.copy(
+                    z_bf[:].bitcast(F32)[:, half * M_OUT : (half + 1) * M_OUT].rearrange("p (k m u) -> p k m u", k=2, u=2),
+                    bank[:].rearrange("p (k u m) -> p k m u", k=2, u=2),
+                )
+            casts[f"z{g}"] = z_bf
 
         def finish_tile(i, fetched):
             g, t = divmod(i, PACK)
-            every = slice(0, BLOCKS)
-            if t == 0:
-                turned[g] = tenant([P, BLOCKS, R_PASS], BF16, "turned", f"turned{g % 2}")
             nc.vector.tensor_copy(fetched, pages[i % 2][:].indirect(idx3[:]))
-            exceed(i, every, (negated_margin(i), fetched))
+            bank = turn((negated_margin(i), fetched), "turn")
+            if g == LAST:
+                if t == 0:
+                    dealt["diffs"] = tenant([P, PACK, M_OUT], F32, "diffs", "margin0")
+                across = tenant([P, M_OUT], F32, "across", "turned0")
+                nc.scalar.copy(across[:], bank[:])
+                nc.scalar.copy(dealt["diffs"][:, t, :], turn((across,), "back")[:])
+                return
+            if t == 0:
+                turned[g] = tenant([P, BLOCKS * R_PASS], BF16, "turned", f"turned{g}")
+            words = turned[g][:].rearrange("p (k u w e) -> p k u w e", k=BLOCKS, u=2, e=2)
+            rows = bank[:].rearrange("p (k q u e) -> p k u q e", k=BLOCKS, u=2, e=2)
+            for u in range(2):
+                nc.scalar.activation(words[:, :, u, QUAD * t : QUAD * (t + 1), :], rows[:, :, u], ACT.Relu)
             if t == PACK - 1:
-                z_bf = tenant([P, M_OUT * PACK], BF16, "z_bf", f"z_bf{g}")
-                for first in range(0, BLOCKS, 2):
-                    part = z_bf[:, first * P * PACK : (first + 2) * P * PACK]
-                    turn_back(g, slice(first, first + 2), part, on_vector=False)
-                casts[f"z{g}"] = z_bf
+                turn_back(g)
 
         def score(g, bank, z_codes, z_scale):
             for k in range(N_OUT // P):
-                w3_codes, w3_scales = quants["w3_last" if g == LAST else "w3"]
-                first = k * P if g == LAST else g * N_OUT + k * P
-                cols = slice(first, first + P)
+                cols = slice(g * N_OUT + k * P, g * N_OUT + (k + 1) * P)
                 nc.tensor.matmul_mx(
                     out=bank[:, k * P : (k + 1) * P],
-                    lhsT=w3_codes[:, cols].bitcast(FP8X4),
-                    lhsT_scale=w3_scales[:, cols],
+                    lhsT=quants["w3"][0][:, cols].bitcast(FP8X4),
+                    lhsT_scale=quants["w3"][1][:, cols],
                     rhs=z_codes.bitcast(FP8X4),
                     rhs_scale=z_scale,
                     start=(g == 0 and k == 0),
@@ -395,25 +421,32 @@ def tile_list_phishing_verdict_slots_kernel(
                 codes, scales = quants[f"z{g}"]
                 for b in range(BLOCKS):
                     score(g, banks[b], codes[:, b * P : (b + 1) * P], scales[:, b * P : (b + 1) * P])
-            fetched = gathered[:, 0:M_OUT]
-            for b in range(BLOCKS):
-                cols = slice(b * P, (b + 1) * P)
+            rows = dealt["diffs"]
+            blocks = [slice(b * P, (b + 1) * P) for b in range(BLOCKS)]
+            z_bf = [keep.tile([P, P * PACK], BF16, name=f"z_last{b}", align_bytes=ALIGN) for b in range(BLOCKS)]
+            for b, cols in enumerate(blocks):
                 nc.vector.tensor_tensor(
-                    fetched[:, cols],
+                    rows[:, PACK - 1, cols],
                     pages[i % 2][:].indirect(entries(idx3, cols.start, P)),
                     margins[LAST][:, PACK - 1, cols],
                     ALU.subtract,
                 )
-                exceed(i, slice(b, b + 1), (fetched,))
-            quants["w3_last"] = quantised("w3_last", casts["w3_last"], N_OUT, f"margin{LAST}")
-            for b in range(BLOCKS):
-                z_bf = keep.tile([P, P * PACK], BF16, name=f"z_last{b}", align_bytes=ALIGN)
-                turn_back(LAST, slice(b, b + 1), z_bf[:], on_vector=(b != 1))
-                codes, scales = quantised(f"z_last{b}", z_bf, P)
+                if b < BLOCKS // 2:
+                    nc.scalar.activation(*interleaved(z_bf[b][:], rows[:, :, cols]), ACT.Relu)
+
+            def close(b):
+                codes, scales = quantised(f"z_last{b}", z_bf[b], P)
                 score(LAST, banks[b], codes[:], scales[:])
+
+            for b in range(BLOCKS // 2):
+                later = b + BLOCKS // 2
+                nc.vector.tensor_scalar_max(*interleaved(z_bf[later][:], rows[:, :, blocks[later]]), 0.0)
+                close(b)
+            for b in range(BLOCKS // 2, BLOCKS):
+                close(b)
             for b in range(BLOCKS):
                 result = tenant([P, N_OUT], F32, "result", ("table", "scale_rows", "first_rest", "page_odd")[b])
-                if b == BLOCKS - 1:
+                if b % 2 == 1:
                     nc.vector.tensor_copy(result[:], banks[b][:])
                 else:
                     nc.scalar.copy(result[:], banks[b][:])
@@ -432,6 +465,8 @@ def tile_list_phishing_verdict_slots_kernel(
                 ahead = dampings(r + 1)
                 if ROUNDS[r + 1][2] in W1_PARTS:
                     cast_w1(ROUNDS[r + 1][2], f"cast{r + 1}")
+            if r == 1:
+                load_last_weights("w1_third_raw")
             if 1 <= r <= PASSES:
                 cast_w3(r - 1)
             for k, i in enumerate(before):

@@ -36,13 +36,13 @@ FIRST_PIECES = ((0, 256), (256, 256), (512, 512))
 
 ROUNDS = (
     ((1, 2), 512, "w1_second"),
-    ((3, 4), 640, "w1_third"),
-    ((5, 6), 640, "w1_last"),
-    ((7, 8), 640, "z0"),
-    ((9, 10), 640, "w3"),
+    ((3, 4), 704, "w1_third"),
+    ((5, 6), 704, "w1_last"),
+    ((7, 8), 704, "z0"),
+    ((9, 10), 704, "w3"),
     ((11,), 896, "z1"),
 )
-SPARE = 896
+SPARE = 1088
 W1_PARTS = {"w1_tile0": (0, 1), "w1_early": (1, 3), "w1_second": (3, 5), "w1_third": (5, 8), "w1_last": (8, 12)}
 BANKS = {"a_own": 2, "a_share": 1, "b": 1, "turn": 2, "back": 2}
 BLOCKS = M_OUT // P
@@ -387,7 +387,7 @@ def tile_list_phishing_verdict_slots_kernel(
             if g == LAST:
                 if t == 0:
                     dealt["diffs"] = tenant([P, PACK, M_OUT], F32, "diffs", "margin0")
-                across = tenant([P, M_OUT], F32, "across", "turned0")
+                across = tenant([P, M_OUT], F32, "across", f"turned{t % 2}")
                 nc.scalar.copy(across[:], bank[:])
                 nc.scalar.copy(dealt["diffs"][:, t, :], turn((across,), "back")[:])
                 return

@@ -312,7 +312,7 @@ def tile_list_phishing_verdict_slots_kernel(
 
         def dampings(r):
             tiles, share, side = ROUNDS[r]
-            damp_share = tenant([P, len(tiles) * share], F32, "damp_share", side)
+            damp_share = ring.tile([P, len(tiles) * share], F32, name="damp_share", tag="damp_share", bufs=2)
             damp = []
             for k, i in enumerate(tiles):
                 if i != tiles[-1]:
@@ -326,9 +326,20 @@ def tile_list_phishing_verdict_slots_kernel(
         def signatures(r, damp, damp_share):
             tiles, share, side = ROUNDS[r]
             count = len(tiles)
-            own = parts(r, count - 1)[1]
-            across = M_OUT - (own.start + own.stop) // 2
-            square = rest_damping(r, count - 1, damp_share, gathered[:, across : across + HALF])
+            half, own, rest = parts(r, count - 1)
+            outer = (S - share) // 2
+            apart = slice(HALF - outer, HALF) if half else slice(0, outer)
+            others = slice(0, HALF - outer) if half else slice(outer, HALF)
+            inner = slice(own.start, apart.start) if half else slice(apart.stop, own.stop)
+            across = M_OUT - (inner.start + inner.stop) // 2
+            square = gathered[:, across : across + HALF]
+            square_apart = tenant([P, outer], F32, "square_apart", side)
+            b_ps = first_sum("b", w2_operand(tiles[-1]), half * HALF, HALF)
+            nc.scalar.activation(square[:, others], b_ps[:, others], ACT.Square)
+            nc.scalar.activation(square_apart[:], b_ps[:, apart], ACT.Square)
+            if rest.start < rest.stop:
+                damping(damp_share[:, shared(r, count - 1, half, rest)], square[:, rest])
+            late = ((inner.start - own.start, square[:, inner]), (apart.start - own.start, square_apart[:]))
             end = S - ROUNDS[r - 1][1] if r > 0 else HALF
             a_share = stretch(r - 1, end - share * count, share * count)
             a_own = []
@@ -342,7 +353,8 @@ def tile_list_phishing_verdict_slots_kernel(
                     nc.scalar.copy(a_share[:, shared(r, k, half, rest)], bank[:, rest])
             nc.gpsimd.tensor_tensor(stretch(r, S - share, share * count), a_share, damp_share[:], ALU.mult)
             damp.append(stretch(r - 1, end, S - share) if r > 0 else stretch(0, -HALF, HALF))
-            damping(damp[-1], square)
+            for first, part in late:
+                damping(damp[-1][:, first : first + outer], part)
             for k in range(count):
                 half, own, rest = parts(r, k)
                 sig = stretch(r, k * S + half * HALF + own.start, S - share)

@@ -26,6 +26,7 @@ R_PASS = P * PACK
 PASSES = H // R_PASS
 LAST = PASSES - 1
 TILES = H // P
+SCALE_ROWS = R_PASS // QUAD
 HALF = 512
 ALIGN = 64
 QUANT_WORDS = (128, 256, 512, 1024)
@@ -64,8 +65,8 @@ def tile_list_phishing_verdict_slots_kernel(
         def entries(offsets, first, count):
             return offsets[:, first // PER_COLUMN : (first + count) // PER_COLUMN]
 
-        def load_scale_rows(scale_tile, rows):
-            for q in range(QUADS):
+        def load_scale_rows(scale_tile, rows, quads=range(QUADS)):
+            for q in quads:
                 nc.sync.dma_start(
                     scale_tile[QUAD * q : QUAD * q + PACK, :].bitcast(I32),
                     rows[PACK * q : PACK * (q + 1), :].bitcast(I32),
@@ -73,14 +74,14 @@ def tile_list_phishing_verdict_slots_kernel(
 
         w1_raw = {}
 
-        def load_w1(part):
+        def load_w1(part, tag):
             first, stop = W1_PARTS[part]
-            w1_raw[part] = tenant([P, PACK, (stop - first) * P], F32, "w1_raw", part + "_raw")
+            w1_raw[part] = tenant([P, PACK, (stop - first) * P], F32, "w1_raw", tag)
             nc.sync.dma_start(w1_raw[part][:], w1[:, first * P : stop * P].rearrange("(p j) c -> p j c", j=PACK))
 
-        def load_w2_words(g):
-            words = keep.tile([P, 2 * R_PASS], U8, name=f"w2_w{g}", align_bytes=ALIGN)
-            nc.sync.dma_start(words[:].bitcast(I32), w2_words[0, :, 2 * g * R_PASS : 2 * (g + 1) * R_PASS].bitcast(I32))
+        def load_w2_words(first, stop, tag):
+            words = tenant([P, 2 * (stop - first)], U8, "w2_w", tag)
+            nc.sync.dma_start(words[:].bitcast(I32), w2_words[0, :, 2 * first : 2 * stop].bitcast(I32))
             return words
 
         def quantised(name, grouped, width, tag=None, codes=None):
@@ -108,60 +109,58 @@ def tile_list_phishing_verdict_slots_kernel(
         idx2 = lists.tile([P, S // PER_COLUMN], U16, name="idx2")
         idx3 = lists.tile([P, M_OUT // PER_COLUMN], U16, name="idx3")
 
-        tab_scale_rows = tenant([P, T], U8, "tab_scale_rows", "scale_rows")
-        load_scale_rows(tab_scale_rows, tab_scales[0])
+        tab_scale_rows = tenant([P, T], U8, "tab_scale_rows", "page_odd")
+        nc.sync.dma_start(tab_scale_rows[0:SCALE_ROWS, :].bitcast(I32), tab_scales[0].bitcast(I32))
         nc.sync.dma_start(idx[:], offs)
-        load_w1("w1_tile0")
+        nc.sync.dma_start(idx2[:], offs2)
+        nc.sync.dma_start(idx3[:], offs3)
+        w2_s_first = keep.tile([P, R_PASS], U8, name="w2_s_first", align_bytes=ALIGN)
+        load_scale_rows(w2_s_first, w2_scales[0, :, 0:R_PASS], range(QUADS - 1))
         tab_w = tenant([P, T], I32, "tab_w", "table")
         nc.sync.dma_start(tab_w[:], tab_words[0].rearrange("p t i -> p (t i)").bitcast(I32))
-        w2_w = {0: load_w2_words(0)}
-        w2_s = keep.tile([P, H], U8, name="w2_s", align_bytes=ALIGN)
-        nc.gpsimd.memset(w2_s[:].bitcast(I32), 0)
-        load_scale_rows(w2_s, w2_scales[0])
-        weights = keep.tile([P, S], F32, name="weights")
-        first_count = FIRST_PIECES[0][1]
-        nc.sync.dma_start(idx2[:], offs2)
-        nc.sync.dma_start(weights[:, 0:first_count], wgs[:, 0:first_count])
-        load_w1("w1_early")
-        nc.sync.dma_start(weights[:, first_count:S], wgs[:, first_count:S])
-        nc.sync.dma_start(idx3[:], offs3)
+        load_w1("w1_tile0", "w1_a")
+        load_scale_rows(w2_s_first, w2_scales[0, :, 0:R_PASS], range(QUADS - 1, QUADS))
+        w2_first = load_w2_words(0, R_PASS, "w2_first")
 
         margins = {}
 
-        def load_margin(g):
-            margins[g] = tenant([P, PACK, M_OUT], F32, "margin", f"margin{g}")
+        def load_margin(g, tag):
+            margins[g] = tenant([P, PACK, M_OUT], F32, "margin", tag)
             order = "(p t) m -> p t m" if g == LAST else "(t p) m -> p t m"
             nc.sync.dma_start(margins[g][:], margin[g * R_PASS : (g + 1) * R_PASS, :].rearrange(order, t=PACK))
 
-        load_w1("w1_second")
-        w2_w[1] = load_w2_words(1)
-        load_margin(0)
-        load_w1("w1_third")
-        w2_w[LAST] = load_w2_words(LAST)
-        load_w1("w1_last")
-        load_margin(1)
-        load_margin(LAST)
-
-        tab_s = keep.tile([P, T], U8, name="tab_s", align_bytes=ALIGN)
+        tab_s = tenant([P, T], U8, "tab_s", "window")
         nc.vector.memset(tab_s[:].bitcast(I32), 0)
         page_even = keep.tile([P, T2], F32, name="page_even")
         nc.vector.memset(page_even[:], 0.0)
-        for q in range(QUADS):
-            live = slice(QUAD * q, QUAD * q + PACK)
-            nc.vector.tensor_copy(tab_s[live, :].bitcast(I32), tab_scale_rows[live, :].bitcast(I32))
-
-        first_bf = tenant([P, P * PACK], BF16, "first_bf", "page_odd")
-        nc.scalar.activation(*interleaved(first_bf[:], w1_raw["w1_tile0"][:]), ACT.Copy)
-        w1_q = {"w1_tile0": quantised("w1_tile0", first_bf, P)}
+        nc.vector.tensor_copy(tab_s[0:SCALE_ROWS, :].bitcast(I32), tab_scale_rows[0:SCALE_ROWS, :].bitcast(I32))
         page_odd = tenant([P, T2], F32, "page_odd", "page_odd")
         nc.gpsimd.memset(page_odd[:], 0.0)
         pages = [page_even, page_odd]
 
-        v_s = [keep.tile([P, HALF], U8, name=f"v_s{h}", align_bytes=ALIGN) for h in range(S // HALF)]
+        picked_s = tenant([P, S], U8, "picked_s", "w1_b")
+        nc.vector.tensor_copy(picked_s[:], tab_s[:].indirect(idx[:]))
+        v_s = keep.tile([P, S], U8, name="v_s", align_bytes=ALIGN)
+        for q in range(QUADS):
+            nc.sync.dma_start(
+                v_s[QUAD * q : QUAD * q + PACK, :].bitcast(I32), picked_s[PACK * q : PACK * (q + 1), :].bitcast(I32)
+            )
+        weights = tenant([P, S], F32, "weights", "window")
+        first_count = FIRST_PIECES[0][1]
+        nc.sync.dma_start(weights[:, 0:first_count], wgs[:, 0:first_count])
+        load_w1("w1_early", "w1_b")
+        nc.sync.dma_start(weights[:, first_count:S], wgs[:, first_count:S])
         v_w = [keep.tile([P, HALF], U32, name=f"v_w{h}", align_bytes=ALIGN) for h in range(S // HALF)]
         for h in range(S // HALF):
-            nc.vector.tensor_copy(v_s[h][:], tab_s[:].indirect(entries(idx, h * HALF, HALF)))
             nc.vector.tensor_copy(v_w[h][:], tab_w[:].bitcast(U32).indirect(entries(idx, h * HALF, HALF)))
+
+        first_bf = tenant([P, P * PACK], BF16, "first_bf", "first_bf")
+        nc.scalar.activation(*interleaved(first_bf[:], w1_raw["w1_tile0"][:]), ACT.Copy)
+        w1_q = {"w1_tile0": quantised("w1_tile0", first_bf, P)}
+
+        load_w1("w1_second", "w1_a")
+        load_w1("w1_third", "table")
+        w2_rest = load_w2_words(R_PASS, H, "first_bf")
 
         identity = keep.tile([P, P], F32, name="identity")
         make_identity(nc, identity[:])
@@ -192,24 +191,33 @@ def tile_list_phishing_verdict_slots_kernel(
         def reorder_w2(words, scales):
             nc.vector.tensor_copy(
                 words.bitcast(U16).rearrange("p (t u) -> p t u", t=PACK),
-                w2_w[LAST][:].bitcast(U16).rearrange("p (u t) -> p t u", t=PACK),
+                w2_rest[:, 2 * R_PASS : 4 * R_PASS].bitcast(U16).rearrange("p (u t) -> p t u", t=PACK),
             )
             nc.vector.tensor_copy(
                 scales.rearrange("p (t u) -> p t u", t=PACK),
-                w2_s[:, LAST * R_PASS : H].rearrange("p (u t) -> p t u", t=PACK),
+                dealt["w2_s_rest"][:, R_PASS : 2 * R_PASS].rearrange("p (u t) -> p t u", t=PACK),
             )
             dealt["w2"] = (words, scales)
 
-        w3_raw = tenant([P, PASSES, PACK, N_OUT], F32, "w3_raw", "table")
-        for g in range(PASSES):
-            nc.sync.dma_start(
-                w3_raw[:, g, :, :], w3[g * R_PASS : (g + 1) * R_PASS, :].rearrange("(p j) n -> p j n", j=PACK)
-            )
+        def load_w3(tag):
+            dealt["w3_raw"] = tenant([P, PASSES, PACK, N_OUT], F32, "w3_raw", tag)
+            for g in range(PASSES):
+                nc.sync.dma_start(
+                    dealt["w3_raw"][:, g, :, :],
+                    w3[g * R_PASS : (g + 1) * R_PASS, :].rearrange("(p j) n -> p j n", j=PACK),
+                )
+
+        def load_w2_scales(tag):
+            rest = tenant([P, H - R_PASS], U8, "w2_s_rest", tag)
+            nc.gpsimd.memset(rest[:].bitcast(I32), 0)
+            load_scale_rows(rest, w2_scales[0, :, R_PASS:H])
+            dealt["w2_s_rest"] = rest
+
         casts["w3"] = keep.tile([P, PASSES * N_OUT * PACK], BF16, name="w3_bf", align_bytes=ALIGN)
 
         def cast_w3(g):
             part = casts["w3"][:, g * N_OUT * PACK : (g + 1) * N_OUT * PACK]
-            nc.scalar.activation(*interleaved(part, w3_raw[:, g, :, :]), ACT.Copy)
+            nc.scalar.activation(*interleaved(part, dealt["w3_raw"][:, g, :, :]), ACT.Copy)
 
         def side_work(name):
             width = casts[name].shape[1] // PACK
@@ -233,7 +241,10 @@ def tile_list_phishing_verdict_slots_kernel(
 
         def w2_operand(i):
             g, t = divmod(i, PACK)
-            words, scales = dealt["w2"] if g == LAST else (w2_w[g], w2_s[:, g * R_PASS : (g + 1) * R_PASS])
+            if g == 0:
+                words, scales = w2_first, w2_s_first
+            else:
+                words, scales = dealt["w2"] if g == LAST else (w2_rest, dealt["w2_s_rest"])
             return words[:, 2 * t * P : 2 * (t + 1) * P].bitcast(FP4X4), scales[:, t * P : (t + 1) * P]
 
         def first_sum(tag, operand, first, count):
@@ -246,7 +257,7 @@ def tile_list_phishing_verdict_slots_kernel(
                 lhsT=codes,
                 lhsT_scale=scale,
                 rhs=v_w[h][:, part].bitcast(FP8X4),
-                rhs_scale=v_s[h][:, part],
+                rhs_scale=v_s[:, first : first + count],
                 start=True,
                 stop=True,
             )
@@ -277,9 +288,11 @@ def tile_list_phishing_verdict_slots_kernel(
             return stretches[:, start : start + count]
 
         def first_tile():
-            low = keep.tile([P, HALF], F32, name="damp_first")
             for first, count in FIRST_PIECES:
-                damp = low[:, first : first + count] if first < HALF else stretch(0, -count // 2, count)
+                if first < HALF:
+                    damp = tenant([P, count], F32, "damp_first", f"low{first}")[:]
+                else:
+                    damp = stretch(0, -count // 2, count)
                 damping(damp, squared(0, first, count, scratch(count)))
                 if first < HALF:
                     sig = stretch(-1, first, count)
@@ -398,7 +411,7 @@ def tile_list_phishing_verdict_slots_kernel(
             bank = turn((negated_margin(i), fetched), "turn")
             if g == LAST:
                 if t == 0:
-                    dealt["diffs"] = tenant([P, PACK, M_OUT], F32, "diffs", "margin0")
+                    dealt["diffs"] = tenant([P, PACK, M_OUT], F32, "diffs", f"low{FIRST_PIECES[1][0]}")
                 across = tenant([P, M_OUT], F32, "across", f"turned{t % 2}")
                 nc.scalar.copy(across[:], bank[:])
                 nc.scalar.copy(dealt["diffs"][:, t, :], turn((across,), "back")[:])
@@ -457,7 +470,7 @@ def tile_list_phishing_verdict_slots_kernel(
             for b in range(BLOCKS // 2, BLOCKS):
                 close(b)
             for b in range(BLOCKS):
-                result = tenant([P, N_OUT], F32, "result", ("table", "scale_rows", "first_rest", "page_odd")[b])
+                result = tenant([P, N_OUT], F32, "result", ("table", "window", "first_rest", "page_odd")[b])
                 if b % 2 == 1:
                     nc.vector.tensor_copy(result[:], banks[b][:])
                 else:
@@ -468,17 +481,24 @@ def tile_list_phishing_verdict_slots_kernel(
                 )
 
         first_tile()
+        load_w2_scales(f"low{FIRST_PIECES[0][0]}")
+        load_margin(0, f"low{FIRST_PIECES[1][0]}")
+        load_w1("w1_last", "w1_b")
+        load_margin(1, "first_rest")
         before = (0,)
         ahead = dampings(0)
         cast_w1(ROUNDS[0][2], "cast0")
+        load_margin(LAST, "w1_a")
         for r, (tiles, share, side) in enumerate(ROUNDS):
             signatures(r, *ahead)
             if r + 1 < len(ROUNDS):
                 ahead = dampings(r + 1)
                 if ROUNDS[r + 1][2] in W1_PARTS:
                     cast_w1(ROUNDS[r + 1][2], f"cast{r + 1}")
+            if r == 0:
+                load_w3("table")
             if r == 1:
-                load_last_weights("w1_third_raw")
+                load_last_weights("w1_b")
             if 1 <= r <= PASSES:
                 cast_w3(r - 1)
             for k, i in enumerate(before):

@@ -65,9 +65,9 @@ def tile_list_phishing_verdict_slots_kernel(
         def entries(offsets, first, count):
             return offsets[:, first // PER_COLUMN : (first + count) // PER_COLUMN]
 
-        def load_scale_rows(scale_tile, rows, quads=range(QUADS)):
+        def load_scale_rows(scale_tile, rows, quads=range(QUADS), queue=nc.sync):
             for q in quads:
-                nc.sync.dma_start(
+                queue.dma_start(
                     scale_tile[QUAD * q : QUAD * q + PACK, :].bitcast(I32),
                     rows[PACK * q : PACK * (q + 1), :].bitcast(I32),
                 )
@@ -115,7 +115,7 @@ def tile_list_phishing_verdict_slots_kernel(
         nc.sync.dma_start(idx2[:], offs2)
         nc.sync.dma_start(idx3[:], offs3)
         w2_s_first = keep.tile([P, R_PASS], U8, name="w2_s_first", align_bytes=ALIGN)
-        load_scale_rows(w2_s_first, w2_scales[0, :, 0:R_PASS], range(QUADS - 1))
+        load_scale_rows(w2_s_first, w2_scales[0, :, 0:R_PASS], range(QUADS - 1), nc.scalar)
         tab_w = tenant([P, T], I32, "tab_w", "table")
         nc.sync.dma_start(tab_w[:], tab_words[0].rearrange("p t i -> p (t i)").bitcast(I32))
         load_w1("w1_tile0", "w1_a")
@@ -449,36 +449,51 @@ def tile_list_phishing_verdict_slots_kernel(
             rows = dealt["diffs"]
             blocks = [slice(b * P, (b + 1) * P) for b in range(BLOCKS)]
             z_bf = [keep.tile([P, P * PACK], BF16, name=f"z_last{b}", align_bytes=ALIGN) for b in range(BLOCKS)]
-            for b, cols in enumerate(blocks):
+
+            def fetch(b):
                 nc.vector.tensor_tensor(
-                    rows[:, PACK - 1, cols],
-                    pages[i % 2][:].indirect(entries(idx3, cols.start, P)),
-                    margins[LAST][:, PACK - 1, cols],
+                    rows[:, PACK - 1, blocks[b]],
+                    pages[i % 2][:].indirect(entries(idx3, blocks[b].start, P)),
+                    margins[LAST][:, PACK - 1, blocks[b]],
                     ALU.subtract,
                 )
-                if b < BLOCKS // 2:
-                    nc.scalar.activation(*interleaved(z_bf[b][:], rows[:, :, cols]), ACT.Relu)
+
+            def relu(b, on_vector):
+                views = interleaved(z_bf[b][:], rows[:, :, blocks[b]])
+                if on_vector:
+                    nc.vector.tensor_scalar_max(*views, 0.0)
+                else:
+                    nc.scalar.activation(*views, ACT.Relu)
 
             def close(b):
                 codes, scales = quantised(f"z_last{b}", z_bf[b], P)
                 score(LAST, banks[b], codes[:], scales[:])
 
-            for b in range(BLOCKS // 2):
-                later = b + BLOCKS // 2
-                nc.vector.tensor_scalar_max(*interleaved(z_bf[later][:], rows[:, :, blocks[later]]), 0.0)
-                close(b)
-            for b in range(BLOCKS // 2, BLOCKS):
-                close(b)
-            for b in range(BLOCKS):
+            def store(b, on_vector):
                 result = tenant([P, N_OUT], F32, "result", ("table", "window", "first_rest", "page_odd")[b])
-                if b % 2 == 1:
+                if on_vector:
                     nc.vector.tensor_copy(result[:], banks[b][:])
                 else:
                     nc.scalar.copy(result[:], banks[b][:])
                 nc.sync.dma_start(
-                    out[:, b * P : (b + 1) * P].rearrange("(k p) m -> p k m", p=P),
+                    out[:, blocks[b]].rearrange("(k p) m -> p k m", p=P),
                     result[:].rearrange("p (k m) -> p k m", m=P),
                 )
+
+            fetch(0)
+            fetch(1)
+            relu(0, True)
+            relu(1, False)
+            fetch(2)
+            relu(2, False)
+            close(0)
+            fetch(3)
+            close(1)
+            relu(3, True)
+            close(2)
+            close(3)
+            for b in range(BLOCKS):
+                store(b, b == BLOCKS - 1)
 
         first_tile()
         load_w2_scales(f"low{FIRST_PIECES[0][0]}")

@@ -41,7 +41,7 @@ ROUNDS = (
     ((5, 6), 704, "w1_last"),
     ((7, 8), 704, "z0"),
     ((9, 10), 704, "w3"),
-    ((11,), 896, "z1"),
+    ((11,), 992, "z1"),
 )
 SPARE = 1088
 W1_PARTS = {"w1_tile0": (0, 1), "w1_early": (1, 3), "w1_second": (3, 5), "w1_third": (5, 8), "w1_last": (8, 12)}
@@ -74,10 +74,12 @@ def tile_list_phishing_verdict_slots_kernel(
 
         w1_raw = {}
 
-        def load_w1(part, tag):
+        def load_w1(part, tag, place=None):
             first, stop = W1_PARTS[part]
-            w1_raw[part] = tenant([P, PACK, (stop - first) * P], F32, "w1_raw", tag)
-            nc.sync.dma_start(w1_raw[part][:], w1[:, first * P : stop * P].rearrange("(p j) c -> p j c", j=PACK))
+            if place is None:
+                place = tenant([P, PACK * (stop - first) * P], F32, "w1_raw", tag)[:]
+            w1_raw[part] = place.rearrange("p (j c) -> p j c", j=PACK)
+            nc.sync.dma_start(w1_raw[part], w1[:, first * P : stop * P].rearrange("(p j) c -> p j c", j=PACK))
 
         def load_w2_words(first, stop, tag):
             words = tenant([P, 2 * (stop - first)], U8, "w2_w", tag)
@@ -110,7 +112,7 @@ def tile_list_phishing_verdict_slots_kernel(
         idx3 = lists.tile([P, M_OUT // PER_COLUMN], U16, name="idx3")
 
         tab_scale_rows = tenant([P, T], U8, "tab_scale_rows", "page_odd")
-        nc.sync.dma_start(tab_scale_rows[0:SCALE_ROWS, :].bitcast(I32), tab_scales[0].bitcast(I32))
+        nc.scalar.dma_start(tab_scale_rows[0:SCALE_ROWS, :].bitcast(I32), tab_scales[0].bitcast(I32))
         nc.sync.dma_start(idx[:], offs)
         nc.sync.dma_start(idx2[:], offs2)
         nc.sync.dma_start(idx3[:], offs3)
@@ -120,7 +122,11 @@ def tile_list_phishing_verdict_slots_kernel(
         nc.sync.dma_start(tab_w[:], tab_words[0].rearrange("p t i -> p (t i)").bitcast(I32))
         load_w1("w1_tile0", "w1_a")
         load_scale_rows(w2_s_first, w2_scales[0, :, 0:R_PASS], range(QUADS - 1, QUADS))
-        w2_first = load_w2_words(0, R_PASS, "w2_first")
+        w2_outer = keep.tile([P, 2, 2 * R_PASS], U8, name="w2_outer", align_bytes=ALIGN)
+        nc.sync.dma_start(
+            w2_outer[:].bitcast(I32), w2_words[0].rearrange("p (g c) -> p g c", g=PASSES)[:, 0:PASSES:LAST, :].bitcast(I32)
+        )
+        w2_first = w2_outer[:, 0, :]
 
         margins = {}
 
@@ -145,10 +151,11 @@ def tile_list_phishing_verdict_slots_kernel(
             nc.sync.dma_start(
                 v_s[QUAD * q : QUAD * q + PACK, :].bitcast(I32), picked_s[PACK * q : PACK * (q + 1), :].bitcast(I32)
             )
-        weights = tenant([P, S], F32, "weights", "window")
+        after_window = tenant([P, 2 * S], F32, "after_window", "window")
+        weights = after_window[:, 0:S]
         first_count = FIRST_PIECES[0][1]
         nc.sync.dma_start(weights[:, 0:first_count], wgs[:, 0:first_count])
-        load_w1("w1_early", "w1_b")
+        load_w1("w1_early", None, after_window[:, S : 2 * S])
         nc.sync.dma_start(weights[:, first_count:S], wgs[:, first_count:S])
         v_w = [keep.tile([P, HALF], U32, name=f"v_w{h}", align_bytes=ALIGN) for h in range(S // HALF)]
         for h in range(S // HALF):
@@ -158,9 +165,15 @@ def tile_list_phishing_verdict_slots_kernel(
         nc.scalar.activation(*interleaved(first_bf[:], w1_raw["w1_tile0"][:]), ACT.Copy)
         w1_q = {"w1_tile0": quantised("w1_tile0", first_bf, P)}
 
-        load_w1("w1_second", "w1_a")
+        w2_last = tenant([P, 2 * R_PASS], U8, "w2_last", "first_bf")
+        nc.vector.tensor_copy(
+            w2_last[:].bitcast(U16).rearrange("p (t u) -> p t u", t=PACK),
+            w2_outer[:, 1, :].bitcast(U16).rearrange("p (u t) -> p t u", t=PACK),
+        )
+
+        load_w1("w1_second", "w1_b")
         load_w1("w1_third", "table")
-        w2_rest = load_w2_words(R_PASS, H, "first_bf")
+        w2_rest = load_w2_words(R_PASS, 2 * R_PASS, "w1_a")
 
         identity = keep.tile([P, P], F32, name="identity")
         make_identity(nc, identity[:])
@@ -170,8 +183,9 @@ def tile_list_phishing_verdict_slots_kernel(
         dealt = {}
         turned = {}
 
-        def cast_w1(part, tag):
-            bf = tenant([P, w1_raw[part].shape[2] * PACK], BF16, part + "_bf", tag)
+        def cast_w1(part, tag, bf=None):
+            if bf is None:
+                bf = tenant([P, w1_raw[part].shape[2] * PACK], BF16, part + "_bf", tag)
             if part == "w1_last":
                 dst = bf[:].rearrange("p (t u j) -> p u t j", t=PACK, j=PACK)
                 rows = w1_raw[part][:].rearrange("p j (u t) -> p u t j", t=PACK)
@@ -188,16 +202,12 @@ def tile_list_phishing_verdict_slots_kernel(
                 )
             dealt["weights"] = weights_last
 
-        def reorder_w2(words, scales):
-            nc.vector.tensor_copy(
-                words.bitcast(U16).rearrange("p (t u) -> p t u", t=PACK),
-                w2_rest[:, 2 * R_PASS : 4 * R_PASS].bitcast(U16).rearrange("p (u t) -> p t u", t=PACK),
-            )
+        def reorder_w2(scales):
             nc.vector.tensor_copy(
                 scales.rearrange("p (t u) -> p t u", t=PACK),
                 dealt["w2_s_rest"][:, R_PASS : 2 * R_PASS].rearrange("p (u t) -> p t u", t=PACK),
             )
-            dealt["w2"] = (words, scales)
+            dealt["w2"] = (w2_last, scales)
 
         def load_w3(tag):
             dealt["w3_raw"] = tenant([P, PASSES, PACK, N_OUT], F32, "w3_raw", tag)
@@ -222,10 +232,9 @@ def tile_list_phishing_verdict_slots_kernel(
         def side_work(name):
             width = casts[name].shape[1] // PACK
             if name == "w1_third":
-                both = tenant([P, 4 * width + 3 * R_PASS], U8, "both", name)
+                both = tenant([P, 4 * width + R_PASS], U8, "both", name)
                 made = quantised(name, casts[name], width, codes=both[:, 0 : 4 * width].bitcast(U32))
-                words, scales = 4 * width, 4 * width + 2 * R_PASS
-                reorder_w2(both[:, words:scales], both[:, scales : scales + R_PASS])
+                reorder_w2(both[:, 4 * width : 4 * width + R_PASS])
             else:
                 made = quantised(name, casts[name], width)
             if name in W1_PARTS:
@@ -281,7 +290,7 @@ def tile_list_phishing_verdict_slots_kernel(
                 pages[i % 2][:].indirect(entries(idx2, first, count)), sig, weight[:, first : first + count], ALU.mult
             )
 
-        stretches = keep.tile([P, 2 * (SPARE + 2 * S)], F32, name="stretches")
+        stretches = keep.tile([P, 2 * (SPARE + 2 * S)], F32, name="stretches", align_bytes=ALIGN)
 
         def stretch(r, first, count):
             start = (r % 2) * (SPARE + 2 * S) + SPARE + first
@@ -293,16 +302,17 @@ def tile_list_phishing_verdict_slots_kernel(
                     damp = tenant([P, count], F32, "damp_first", f"low{first}")[:]
                 else:
                     damp = stretch(0, -count // 2, count)
-                damping(damp, squared(0, first, count, scratch(count)))
-                if first < HALF:
-                    sig = stretch(-1, first, count)
-                else:
-                    cast_w1("w1_early", "first_rest")
+                square = tenant([P, count], F32, "square_last", "w1_c")[:] if first >= HALF else scratch(count)
+                damping(damp, squared(0, first, count, square))
+                sig = stretch(-1, first, count)
+                if first >= HALF:
+                    cast_w1("w1_early", None, sig.bitcast(BF16))
                     side_work("w1_early")
-                    sig = tenant([P, count], F32, "sig_first", "first_rest")[:]
                 a_ps = first_sum("a_own", w1_operand(0), first, count)
                 nc.vector.tensor_tensor(sig, a_ps, damp, ALU.mult)
-                scatter(0, first, count, sig)
+                if first == 0:
+                    scatter(0, first, count, sig)
+            scatter(0, first_count, S - first_count, stretch(-1, first_count, S - first_count))
 
         def parts(r, k):
             own = S - ROUNDS[r][1]
@@ -353,7 +363,7 @@ def tile_list_phishing_verdict_slots_kernel(
             if rest.start < rest.stop:
                 damping(damp_share[:, shared(r, count - 1, half, rest)], square[:, rest])
             late = ((inner.start - own.start, square[:, inner]), (apart.start - own.start, square_apart[:]))
-            end = S - ROUNDS[r - 1][1] if r > 0 else HALF
+            end = S - ROUNDS[r - 1][1] if r > 0 else first_count
             a_share = stretch(r - 1, end - share * count, share * count)
             a_own = []
             for k, i in enumerate(tiles):
@@ -470,7 +480,7 @@ def tile_list_phishing_verdict_slots_kernel(
                 score(LAST, banks[b], codes[:], scales[:])
 
             def store(b, on_vector):
-                result = tenant([P, N_OUT], F32, "result", ("table", "window", "first_rest", "page_odd")[b])
+                result = tenant([P, N_OUT], F32, "result", ("table", "window", "cast0", "page_odd")[b])
                 if on_vector:
                     nc.vector.tensor_copy(result[:], banks[b][:])
                 else:
@@ -498,12 +508,11 @@ def tile_list_phishing_verdict_slots_kernel(
         first_tile()
         load_w2_scales(f"low{FIRST_PIECES[0][0]}")
         load_margin(0, f"low{FIRST_PIECES[1][0]}")
-        load_w1("w1_last", "w1_b")
-        load_margin(1, "first_rest")
+        load_w1("w1_last", "w1_c")
         before = (0,)
         ahead = dampings(0)
         cast_w1(ROUNDS[0][2], "cast0")
-        load_margin(LAST, "w1_a")
+        load_margin(LAST, "w1_b")
         for r, (tiles, share, side) in enumerate(ROUNDS):
             signatures(r, *ahead)
             if r + 1 < len(ROUNDS):
@@ -513,12 +522,14 @@ def tile_list_phishing_verdict_slots_kernel(
             if r == 0:
                 load_w3("table")
             if r == 1:
-                load_last_weights("w1_b")
+                load_last_weights("w1_c")
             if 1 <= r <= PASSES:
                 cast_w3(r - 1)
             for k, i in enumerate(before):
                 finish_tile(i, gathered[:, k * M_OUT : (k + 1) * M_OUT])
             side_work(side)
+            if r == 0:
+                load_margin(1, "cast0")
             for k, i in enumerate(tiles):
                 scatter(i, 0, S, stretch(r, k * S, S))
             before = tiles

@@ -147,15 +147,16 @@ def tile_list_phishing_verdict_slots_kernel(
         picked_s = tenant([P, S], U8, "picked_s", "w1_b")
         nc.vector.tensor_copy(picked_s[:], tab_s[:].indirect(idx[:]))
         v_s = keep.tile([P, S], U8, name="v_s", align_bytes=ALIGN)
-        for q in range(QUADS):
+        nc.vector.tensor_copy(v_s[0:SCALE_ROWS, :].bitcast(I32), picked_s[0:SCALE_ROWS, :].bitcast(I32))
+        for q in range(1, QUADS):
             nc.sync.dma_start(
                 v_s[QUAD * q : QUAD * q + PACK, :].bitcast(I32), picked_s[PACK * q : PACK * (q + 1), :].bitcast(I32)
             )
         after_window = tenant([P, 2 * S], F32, "after_window", "window")
         weights = after_window[:, 0:S]
         first_count = FIRST_PIECES[0][1]
-        nc.sync.dma_start(weights[:, 0:first_count], wgs[:, 0:first_count])
         load_w1("w1_early", None, after_window[:, S : 2 * S])
+        nc.sync.dma_start(weights[:, 0:first_count], wgs[:, 0:first_count])
         nc.sync.dma_start(weights[:, first_count:S], wgs[:, first_count:S])
         v_w = [keep.tile([P, HALF], U32, name=f"v_w{h}", align_bytes=ALIGN) for h in range(S // HALF)]
         for h in range(S // HALF):
@@ -511,10 +512,11 @@ def tile_list_phishing_verdict_slots_kernel(
         load_w1("w1_last", "w1_c")
         before = (0,)
         ahead = dampings(0)
-        cast_w1(ROUNDS[0][2], "cast0")
-        load_margin(LAST, "w1_b")
         for r, (tiles, share, side) in enumerate(ROUNDS):
             signatures(r, *ahead)
+            if r == 0:
+                cast_w1(side, "cast0")
+                load_margin(LAST, "w1_b")
             if r + 1 < len(ROUNDS):
                 ahead = dampings(r + 1)
                 if ROUNDS[r + 1][2] in W1_PARTS:

@@ -65,9 +65,9 @@ def tile_list_phishing_verdict_slots_kernel(
         def entries(offsets, first, count):
             return offsets[:, first // PER_COLUMN : (first + count) // PER_COLUMN]
 
-        def load_scale_rows(scale_tile, rows, quads=range(QUADS), queue=nc.sync):
-            for q in quads:
-                queue.dma_start(
+        def load_scale_rows(scale_tile, rows):
+            for q in range(QUADS):
+                nc.sync.dma_start(
                     scale_tile[QUAD * q : QUAD * q + PACK, :].bitcast(I32),
                     rows[PACK * q : PACK * (q + 1), :].bitcast(I32),
                 )
@@ -116,12 +116,11 @@ def tile_list_phishing_verdict_slots_kernel(
         nc.sync.dma_start(idx[:], offs)
         nc.sync.dma_start(idx2[:], offs2)
         nc.sync.dma_start(idx3[:], offs3)
-        w2_s_first = keep.tile([P, R_PASS], U8, name="w2_s_first", align_bytes=ALIGN)
-        load_scale_rows(w2_s_first, w2_scales[0, :, 0:R_PASS], range(QUADS - 1), nc.scalar)
+        joined = tenant([P, S + R_PASS], U8, "joined", "w1_b")
+        nc.scalar.dma_start(joined[0:SCALE_ROWS, S : S + R_PASS].bitcast(I32), w2_scales[0, :, 0:R_PASS].bitcast(I32))
         tab_w = tenant([P, T], I32, "tab_w", "table")
         nc.sync.dma_start(tab_w[:], tab_words[0].rearrange("p t i -> p (t i)").bitcast(I32))
         load_w1("w1_tile0", "w1_a")
-        load_scale_rows(w2_s_first, w2_scales[0, :, 0:R_PASS], range(QUADS - 1, QUADS))
         w2_outer = keep.tile([P, 2, 2 * R_PASS], U8, name="w2_outer", align_bytes=ALIGN)
         nc.sync.dma_start(
             w2_outer[:].bitcast(I32), w2_words[0].rearrange("p (g c) -> p g c", g=PASSES)[:, 0:PASSES:LAST, :].bitcast(I32)
@@ -144,15 +143,17 @@ def tile_list_phishing_verdict_slots_kernel(
         nc.gpsimd.memset(page_odd[:], 0.0)
         pages = [page_even, page_odd]
 
-        picked_s = tenant([P, S], U8, "picked_s", "w1_b")
+        picked_s = tenant([P, S], U8, "picked_s", "after_picked")
         nc.vector.tensor_copy(picked_s[:], tab_s[:].indirect(idx[:]))
-        v_s = keep.tile([P, S], U8, name="v_s", align_bytes=ALIGN)
-        nc.vector.tensor_copy(v_s[0:SCALE_ROWS, :].bitcast(I32), picked_s[0:SCALE_ROWS, :].bitcast(I32))
+        nc.vector.tensor_copy(joined[0:SCALE_ROWS, 0:S].bitcast(I32), picked_s[0:SCALE_ROWS, :].bitcast(I32))
+        first_s = keep.tile([P, S + R_PASS], U8, name="first_s", align_bytes=ALIGN)
+        v_s, w2_s_first = first_s[:, 0:S], first_s[:, S : S + R_PASS]
+        nc.vector.tensor_copy(first_s[0:SCALE_ROWS, :].bitcast(I32), joined[0:SCALE_ROWS, :].bitcast(I32))
         for q in range(1, QUADS):
             nc.sync.dma_start(
-                v_s[QUAD * q : QUAD * q + PACK, :].bitcast(I32), picked_s[PACK * q : PACK * (q + 1), :].bitcast(I32)
+                first_s[QUAD * q : QUAD * q + PACK, :].bitcast(I32), joined[PACK * q : PACK * (q + 1), :].bitcast(I32)
             )
-        after_window = tenant([P, 2 * S], F32, "after_window", "window")
+        after_window = tenant([P, 2 * S], F32, "after_window", "after_picked")
         weights = after_window[:, 0:S]
         first_count = FIRST_PIECES[0][1]
         load_w1("w1_early", None, after_window[:, S : 2 * S])
@@ -481,7 +482,7 @@ def tile_list_phishing_verdict_slots_kernel(
                 score(LAST, banks[b], codes[:], scales[:])
 
             def store(b, on_vector):
-                result = tenant([P, N_OUT], F32, "result", ("table", "window", "cast0", "page_odd")[b])
+                result = tenant([P, N_OUT], F32, "result", ("table", "after_picked", "cast0", "page_odd")[b])
                 if on_vector:
                     nc.vector.tensor_copy(result[:], banks[b][:])
                 else:

@@ -46,6 +46,8 @@ ROUNDS = (
 SPARE = 1088
 W1_PARTS = {"w1_tile0": (0, 1), "w1_early": (1, 3), "w1_second": (3, 5), "w1_third": (5, 8), "w1_last": (8, 12)}
 BANKS = {"a_own": 2, "a_share": 1, "b": 1, "turn": 2, "back": 2}
+FIRST_BANK = {"a_own": 0, "a_share": 2, "b": 3, "turn": 4, "back": 6}
+BANK_BYTES = 2048
 BLOCKS = M_OUT // P
 
 
@@ -262,7 +264,7 @@ def tile_list_phishing_verdict_slots_kernel(
             codes, scale = operand
             h = first // HALF
             part = slice(first - h * HALF, first - h * HALF + count)
-            bank = psum.tile([P, HALF], F32, name="first_ps", tag=tag, bufs=BANKS[tag])
+            bank = psum.tile([P, HALF], F32, name="first_ps", tag=tag, bufs=BANKS[tag], offset=FIRST_BANK[tag] * BANK_BYTES)
             nc.tensor.matmul_mx(
                 out=bank[:, 0:count],
                 lhsT=codes,
@@ -392,7 +394,10 @@ def tile_list_phishing_verdict_slots_kernel(
             return negated
 
         def turn(terms, tag):
-            bank = psum.tile([P, M_OUT], F32, name="turn_ps", tag=tag, bufs=BANKS[tag])
+            if tag == "final":
+                bank = psum.tile([P, BLOCKS, M_OUT], F32, name="final_ps", bufs=1, offset=FIRST_BANK["turn"] * BANK_BYTES)[:, 0, :]
+            else:
+                bank = psum.tile([P, M_OUT], F32, name="turn_ps", tag=tag, bufs=BANKS[tag], offset=FIRST_BANK[tag] * BANK_BYTES)
             for k in range(BLOCKS):
                 cols = slice(k * P, (k + 1) * P)
                 for n, rows in enumerate(terms):
@@ -426,7 +431,7 @@ def tile_list_phishing_verdict_slots_kernel(
                     dealt["diffs"] = tenant([P, PACK, M_OUT], F32, "diffs", f"low{FIRST_PIECES[1][0]}")
                 across = tenant([P, M_OUT], F32, "across", f"turned{t % 2}")
                 nc.scalar.copy(across[:], bank[:])
-                nc.scalar.copy(dealt["diffs"][:, t, :], turn((across,), "back")[:])
+                nc.scalar.copy(dealt["diffs"][:, t, :], turn((across,), "final" if i == TILES - 2 else "back")[:])
                 return
             if t == 0:
                 turned[g] = tenant([P, BLOCKS * R_PASS], BF16, "turned", f"turned{g}")
@@ -452,8 +457,10 @@ def tile_list_phishing_verdict_slots_kernel(
 
         def finish():
             i = TILES - 1
-            tags = ("b", "a_share", "a_own", "a_own")
-            banks = [psum.tile([P, N_OUT], F32, name="out_ps", tag=tag, bufs=BANKS[tag]) for tag in tags]
+            banks = [
+                psum.tile([P, N_OUT], F32, name=f"out_ps{b}", bufs=1, offset=(FIRST_BANK["turn"] + b) * BANK_BYTES)[:]
+                for b in range(BLOCKS)
+            ]
             for g in range(LAST):
                 codes, scales = quants[f"z{g}"]
                 for b in range(BLOCKS):
@@ -484,9 +491,9 @@ def tile_list_phishing_verdict_slots_kernel(
             def store(b, on_vector):
                 result = tenant([P, N_OUT], F32, "result", ("table", "after_picked", "cast0", "page_odd")[b])
                 if on_vector:
-                    nc.vector.tensor_copy(result[:], banks[b][:])
+                    nc.vector.tensor_copy(result[:], banks[b])
                 else:
-                    nc.scalar.copy(result[:], banks[b][:])
+                    nc.scalar.copy(result[:], banks[b])
                 nc.sync.dma_start(
                     out[:, blocks[b]].rearrange("(k p) m -> p k m", p=P),
                     result[:].rearrange("p (k m) -> p k m", m=P),

@@ -40,9 +40,10 @@ ROUNDS = (
     ((3, 4), 704, "w1_third"),
     ((5, 6), 704, "w1_last"),
     ((7, 8), 704, "z0"),
-    ((9, 10), 704, "w3"),
+    ((9, 10), 704, "w3_early"),
     ((11,), 992, "z1"),
 )
+W3_CASTS = {2: 0, 3: 1, 5: 2}
 SPARE = 1088
 W1_PARTS = {"w1_tile0": (0, 1), "w1_early": (1, 3), "w1_second": (3, 5), "w1_third": (5, 8), "w1_last": (8, 12)}
 BANKS = {"a_own": 2, "a_share": 1, "b": 1, "turn": 2, "back": 2}
@@ -227,10 +228,11 @@ def tile_list_phishing_verdict_slots_kernel(
             load_scale_rows(rest, w2_scales[0, :, R_PASS:H])
             dealt["w2_s_rest"] = rest
 
-        casts["w3"] = keep.tile([P, PASSES * N_OUT * PACK], BF16, name="w3_bf", align_bytes=ALIGN)
+        casts["w3_early"] = keep.tile([P, LAST * N_OUT * PACK], BF16, name="w3_early_bf", align_bytes=ALIGN)
+        casts["w3_last"] = keep.tile([P, N_OUT * PACK], BF16, name="w3_last_bf", align_bytes=ALIGN)
 
         def cast_w3(g):
-            part = casts["w3"][:, g * N_OUT * PACK : (g + 1) * N_OUT * PACK]
+            part = casts["w3_last"][:] if g == LAST else casts["w3_early"][:, g * N_OUT * PACK : (g + 1) * N_OUT * PACK]
             nc.scalar.activation(*interleaved(part, dealt["w3_raw"][:, g, :, :]), ACT.Copy)
 
         def side_work(name):
@@ -339,7 +341,10 @@ def tile_list_phishing_verdict_slots_kernel(
 
         def dampings(r):
             tiles, share, side = ROUNDS[r]
-            damp_share = ring.tile([P, len(tiles) * share], F32, name="damp_share", tag="damp_share", bufs=2)
+            if r + 1 < len(ROUNDS):
+                damp_share = ring.tile([P, len(tiles) * share], F32, name="damp_share", tag="damp_share", bufs=2)
+            else:
+                damp_share = tenant([P, share], F32, "damp_share", "w3_last")
             damp = []
             for k, i in enumerate(tiles):
                 if i != tiles[-1]:
@@ -444,11 +449,13 @@ def tile_list_phishing_verdict_slots_kernel(
 
         def score(g, bank, z_codes, z_scale):
             for k in range(N_OUT // P):
-                cols = slice(g * N_OUT + k * P, g * N_OUT + (k + 1) * P)
+                first = k * P if g == LAST else g * N_OUT + k * P
+                cols = slice(first, first + P)
+                codes, scales = quants["w3_last" if g == LAST else "w3_early"]
                 nc.tensor.matmul_mx(
                     out=bank[:, k * P : (k + 1) * P],
-                    lhsT=quants["w3"][0][:, cols].bitcast(FP8X4),
-                    lhsT_scale=quants["w3"][1][:, cols],
+                    lhsT=codes[:, cols].bitcast(FP8X4),
+                    lhsT_scale=scales[:, cols],
                     rhs=z_codes.bitcast(FP8X4),
                     rhs_scale=z_scale,
                     start=(g == 0 and k == 0),
@@ -457,6 +464,7 @@ def tile_list_phishing_verdict_slots_kernel(
 
         def finish():
             i = TILES - 1
+            side_work("w3_last")
             banks = [
                 psum.tile([P, N_OUT], F32, name=f"out_ps{b}", bufs=1, offset=(FIRST_BANK["turn"] + b) * BANK_BYTES)[:]
                 for b in range(BLOCKS)
@@ -533,8 +541,8 @@ def tile_list_phishing_verdict_slots_kernel(
                 load_w3("table")
             if r == 1:
                 load_last_weights("w1_c")
-            if 1 <= r <= PASSES:
-                cast_w3(r - 1)
+            if r in W3_CASTS:
+                cast_w3(W3_CASTS[r])
             for k, i in enumerate(before):
                 finish_tile(i, gathered[:, k * M_OUT : (k + 1) * M_OUT])
             side_work(side)

@@ -156,10 +156,15 @@ def tile_list_phishing_verdict_slots_kernel(
             nc.sync.dma_start(
                 first_s[QUAD * q : QUAD * q + PACK, :].bitcast(I32), joined[PACK * q : PACK * (q + 1), :].bitcast(I32)
             )
-        after_window = tenant([P, 2 * S], F32, "after_window", "after_picked")
-        weights = after_window[:, 0:S]
+        stretches = keep.tile([P, 2 * (SPARE + 2 * S)], F32, name="stretches", align_bytes=ALIGN)
+
+        def stretch(r, first, count):
+            start = (r % 2) * (SPARE + 2 * S) + SPARE + first
+            return stretches[:, start : start + count]
+
+        weights = tenant([P, S], F32, "weights", "after_picked")
         first_count = FIRST_PIECES[0][1]
-        load_w1("w1_early", None, after_window[:, S : 2 * S])
+        load_w1("w1_early", None, stretch(-1, 0, S))
         nc.sync.dma_start(weights[:, 0:first_count], wgs[:, 0:first_count])
         nc.sync.dma_start(weights[:, first_count:S], wgs[:, first_count:S])
         v_w = [keep.tile([P, HALF], U32, name=f"v_w{h}", align_bytes=ALIGN) for h in range(S // HALF)]
@@ -296,12 +301,6 @@ def tile_list_phishing_verdict_slots_kernel(
                 pages[i % 2][:].indirect(entries(idx2, first, count)), sig, weight[:, first : first + count], ALU.mult
             )
 
-        stretches = keep.tile([P, 2 * (SPARE + 2 * S)], F32, name="stretches", align_bytes=ALIGN)
-
-        def stretch(r, first, count):
-            start = (r % 2) * (SPARE + 2 * S) + SPARE + first
-            return stretches[:, start : start + count]
-
         def first_tile():
             for first, count in FIRST_PIECES:
                 if first < HALF:
@@ -311,12 +310,14 @@ def tile_list_phishing_verdict_slots_kernel(
                 square = tenant([P, count], F32, "square_last", "w1_c")[:] if first >= HALF else scratch(count)
                 damping(damp, squared(0, first, count, square))
                 sig = stretch(-1, first, count)
-                if first >= HALF:
-                    cast_w1("w1_early", None, sig.bitcast(BF16))
-                    side_work("w1_early")
+                if first == 0:
+                    early_bf = tenant([P, S], BF16, "early_bf", "early_bf")
+                    nc.vector.tensor_copy(*interleaved(early_bf[:], w1_raw["w1_early"]))
+                    casts["w1_early"] = early_bf
                 a_ps = first_sum("a_own", w1_operand(0), first, count)
                 nc.vector.tensor_tensor(sig, a_ps, damp, ALU.mult)
                 if first == 0:
+                    side_work("w1_early")
                     scatter(0, first, count, sig)
             scatter(0, first_count, S - first_count, stretch(-1, first_count, S - first_count))
 

@@ -29,7 +29,7 @@ TILES = H // P
 SCALE_ROWS = R_PASS // QUAD
 HALF = 512
 ALIGN = 64
-QUANT_WORDS = (128, 256, 512, 1024)
+QUANT_WORDS = (128, 256, 384, 512)
 RUN = 4
 
 FIRST_PIECES = ((0, 256), (256, 256), (512, 512))
@@ -175,12 +175,6 @@ def tile_list_phishing_verdict_slots_kernel(
         nc.scalar.activation(*interleaved(first_bf[:], w1_raw["w1_tile0"][:]), ACT.Copy)
         w1_q = {"w1_tile0": quantised("w1_tile0", first_bf, P)}
 
-        w2_last = tenant([P, 2 * R_PASS], U8, "w2_last", "first_bf")
-        nc.vector.tensor_copy(
-            w2_last[:].bitcast(U16).rearrange("p (t u) -> p t u", t=PACK),
-            w2_outer[:, 1, :].bitcast(U16).rearrange("p (u t) -> p t u", t=PACK),
-        )
-
         load_w1("w1_second", "w1_b")
         load_w1("w1_third", "table")
         w2_rest = load_w2_words(R_PASS, 2 * R_PASS, "w1_a")
@@ -217,7 +211,7 @@ def tile_list_phishing_verdict_slots_kernel(
                 scales.rearrange("p (t u) -> p t u", t=PACK),
                 dealt["w2_s_rest"][:, R_PASS : 2 * R_PASS].rearrange("p (u t) -> p t u", t=PACK),
             )
-            dealt["w2"] = (w2_last, scales)
+            dealt["w2"] = (dealt["w2_words"], scales)
 
         def load_w3(tag):
             dealt["w3_raw"] = tenant([P, PASSES, PACK, N_OUT], F32, "w3_raw", tag)
@@ -304,10 +298,10 @@ def tile_list_phishing_verdict_slots_kernel(
         def first_tile():
             for first, count in FIRST_PIECES:
                 if first < HALF:
-                    damp = tenant([P, count], F32, "damp_first", f"low{first}")[:]
+                    damp = tenant([P, count], F32, "damp_first", "damp_mid" if first else "low0")[:]
                 else:
                     damp = stretch(0, -count // 2, count)
-                square = tenant([P, count], F32, "square_last", "w1_c")[:] if first >= HALF else scratch(count)
+                square = tenant([P, count], F32, "square", "w1_c" if first >= HALF else f"low{first}")[:] if first else scratch(count)
                 damping(damp, squared(0, first, count, square))
                 sig = stretch(-1, first, count)
                 if first == 0:
@@ -319,6 +313,11 @@ def tile_list_phishing_verdict_slots_kernel(
                 if first == 0:
                     side_work("w1_early")
                     scatter(0, first, count, sig)
+            dealt["w2_words"] = tenant([P, 2 * R_PASS], U8, "w2_last", "damp_mid")
+            nc.vector.tensor_copy(
+                dealt["w2_words"][:].bitcast(U16).rearrange("p (t u) -> p t u", t=PACK),
+                w2_outer[:, 1, :].bitcast(U16).rearrange("p (u t) -> p t u", t=PACK),
+            )
             scatter(0, first_count, S - first_count, stretch(-1, first_count, S - first_count))
 
         def parts(r, k):

@@ -68,9 +68,9 @@ def tile_list_phishing_verdict_slots_kernel(
         def entries(offsets, first, count):
             return offsets[:, first // PER_COLUMN : (first + count) // PER_COLUMN]
 
-        def load_scale_rows(scale_tile, rows):
+        def load_scale_rows(scale_tile, rows, queues):
             for q in range(QUADS):
-                nc.sync.dma_start(
+                queues[q].dma_start(
                     scale_tile[QUAD * q : QUAD * q + PACK, :].bitcast(I32),
                     rows[PACK * q : PACK * (q + 1), :].bitcast(I32),
                 )
@@ -118,9 +118,8 @@ def tile_list_phishing_verdict_slots_kernel(
         nc.scalar.dma_start(tab_scale_rows[0:SCALE_ROWS, :].bitcast(I32), tab_scales[0].bitcast(I32))
         nc.sync.dma_start(idx[:], offs)
         nc.sync.dma_start(idx2[:], offs2)
-        nc.sync.dma_start(idx3[:], offs3)
-        joined = tenant([P, S + R_PASS], U8, "joined", "w1_b")
-        nc.scalar.dma_start(joined[0:SCALE_ROWS, S : S + R_PASS].bitcast(I32), w2_scales[0, :, 0:R_PASS].bitcast(I32))
+        w2_s_first = keep.tile([P, R_PASS], U8, name="w2_s_first", align_bytes=ALIGN)
+        load_scale_rows(w2_s_first, w2_scales[0, :, 0:R_PASS], (nc.scalar, nc.scalar, nc.scalar, nc.sync))
         tab_w = tenant([P, T], I32, "tab_w", "table")
         nc.sync.dma_start(tab_w[:], tab_words[0].rearrange("p t i -> p (t i)").bitcast(I32))
         load_w1("w1_tile0", "w1_a")
@@ -146,16 +145,15 @@ def tile_list_phishing_verdict_slots_kernel(
         nc.gpsimd.memset(page_odd[:], 0.0)
         pages = [page_even, page_odd]
 
-        picked_s = tenant([P, S], U8, "picked_s", "after_picked")
+        picked_s = tenant([P, S], U8, "picked_s", "w1_b")
         nc.vector.tensor_copy(picked_s[:], tab_s[:].indirect(idx[:]))
-        nc.vector.tensor_copy(joined[0:SCALE_ROWS, 0:S].bitcast(I32), picked_s[0:SCALE_ROWS, :].bitcast(I32))
-        first_s = keep.tile([P, S + R_PASS], U8, name="first_s", align_bytes=ALIGN)
-        v_s, w2_s_first = first_s[:, 0:S], first_s[:, S : S + R_PASS]
-        nc.vector.tensor_copy(first_s[0:SCALE_ROWS, :].bitcast(I32), joined[0:SCALE_ROWS, :].bitcast(I32))
+        v_s = keep.tile([P, S], U8, name="v_s", align_bytes=ALIGN)
+        nc.vector.tensor_copy(v_s[0:SCALE_ROWS, :].bitcast(I32), picked_s[0:SCALE_ROWS, :].bitcast(I32))
         for q in range(1, QUADS):
             nc.sync.dma_start(
-                first_s[QUAD * q : QUAD * q + PACK, :].bitcast(I32), joined[PACK * q : PACK * (q + 1), :].bitcast(I32)
+                v_s[QUAD * q : QUAD * q + PACK, :].bitcast(I32), picked_s[PACK * q : PACK * (q + 1), :].bitcast(I32)
             )
+
         stretches = keep.tile([P, 2 * (SPARE + 2 * S)], F32, name="stretches", align_bytes=ALIGN)
 
         def stretch(r, first, count):
@@ -167,9 +165,13 @@ def tile_list_phishing_verdict_slots_kernel(
         load_w1("w1_early", None, stretch(-1, 0, S))
         nc.sync.dma_start(weights[:, 0:first_count], wgs[:, 0:first_count])
         nc.sync.dma_start(weights[:, first_count:S], wgs[:, first_count:S])
+        nc.sync.dma_start(idx3[:], offs3)
         v_w = [keep.tile([P, HALF], U32, name=f"v_w{h}", align_bytes=ALIGN) for h in range(S // HALF)]
-        for h in range(S // HALF):
-            nc.vector.tensor_copy(v_w[h][:], tab_w[:].bitcast(U32).indirect(entries(idx, h * HALF, HALF)))
+        for first, count in FIRST_PIECES:
+            nc.vector.tensor_copy(
+                v_w[first // HALF][:, first % HALF : first % HALF + count],
+                tab_w[:].bitcast(U32).indirect(entries(idx, first, count)),
+            )
 
         first_bf = tenant([P, P * PACK], BF16, "first_bf", "first_bf")
         nc.scalar.activation(*interleaved(first_bf[:], w1_raw["w1_tile0"][:]), ACT.Copy)
@@ -224,7 +226,7 @@ def tile_list_phishing_verdict_slots_kernel(
         def load_w2_scales(tag):
             rest = tenant([P, H - R_PASS], U8, "w2_s_rest", tag)
             nc.gpsimd.memset(rest[:].bitcast(I32), 0)
-            load_scale_rows(rest, w2_scales[0, :, R_PASS:H])
+            load_scale_rows(rest, w2_scales[0, :, R_PASS:H], (nc.sync,) * QUADS)
             dealt["w2_s_rest"] = rest
 
         casts["w3_early"] = keep.tile([P, LAST * N_OUT * PACK], BF16, name="w3_early_bf", align_bytes=ALIGN)

@@ -477,7 +477,7 @@ def tile_list_phishing_verdict_slots_kernel(
                     score(g, banks[b], codes[:, b * P : (b + 1) * P], scales[:, b * P : (b + 1) * P])
             rows = dealt["diffs"]
             blocks = [slice(b * P, (b + 1) * P) for b in range(BLOCKS)]
-            z_bf = [keep.tile([P, P * PACK], BF16, name=f"z_last{b}", align_bytes=ALIGN) for b in range(BLOCKS)]
+            z_bf = {}
 
             def fetch(b):
                 nc.vector.tensor_tensor(
@@ -488,6 +488,7 @@ def tile_list_phishing_verdict_slots_kernel(
                 )
 
             def relu(b, on_vector):
+                z_bf[b] = tenant([P, P * PACK], BF16, "z_last", ("z_a", "z_b", "z_c", "z_b")[b])
                 views = interleaved(z_bf[b][:], rows[:, :, blocks[b]])
                 if on_vector:
                     nc.vector.tensor_scalar_max(*views, 0.0)
@@ -518,8 +519,8 @@ def tile_list_phishing_verdict_slots_kernel(
             close(0)
             fetch(3)
             close(1)
-            relu(3, True)
             close(2)
+            relu(3, True)
             close(3)
             for b in range(BLOCKS):
                 store(b, b == BLOCKS - 1)

from contextlib import ExitStack

import concourse.mybir as mybir
from concourse.masks import make_identity

K, T, S, H, T2, M_OUT, N_OUT = 512, 4096, 1024, 1536, 2048, 512, 384
FLOPS = 2 * K * H * S * 2 + 2 * H * N_OUT * M_OUT

F32 = mybir.dt.float32
BF16 = mybir.dt.bfloat16
I32 = mybir.dt.int32
U32 = mybir.dt.uint32
U16 = mybir.dt.uint16
U8 = mybir.dt.uint8
FP8X4 = mybir.dt.float8_e4m3fn_x4
FP4X4 = mybir.dt.float4_e2m1fn_x4
ACT = mybir.ActivationFunctionType
ALU = mybir.AluOpType

P = 128
PACK = 4
QUADS = 4
QUAD = P // QUADS
PER_COLUMN = 16
R_PASS = P * PACK
PASSES = H // R_PASS
LAST = PASSES - 1
TILES = H // P
SCALE_ROWS = R_PASS // QUAD
HALF = 512
ALIGN = 64
QUANT_WORDS = (128, 256, 384, 512)
RUN = 4

FIRST_PIECES = ((0, 256), (256, 256), (512, 512))


ROUNDS = (
    ((1, 2), 512, "w1_second"),
    ((3, 4), 704, "w1_third"),
    ((5, 6), 704, "w1_last"),
    ((7, 8), 704, "z0"),
    ((9, 10), 704, "w3_early"),
    ((11,), 992, "z1"),
)
W3_CASTS = {2: 0, 3: 1, 5: 2}
SPARE = 1088
W1_PARTS = {"w1_tile0": (0, 1), "w1_early": (1, 3), "w1_second": (3, 5), "w1_third": (5, 8), "w1_last": (8, 12)}
BANKS = {"a_own": 2, "a_share": 1, "b": 1, "turn": 2, "back": 2}
FIRST_BANK = {"a_own": 0, "a_share": 2, "b": 3, "turn": 4, "back": 6}
BANK_BYTES = 2048
BLOCKS = M_OUT // P


def tile_list_phishing_verdict_slots_kernel(
    tc, tab_words, tab_scales, offs, w1, w2_words, w2_scales, wgs, offs2, offs3, margin, w3, out
):
    nc = tc.nc
    with ExitStack() as ctx:
        lists = ctx.enter_context(tc.tile_pool(name="lists", bufs=1))
        keep = ctx.enter_context(tc.tile_pool(name="keep", bufs=1))
        ring = ctx.enter_context(tc.tile_pool(name="ring", bufs=1))
        psum = ctx.enter_context(tc.psum_pool(name="psum", bufs=1))

        def tenant(shape, dtype, name, tag):
            return ring.tile(shape, dtype, name=name, tag=tag, bufs=1, align_bytes=ALIGN)

        def entries(offsets, first, count):
            return offsets[:, first // PER_COLUMN : (first + count) // PER_COLUMN]

        def load_scale_rows(scale_tile, rows, queues):
            for q in range(QUADS):
                queues[q].dma_start(
                    scale_tile[QUAD * q : QUAD * q + PACK, :].bitcast(I32),
                    rows[PACK * q : PACK * (q + 1), :].bitcast(I32),
                )

        w1_raw = {}

        def load_w1(part, tag, place=None):
            first, stop = W1_PARTS[part]
            if place is None:
                place = tenant([P, PACK * (stop - first) * P], F32, "w1_raw", tag)[:]
            w1_raw[part] = place.rearrange("p (j c) -> p j c", j=PACK)
            nc.sync.dma_start(w1_raw[part], w1[:, first * P : stop * P].rearrange("(p j) c -> p j c", j=PACK))

        def load_w2_words(first, stop, tag):
            words = tenant([P, 2 * (stop - first)], U8, "w2_w", tag)
            nc.sync.dma_start(words[:].bitcast(I32), w2_words[0, :, 2 * first : 2 * stop].bitcast(I32))
            return words

        def quantised(name, grouped, width, tag=None, codes=None):
            if codes is None:
                codes = tenant([P, width], U32, name + "_codes", tag or name)
            scales = keep.tile([P, width], U8, name=name + "_scales", align_bytes=ALIGN)
            done = 0
            while done < width:
                step = max(w for w in QUANT_WORDS if w <= width - done)
                nc.vector.quantize_mx(
                    out=codes[:, done : done + step].bitcast(FP8X4),
                    scales=scales[:, done : done + step],
                    in_=grouped[:, PACK * done : PACK * (done + step)],
                )
                done = done + step
            return codes, scales

        def interleaved(grouped, rows):
            return (
                grouped.rearrange("p (c i j) -> p c j i", i=RUN, j=PACK),
                rows.rearrange("p j (c i) -> p c j i", i=RUN),
            )

        idx = lists.tile([P, S // PER_COLUMN], U16, name="idx")
        idx2 = lists.tile([P, S // PER_COLUMN], U16, name="idx2")
        idx3 = lists.tile([P, M_OUT // PER_COLUMN], U16, name="idx3")

        tab_scale_rows = tenant([P, T], U8, "tab_scale_rows", "page_odd")
        nc.scalar.dma_start(tab_scale_rows[0:SCALE_ROWS, :].bitcast(I32), tab_scales[0].bitcast(I32))
        nc.sync.dma_start(idx[:], offs)
        nc.sync.dma_start(idx2[:], offs2)
        w2_s_first = keep.tile([P, R_PASS], U8, name="w2_s_first", align_bytes=ALIGN)
        load_scale_rows(w2_s_first, w2_scales[0, :, 0:R_PASS], (nc.scalar, nc.scalar, nc.scalar, nc.sync))
        tab_w = tenant([P, T], I32, "tab_w", "table")
        nc.sync.dma_start(tab_w[:], tab_words[0].rearrange("p t i -> p (t i)").bitcast(I32))
        load_w1("w1_tile0", "w1_a")
        w2_outer = keep.tile([P, 2, 2 * R_PASS], U8, name="w2_outer", align_bytes=ALIGN)
        nc.sync.dma_start(
            w2_outer[:].bitcast(I32), w2_words[0].rearrange("p (g c) -> p g c", g=PASSES)[:, 0:PASSES:LAST, :].bitcast(I32)
        )
        w2_first = w2_outer[:, 0, :]

        margins = {}

        def load_margin(g, tag):
            margins[g] = tenant([P, PACK, M_OUT], F32, "margin", tag)
            order = "(p t) m -> p t m" if g == LAST else "(t p) m -> p t m"
            nc.sync.dma_start(margins[g][:], margin[g * R_PASS : (g + 1) * R_PASS, :].rearrange(order, t=PACK))

        tab_s = tenant([P, T], U8, "tab_s", "window")
        nc.vector.memset(tab_s[:].bitcast(I32), 0)
        page_even = keep.tile([P, T2], F32, name="page_even")
        nc.vector.memset(page_even[:], 0.0)
        nc.vector.tensor_copy(tab_s[0:SCALE_ROWS, :].bitcast(I32), tab_scale_rows[0:SCALE_ROWS, :].bitcast(I32))
        page_odd = tenant([P, T2], F32, "page_odd", "page_odd")
        nc.gpsimd.memset(page_odd[:], 0.0)
        pages = [page_even, page_odd]

        picked_s = tenant([P, S], U8, "picked_s", "w1_b")
        nc.vector.tensor_copy(picked_s[:], tab_s[:].indirect(idx[:]))
        v_s = keep.tile([P, S], U8, name="v_s", align_bytes=ALIGN)
        nc.vector.tensor_copy(v_s[0:SCALE_ROWS, :].bitcast(I32), picked_s[0:SCALE_ROWS, :].bitcast(I32))
        for q in range(1, QUADS):
            nc.sync.dma_start(
                v_s[QUAD * q : QUAD * q + PACK, :].bitcast(I32), picked_s[PACK * q : PACK * (q + 1), :].bitcast(I32)
            )

        stretches = keep.tile([P, 2 * (SPARE + 2 * S)], F32, name="stretches", align_bytes=ALIGN)

        def stretch(r, first, count):
            start = (r % 2) * (SPARE + 2 * S) + SPARE + first
            return stretches[:, start : start + count]

        weights = tenant([P, S], F32, "weights", "after_picked")
        first_count = FIRST_PIECES[0][1]
        load_w1("w1_early", None, stretch(-1, 0, S))
        nc.sync.dma_start(weights[:, 0:first_count], wgs[:, 0:first_count])
        nc.sync.dma_start(weights[:, first_count:S], wgs[:, first_count:S])
        nc.sync.dma_start(idx3[:], offs3)
        v_w = [keep.tile([P, HALF], U32, name=f"v_w{h}", align_bytes=ALIGN) for h in range(S // HALF)]
        for first, count in FIRST_PIECES:
            nc.vector.tensor_copy(
                v_w[first // HALF][:, first % HALF : first % HALF + count],
                tab_w[:].bitcast(U32).indirect(entries(idx, first, count)),
            )

        first_bf = tenant([P, P * PACK], BF16, "first_bf", "first_bf")
        nc.scalar.activation(*interleaved(first_bf[:], w1_raw["w1_tile0"][:]), ACT.Copy)
        w1_q = {"w1_tile0": quantised("w1_tile0", first_bf, P)}

        load_w1("w1_second", "w1_b")
        load_w1("w1_third", "table")
        w2_rest = load_w2_words(R_PASS, 2 * R_PASS, "w1_a")

        identity = keep.tile([P, P], F32, name="identity")
        make_identity(nc, identity[:])

        casts = {}
        quants = {}
        dealt = {}
        turned = {}

        def cast_w1(part, tag, bf=None):
            if bf is None:
                bf = tenant([P, w1_raw[part].shape[2] * PACK], BF16, part + "_bf", tag)
            if part == "w1_last":
                dst = bf[:].rearrange("p (t u j) -> p u t j", t=PACK, j=PACK)
                rows = w1_raw[part][:].rearrange("p j (u t) -> p u t j", t=PACK)
            else:
                dst, rows = interleaved(bf[:], w1_raw[part][:])
            nc.scalar.activation(dst, rows, ACT.Copy)
            casts[part] = bf

        def load_last_weights(tag):
            weights_last = tenant([P, PACK, S], F32, "weights_last", tag)
            for q in range(QUADS):
                nc.sync.dma_start(
                    weights_last[QUAD * q : QUAD * (q + 1), :, :], wgs.rearrange("(u t) j -> u t j", t=PACK)
                )
            dealt["weights"] = weights_last

        def reorder_w2(scales):
            nc.vector.tensor_copy(
                scales.rearrange("p (t u) -> p t u", t=PACK),
                dealt["w2_s_rest"][:, R_PASS : 2 * R_PASS].rearrange("p (u t) -> p t u", t=PACK),
            )
            dealt["w2"] = (dealt["w2_words"], scales)

        def load_w3(tag):
            dealt["w3_raw"] = tenant([P, PASSES, PACK, N_OUT], F32, "w3_raw", tag)
            for g in range(PASSES):
                nc.sync.dma_start(
                    dealt["w3_raw"][:, g, :, :],
                    w3[g * R_PASS : (g + 1) * R_PASS, :].rearrange("(p j) n -> p j n", j=PACK),
                )

        def load_w2_scales(tag):
            rest = tenant([P, H - R_PASS], U8, "w2_s_rest", tag)
            nc.gpsimd.memset(rest[:].bitcast(I32), 0)
            load_scale_rows(rest, w2_scales[0, :, R_PASS:H], (nc.sync,) * QUADS)
            dealt["w2_s_rest"] = rest

        casts["w3_early"] = keep.tile([P, LAST * N_OUT * PACK], BF16, name="w3_early_bf", align_bytes=ALIGN)
        casts["w3_last"] = keep.tile([P, N_OUT * PACK], BF16, name="w3_last_bf", align_bytes=ALIGN)

        def cast_w3(g):
            part = casts["w3_last"][:] if g == LAST else casts["w3_early"][:, g * N_OUT * PACK : (g + 1) * N_OUT * PACK]
            nc.scalar.activation(*interleaved(part, dealt["w3_raw"][:, g, :, :]), ACT.Copy)

        def side_work(name):
            width = casts[name].shape[1] // PACK
            if name == "w1_third":
                both = tenant([P, 4 * width + R_PASS], U8, "both", name)
                made = quantised(name, casts[name], width, codes=both[:, 0 : 4 * width].bitcast(U32))
                reorder_w2(both[:, 4 * width : 4 * width + R_PASS])
            else:
                made = quantised(name, casts[name], width)
            if name in W1_PARTS:
                w1_q[name] = made
            else:
                quants[name] = made

        def w1_operand(i):
            part = [name for name in W1_PARTS if W1_PARTS[name][0] <= i < W1_PARTS[name][1]][0]
            codes, scales = w1_q[part]
            col = (i - W1_PARTS[part][0]) * P
            return codes[:, col : col + P].bitcast(FP8X4), scales[:, col : col + P]

        def w2_operand(i):
            g, t = divmod(i, PACK)
            if g == 0:
                words, scales = w2_first, w2_s_first
            else:
                words, scales = dealt["w2"] if g == LAST else (w2_rest, dealt["w2_s_rest"])
            return words[:, 2 * t * P : 2 * (t + 1) * P].bitcast(FP4X4), scales[:, t * P : (t + 1) * P]

        def first_sum(tag, operand, first, count):
            codes, scale = operand
            h = first // HALF
            part = slice(first - h * HALF, first - h * HALF + count)
            bank = psum.tile([P, HALF], F32, name="first_ps", tag=tag, bufs=BANKS[tag], offset=FIRST_BANK[tag] * BANK_BYTES)
            nc.tensor.matmul_mx(
                out=bank[:, 0:count],
                lhsT=codes,
                lhsT_scale=scale,
                rhs=v_w[h][:, part].bitcast(FP8X4),
                rhs_scale=v_s[:, first : first + count],
                start=True,
                stop=True,
            )
            return bank[:, 0:count]

        def scratch(count):
            return ring.tile([P, HALF], F32, name="square", tag="square", bufs=2)[:, 0:count]

        def squared(i, first, count, square):
            tag = ("turn", "back")[first // HALF] if i <= ROUNDS[0][0][0] else "b"
            nc.scalar.activation(square, first_sum(tag, w2_operand(i), first, count), ACT.Square)
            return square

        def damping(dst, square):
            nc.scalar.activation(dst, square, ACT.Exp, scale=-1.0)

        def scatter(i, first, count, sig):
            g, t = divmod(i, PACK)
            weight = dealt["weights"][:, t, :] if g == LAST else weights[:]
            nc.vector.tensor_tensor(
                pages[i % 2][:].indirect(entries(idx2, first, count)), sig, weight[:, first : first + count], ALU.mult
            )

        def first_tile():
            for first, count in FIRST_PIECES:
                if first < HALF:
                    damp = tenant([P, count], F32, "damp_first", "damp_mid" if first else "low0")[:]
                else:
                    damp = stretch(0, -count // 2, count)
                square = tenant([P, count], F32, "square", "w1_c" if first >= HALF else f"low{first}")[:] if first else scratch(count)
                damping(damp, squared(0, first, count, square))
                sig = stretch(-1, first, count)
                if first == 0:
                    early_bf = tenant([P, S], BF16, "early_bf", "early_bf")
                    nc.vector.tensor_copy(*interleaved(early_bf[:], w1_raw["w1_early"]))
                    casts["w1_early"] = early_bf
                a_ps = first_sum("a_own", w1_operand(0), first, count)
                nc.vector.tensor_tensor(sig, a_ps, damp, ALU.mult)
                if first == 0:
                    side_work("w1_early")
                    scatter(0, first, count, sig)
            dealt["w2_words"] = tenant([P, 2 * R_PASS], U8, "w2_last", "damp_mid")
            nc.vector.tensor_copy(
                dealt["w2_words"][:].bitcast(U16).rearrange("p (t u) -> p t u", t=PACK),
                w2_outer[:, 1, :].bitcast(U16).rearrange("p (u t) -> p t u", t=PACK),
            )
            scatter(0, first_count, S - first_count, stretch(-1, first_count, S - first_count))

        def parts(r, k):
            own = S - ROUNDS[r][1]
            if k == 0:
                return 0, slice(0, own), slice(own, HALF)
            return 1, slice(HALF - own, HALF), slice(0, HALF - own)

        def shared(r, k, half, cols):
            first = k * S + half * HALF - (S - ROUNDS[r][1])
            return slice(first + cols.start, first + cols.stop)

        gathered = keep.tile([P, 2 * M_OUT], F32, name="gathered")

        def rest_damping(r, k, damp_share, square):
            half, own, rest = parts(r, k)
            squared(ROUNDS[r][0][k], half * HALF, HALF, square)
            if rest.start < rest.stop:
                damping(damp_share[:, shared(r, k, half, rest)], square[:, rest])
            return square[:, own]

        def dampings(r):
            tiles, share, side = ROUNDS[r]
            if r + 1 < len(ROUNDS):
                damp_share = ring.tile([P, len(tiles) * share], F32, name="damp_share", tag="damp_share", bufs=2)
            else:
                damp_share = tenant([P, share], F32, "damp_share", "w3_last")
            damp = []
            for k, i in enumerate(tiles):
                if i != tiles[-1]:
                    damp.append(ring.tile([P, HALF], F32, name="damp", tag="damp", bufs=2)[:, 0 : S - share])
                    damping(damp[k], rest_damping(r, k, damp_share, scratch(HALF)))
                other = 1 - parts(r, k)[0]
                square = squared(i, other * HALF, HALF, scratch(HALF))
                damping(damp_share[:, shared(r, k, other, slice(0, HALF))], square)
            return damp, damp_share

        def signatures(r, damp, damp_share):
            tiles, share, side = ROUNDS[r]
            count = len(tiles)
            half, own, rest = parts(r, count - 1)
            outer = (S - share) // 2
            apart = slice(HALF - outer, HALF) if half else slice(0, outer)
            others = slice(0, HALF - outer) if half else slice(outer, HALF)
            inner = slice(own.start, apart.start) if half else slice(apart.stop, own.stop)
            across = M_OUT - (inner.start + inner.stop) // 2
            square = gathered[:, across : across + HALF]
            square_apart = tenant([P, outer], F32, "square_apart", side)
            b_ps = first_sum("b", w2_operand(tiles[-1]), half * HALF, HALF)
            nc.scalar.activation(square[:, others], b_ps[:, others], ACT.Square)
            nc.scalar.activation(square_apart[:], b_ps[:, apart], ACT.Square)
            if rest.start < rest.stop:
                damping(damp_share[:, shared(r, count - 1, half, rest)], square[:, rest])
            late = ((inner.start - own.start, square[:, inner]), (apart.start - own.start, square_apart[:]))
            end = S - ROUNDS[r - 1][1] if r > 0 else first_count
            a_share = stretch(r - 1, end - share * count, share * count)
            a_own = []
            for k, i in enumerate(tiles):
                half, own, rest = parts(r, k)
                bank = first_sum("a_own", w1_operand(i), half * HALF, HALF)
                a_own.append(bank[:, own])
                other = first_sum("a_share", w1_operand(i), (1 - half) * HALF, HALF)
                nc.scalar.copy(a_share[:, shared(r, k, 1 - half, slice(0, HALF))], other)
                if rest.start < rest.stop:
                    nc.scalar.copy(a_share[:, shared(r, k, half, rest)], bank[:, rest])
            nc.gpsimd.tensor_tensor(stretch(r, S - share, share * count), a_share, damp_share[:], ALU.mult)
            damp.append(stretch(r - 1, end, S - share) if r > 0 else stretch(0, -HALF, HALF))
            for first, part in late:
                damping(damp[-1][:, first : first + outer], part)
            for k in range(count):
                half, own, rest = parts(r, k)
                sig = stretch(r, k * S + half * HALF + own.start, S - share)
                nc.vector.tensor_tensor(sig, a_own[k], damp[k], ALU.mult)

        def negated_margin(i):
            g, t = divmod(i, PACK)
            negated = ring.tile([P, M_OUT], F32, name="negated", tag="negated", bufs=2)
            nc.scalar.activation(negated[:], margins[g][:, t, :], ACT.Copy, scale=-1.0)
            return negated

        def turn(terms, tag):
            if tag == "final":
                bank = psum.tile([P, BLOCKS, M_OUT], F32, name="final_ps", bufs=1, offset=FIRST_BANK["turn"] * BANK_BYTES)[:, 0, :]
            else:
                bank = psum.tile([P, M_OUT], F32, name="turn_ps", tag=tag, bufs=BANKS[tag], offset=FIRST_BANK[tag] * BANK_BYTES)
            for k in range(BLOCKS):
                cols = slice(k * P, (k + 1) * P)
                for n, rows in enumerate(terms):
                    nc.tensor.matmul(
                        bank[:, cols],
                        lhsT=rows[:, cols],
                        rhs=identity[:],
                        start=(n == 0),
                        stop=(n == len(terms) - 1),
                        is_transpose=True,
                    )
            return bank

        def turn_back(g):
            z_bf = tenant([P, M_OUT * PACK], BF16, "z_bf", f"z_bf{g}")
            pairs = turned[g][:].bitcast(F32)
            for half in range(2):
                bank = turn((pairs[:, half * M_OUT : (half + 1) * M_OUT],), "back")
                nc.scalar.copy(
                    z_bf[:].bitcast(F32)[:, half * M_OUT : (half + 1) * M_OUT].rearrange("p (k m u) -> p k m u", k=2, u=2),
                    bank[:].rearrange("p (k u m) -> p k m u", k=2, u=2),
                )
            casts[f"z{g}"] = z_bf

        def finish_tile(i, fetched):
            g, t = divmod(i, PACK)
            nc.vector.tensor_copy(fetched, pages[i % 2][:].indirect(idx3[:]))
            bank = turn((negated_margin(i), fetched), "turn")
            if g == LAST:
                if t == 0:
                    dealt["diffs"] = tenant([P, PACK, M_OUT], F32, "diffs", f"low{FIRST_PIECES[1][0]}")
                across = tenant([P, M_OUT], F32, "across", f"turned{t % 2}")
                nc.scalar.copy(across[:], bank[:])
                nc.scalar.copy(dealt["diffs"][:, t, :], turn((across,), "final" if i == TILES - 2 else "back")[:])
                return
            if t == 0:
                turned[g] = tenant([P, BLOCKS * R_PASS], BF16, "turned", f"turned{g}")
            words = turned[g][:].rearrange("p (k u w e) -> p k u w e", k=BLOCKS, u=2, e=2)
            rows = bank[:].rearrange("p (k q u e) -> p k u q e", k=BLOCKS, u=2, e=2)
            for u in range(2):
                nc.scalar.activation(words[:, :, u, QUAD * t : QUAD * (t + 1), :], rows[:, :, u], ACT.Relu)
            if t == PACK - 1:
                turn_back(g)

        def score(g, bank, z_codes, z_scale):
            for k in range(N_OUT // P):
                first = k * P if g == LAST else g * N_OUT + k * P
                cols = slice(first, first + P)
                codes, scales = quants["w3_last" if g == LAST else "w3_early"]
                nc.tensor.matmul_mx(
                    out=bank[:, k * P : (k + 1) * P],
                    lhsT=codes[:, cols].bitcast(FP8X4),
                    lhsT_scale=scales[:, cols],
                    rhs=z_codes.bitcast(FP8X4),
                    rhs_scale=z_scale,
                    start=(g == 0 and k == 0),
                    stop=(g == LAST and k == N_OUT // P - 1),
                )

        def finish():
            i = TILES - 1
            side_work("w3_last")
            banks = [
                psum.tile([P, N_OUT], F32, name=f"out_ps{b}", bufs=1, offset=(FIRST_BANK["turn"] + b) * BANK_BYTES)[:]
                for b in range(BLOCKS)
            ]
            for g in range(LAST):
                codes, scales = quants[f"z{g}"]
                for b in range(BLOCKS):
                    score(g, banks[b], codes[:, b * P : (b + 1) * P], scales[:, b * P : (b + 1) * P])
            rows = dealt["diffs"]
            blocks = [slice(b * P, (b + 1) * P) for b in range(BLOCKS)]
            z_bf = {}

            def fetch(b):
                nc.vector.tensor_tensor(
                    rows[:, PACK - 1, blocks[b]],
                    pages[i % 2][:].indirect(entries(idx3, blocks[b].start, P)),
                    margins[LAST][:, PACK - 1, blocks[b]],
                    ALU.subtract,
                )

            def relu(b, on_vector):
                z_bf[b] = tenant([P, P * PACK], BF16, "z_last", ("z_a", "z_b", "z_c", "z_b")[b])
                views = interleaved(z_bf[b][:], rows[:, :, blocks[b]])
                if on_vector:
                    nc.vector.tensor_scalar_max(*views, 0.0)
                else:
                    nc.scalar.activation(*views, ACT.Relu)

            def close(b):
                codes, scales = quantised(f"z_last{b}", z_bf[b], P)
                score(LAST, banks[b], codes[:], scales[:])

            def store(b, on_vector):
                result = tenant([P, N_OUT], F32, "result", ("table", "after_picked", "cast0", "page_odd")[b])
                if on_vector:
                    nc.vector.tensor_copy(result[:], banks[b])
                else:
                    nc.scalar.copy(result[:], banks[b])
                nc.sync.dma_start(
                    out[:, blocks[b]].rearrange("(k p) m -> p k m", p=P),
                    result[:].rearrange("p (k m) -> p k m", m=P),
                )

            fetch(0)
            fetch(1)
            relu(0, True)
            relu(1, False)
            fetch(2)
            relu(2, False)
            close(0)
            fetch(3)
            close(1)
            close(2)
            relu(3, True)
            close(3)
            for b in range(BLOCKS):
                store(b, b == BLOCKS - 1)

        first_tile()
        load_w2_scales(f"low{FIRST_PIECES[0][0]}")
        load_margin(0, f"low{FIRST_PIECES[1][0]}")
        load_w1("w1_last", "w1_c")
        before = (0,)
        ahead = dampings(0)
        for r, (tiles, share, side) in enumerate(ROUNDS):
            signatures(r, *ahead)
            if r == 0:
                cast_w1(side, "cast0")
                load_margin(LAST, "w1_b")
            if r + 1 < len(ROUNDS):
                ahead = dampings(r + 1)
                if ROUNDS[r + 1][2] in W1_PARTS:
                    cast_w1(ROUNDS[r + 1][2], f"cast{r + 1}")
            if r == 0:
                load_w3("table")
            if r == 1:
                load_last_weights("w1_c")
            if r in W3_CASTS:
                cast_w3(W3_CASTS[r])
            for k, i in enumerate(before):
                finish_tile(i, gathered[:, k * M_OUT : (k + 1) * M_OUT])
            side_work(side)
            if r == 0:
                load_margin(1, "cast0")
            for k, i in enumerate(tiles):
                scatter(i, 0, S, stretch(r, k * S, S))
            before = tiles
        finish()
